import numpy as np
import ml_dtypes


def mxq(x, axis, fmt="e4m3"):
    dtype, down = {"e4m3": (ml_dtypes.float8_e4m3fn, 7), "e5m2": (ml_dtypes.float8_e5m2, 14)}[fmt]
    v = np.moveaxis(np.asarray(x, np.float32).astype(ml_dtypes.bfloat16).astype(np.float64), axis, -1)
    blocks = v.reshape(v.shape[:-1] + (-1, 32))
    amax = np.abs(blocks).max(-1, keepdims=True)
    byte = np.maximum(np.where(amax > 0, np.frexp(amax)[1] - 1 + 127, 0) - down, 1)
    scale = np.exp2(byte - 127.0)
    codes = (blocks / scale).astype(np.float32).astype(dtype).astype(np.float64)
    return np.moveaxis((codes * scale).reshape(v.shape), -1, axis)


WIDE = False


def mx_kscale(k):
    if not WIDE:
        return np.ones(k)
    levels = np.array([30, -30])
    if k % 512:
        return np.exp2(np.random.permutation(np.resize(levels, k // 32))).repeat(32)
    a = np.empty((k // 512, 16))
    for p in range(k // 512):
        a[p, :8] = np.random.permutation(np.resize(levels, 8))
        for g in range(8):
            far = levels[np.abs(levels - a[p, g]) >= 10]
            a[p, g + 8] = far[np.random.randint(len(far))]
    return np.exp2(a.ravel()).repeat(32)


def f64(x):
    return np.asarray(x).astype(np.float64)


def striped8(idx):
    return np.concatenate([v.reshape(-1, 16).T for v in idx]).astype(np.uint16)


def unstriped8(offs):
    return np.stack([offs[16 * g:16 * g + 16].T.reshape(-1) for g in range(8)]).astype(np.int64)


E2M1 = np.array([0.0, 0.5, 1.0, 1.5, 2.0, 3.0, 4.0, 6.0, -0.0, -0.5, -1.0, -1.5, -2.0, -3.0, -4.0, -6.0])


def pack_weight(w, fmt):
    k, n = w.shape
    w = f64(np.asarray(w, np.float32).astype(ml_dtypes.bfloat16)).reshape(k // 32, 32, n)
    amax = np.abs(w).max(1)
    if fmt == "e4m3":
        byte = np.frexp(amax)[1] - 1 + 127 - 7
    else:
        mant, ex = np.frexp(amax / 6.0)
        byte = np.where(mant > 0.5, ex, ex - 1) + 127
    byte = np.clip(np.where(amax > 0, byte, 1), 1, 254)
    scaled = (w * np.exp2(127.0 - byte)[:, None, :]).reshape(k, n).astype(np.float32)
    by_word = np.ascontiguousarray(scaled.reshape(k // 512, 128, 4, n).transpose(0, 1, 3, 2))
    if fmt == "e4m3":
        words = by_word.astype(ml_dtypes.float8_e4m3fn).view(np.uint8)
    else:
        c = by_word.astype(ml_dtypes.float4_e2m1fn).view(np.uint8) & 0xF
        words = (c[..., 0::2] | (c[..., 1::2] << 4)).reshape(k // 512, 128, 2 * n)
    return np.ascontiguousarray(words), np.ascontiguousarray(byte.astype(np.uint8).reshape(k // 512, 16, n))


def unpack_weight(words, scales, fmt):
    g, _, n = scales.shape
    words = np.ascontiguousarray(words).reshape(g, 128, n, -1)
    if fmt == "e4m3":
        vals = words.view(ml_dtypes.float8_e4m3fn).astype(np.float64)
    else:
        nib = np.empty((g, 128, n, 4), np.uint8)
        nib[..., 0::2] = words & 0xF
        nib[..., 1::2] = words >> 4
        vals = E2M1[nib]
    vals = vals * np.repeat(np.exp2(scales.astype(np.float64) - 127.0), 8, axis=1)[..., None]
    return vals.transpose(0, 1, 3, 2).reshape(g * 512, n)


K, N, T, J = 512, 512, 2048, 1024


def setup_inputs():
    n = np.random.standard_normal
    s = mx_kscale(K)[:, None]
    m = np.exp(0.5 * n((1, J)))
    p_w = pack_weight(n((K, N)) / np.sqrt(K) / s, "e2m1")
    return {
        "dy": (m * n((K, J)) * s).astype(np.float32),
        "w_words": p_w[0],
        "w_scales": p_w[1],
        "res": (n((N, J))).astype(np.float32),
        "wgo": np.repeat(np.random.uniform(0.5, 2.0, (8, J)), 16, axis=0).astype(np.float32),
        "offs": striped8(np.stack([np.random.permutation(T)[:J] for _ in range(8)])),
    }


def reference(dy, w_words, w_scales, res, wgo, offs):
    idx = unstriped8(offs)
    dy_q_ = mxq(f64(dy), 0, "e5m2")
    dy_r_ = mxq(f64(dy) - dy_q_, 0, "e4m3")
    w_ = unpack_weight(w_words, w_scales, "e2m1")
    dx = w_.T @ dy_q_ + w_.T @ dy_r_
    out = np.zeros((N, T))
    rows = np.arange(N)
    out[rows[:, None], idx[rows % 128 // 16]] = f64(wgo)[rows % 128] * (dx + f64(res))
    return out

@@ -1,0 +1,208 @@
+from contextlib import ExitStack
+
+import concourse.mybir as mybir
+from concourse.masks import make_identity
+
+K, N, T, J = 512, 512, 2048, 1024
+FLOPS = 3 * 2 * K * N * J
+
+F32 = mybir.dt.float32
+BF16 = mybir.dt.bfloat16
+I32 = mybir.dt.int32
+U32 = mybir.dt.uint32
+U16 = mybir.dt.uint16
+U8 = mybir.dt.uint8
+E4M3 = mybir.dt.float8_e4m3fn_x4
+E5M2 = mybir.dt.float8_e5m2_x4
+E2M1 = mybir.dt.float4_e2m1fn_x4
+ALU = mybir.AluOpType
+
+P = 128
+PACK = 4
+CHUNK = 512
+HALF = CHUNK // 2
+CHUNKS = J // CHUNK
+ROW_TILES = N // P
+RUN = 4
+
+
+def weave(copy, dst, src):
+    copy(out=dst.rearrange("p (c i) t -> p c t i", i=RUN), in_=src.rearrange("p t (c i) -> p c t i", i=RUN))
+
+
+def tile_list_embg_tgq4_res_kernel(tc, dy, w_words, w_scales, res, wgo, offs, out):
+    nc = tc.nc
+    with ExitStack() as ctx:
+        keep = ctx.enter_context(tc.tile_pool(name="keep", bufs=1))
+        ring = ctx.enter_context(tc.tile_pool(name="ring", bufs=3))
+        psum_back = ctx.enter_context(tc.psum_pool(name="psum_back", bufs=4))
+        psum_dx = ctx.enter_context(tc.psum_pool(name="psum_dx", bufs=4))
+
+        offsets = keep.tile([P, J // 16], U16, name="offsets")
+        w_codes = keep.tile([P, 2 * N], U8, name="w_codes", align_bytes=64)
+        w_plane = keep.tile([P, N], U8, name="w_plane", align_bytes=64)
+        raw = [keep.tile([P, 2, PACK, HALF], F32, name=f"raw{c}") for c in range(CHUNKS)]
+        weights = [keep.tile([P, CHUNK], F32, name=f"weights{c}") for c in range(CHUNKS)]
+        skips = {}
+        for c in range(CHUNKS):
+            for i in range(ROW_TILES):
+                tag = "page3" if (c, i) == (0, 2) else f"skip{c}{i}"
+                skips[c, i] = keep.tile([P, CHUNK], F32, name=f"skip{c}{i}", tag=tag, align_bytes=64)
+
+        dy_rows = dy.rearrange("(p t) j -> p t j", t=PACK)
+
+        def load_dy(c):
+            for h in range(2):
+                j0 = c * CHUNK + h * HALF
+                nc.sync.dma_start(out=raw[c][:, h], in_=dy_rows[:, :, j0 : j0 + HALF])
+
+        def load_skip(c, i):
+            nc.sync.dma_start(out=skips[c, i][:], in_=res[i * P : (i + 1) * P, c * CHUNK : (c + 1) * CHUNK])
+
+        def load_weights(c):
+            nc.sync.dma_start(out=weights[c][:], in_=wgo[:, c * CHUNK : (c + 1) * CHUNK])
+
+        nc.vector.memset(w_plane[:].bitcast(I32), 0)
+        load_dy(0)
+        nc.sync.dma_start(out=w_codes[:].bitcast(I32), in_=w_words[0].bitcast(I32))
+        for q in range(4):
+            nc.scalar.dma_start(
+                out=w_plane[32 * q : 32 * q + 4, :].bitcast(I32), in_=w_scales[0, 4 * q : 4 * q + 4, :].bitcast(I32)
+            )
+        load_dy(1)
+        load_skip(0, 0)
+        load_weights(0)
+        nc.sync.dma_start(offsets[:], offs)
+        for i in range(1, ROW_TILES):
+            load_skip(0, i)
+        load_weights(1)
+        for i in range(ROW_TILES):
+            load_skip(1, i)
+
+        eye = keep.tile([P, P], BF16, name="eye")
+        make_identity(nc, eye[:])
+        pitch = PACK * P + 1
+        eye_rows = keep.tile([P, PACK * pitch], BF16, name="eye_rows", align_bytes=64)
+        nc.vector.memset(eye_rows[:], 0.0)
+        nc.scalar.copy(
+            out=eye_rows[:].rearrange("p (t s) -> p t s", s=pitch)[:, :, 0 : PACK * P : PACK],
+            in_=eye[:].unsqueeze(1).to_broadcast([P, PACK, P]),
+        )
+        eye_codes = keep.tile([P, K], U32, name="eye_codes", align_bytes=64)
+        eye_plane = keep.tile([P, K], U8, name="eye_plane", align_bytes=64)
+        nc.vector.quantize_mx(out=eye_codes[:].bitcast(E4M3), scales=eye_plane[:], in_=eye_rows[:, 0 : PACK * K])
+
+        pages = {0: keep.tile([P, T], F32, name="page0", tag="page0")}
+        nc.vector.memset(pages[0][:], 0.0)
+
+        def clear_page(i):
+            pages[i] = keep.tile([P, T], F32, name=f"page{i}", tag=f"page{i}", align_bytes=64)
+            nc.gpsimd.memset(pages[i][:], 0.0)
+
+        def mx_tiles(name, first_tag):
+            tags = [first_tag, f"{name}_woven1"]
+            woven = [
+                keep.tile([P, CHUNK, PACK], BF16, name=f"{name}_woven{c}", tag=tags[c], align_bytes=64) for c in range(CHUNKS)
+            ]
+            codes = [keep.tile([P, CHUNK], U32, name=f"{name}_codes{c}", align_bytes=64) for c in range(CHUNKS)]
+            plane = [keep.tile([P, CHUNK], U8, name=f"{name}_plane{c}", align_bytes=64) for c in range(CHUNKS)]
+            return woven, codes, plane
+
+        q_woven, q_codes, q_plane = mx_tiles("q", "page1")
+        r_woven, r_codes, r_plane = mx_tiles("r", "page2")
+        rest = [keep.tile([P, PACK, CHUNK], BF16, name=f"rest{c}") for c in range(CHUNKS)]
+
+        def quantize(woven, codes, plane, fmt, cols):
+            nc.vector.quantize_mx(
+                out=codes[:, cols].bitcast(fmt), scales=plane[:, cols], in_=woven[:, cols, :].rearrange("p j t -> p (j t)")
+            )
+
+        halves = [slice(0, HALF), slice(HALF, CHUNK)]
+        whole = slice(0, CHUNK)
+        back = {}
+        dx = {}
+
+        def read_back(c):
+            for t in range(PACK):
+                back[c, t] = psum_back.tile([P, CHUNK], F32, name="back")
+                cols = slice(t * P, (t + 1) * P)
+                nc.tensor.matmul_mx(
+                    out=back[c, t][:],
+                    lhsT=eye_codes[:, cols].bitcast(E4M3),
+                    lhsT_scale=eye_plane[:, cols],
+                    rhs=q_codes[c][:].bitcast(E5M2),
+                    rhs_scale=q_plane[c][:],
+                    start=True,
+                    stop=True,
+                )
+
+        def subtract(c):
+            for t in range(PACK):
+                nc.vector.tensor_tensor(
+                    out=rest[c][:, t, :].rearrange("p (h j) -> p h j", h=2),
+                    in0=raw[c][:, :, t, :],
+                    in1=back[c, t][:].rearrange("p (h j) -> p h j", h=2),
+                    op=ALU.subtract,
+                )
+
+        def product(c, i, first):
+            if first:
+                dx[c, i] = psum_dx.tile([P, CHUNK], F32, name="dx")
+            codes, plane, fmt = (q_codes, q_plane, E5M2) if first else (r_codes, r_plane, E4M3)
+            nc.tensor.matmul_mx(
+                out=dx[c, i][:],
+                lhsT=w_codes[:, 2 * P * i : 2 * P * (i + 1)].bitcast(E2M1),
+                lhsT_scale=w_plane[:, P * i : P * (i + 1)],
+                rhs=codes[c][:].bitcast(fmt),
+                rhs_scale=plane[c][:],
+                start=first,
+                stop=not first,
+            )
+
+        def place(c, i):
+            total = ring.tile([P, CHUNK], F32, name="total")
+            scaled = ring.tile([P, CHUNK], F32, name="scaled")
+            if (c, i) == (0, 0):
+                nc.vector.tensor_tensor(out=total[:], in0=dx[c, i][:], in1=skips[c, i][:], op=ALU.add)
+                nc.vector.tensor_tensor(out=scaled[:], in0=total[:], in1=weights[c][:], op=ALU.mult)
+            else:
+                sums = ring.tile([P, CHUNK], F32, name="sums")
+                nc.scalar.copy(out=sums[:], in_=dx[c, i][:])
+                nc.gpsimd.tensor_tensor(out=total[:], in0=sums[:], in1=skips[c, i][:], op=ALU.add)
+                nc.gpsimd.tensor_tensor(out=scaled[:], in0=total[:], in1=weights[c][:], op=ALU.mult)
+            entries = offsets[:, c * CHUNK // 16 : (c + 1) * CHUNK // 16]
+            nc.vector.tensor_copy(out=pages[i][:].indirect(entries), in_=scaled[:])
+            if c == CHUNKS - 1:
+                nc.sync.dma_start(out=out[i * P : (i + 1) * P, :], in_=pages[i][:])
+
+        for h in range(2):
+            weave(nc.vector.tensor_copy, q_woven[0][:, halves[h], :], raw[0][:, h])
+            quantize(q_woven[0], q_codes[0], q_plane[0], E5M2, halves[h])
+        clear_page(1)
+        read_back(0)
+        for i in range(ROW_TILES):
+            product(0, i, True)
+        for h in range(2):
+            weave(nc.scalar.copy, q_woven[1][:, halves[h], :], raw[1][:, h])
+        subtract(0)
+        weave(nc.vector.tensor_copy, r_woven[0][:, halves[0], :], rest[0][:, :, halves[0]])
+        weave(nc.scalar.copy, r_woven[0][:, halves[1], :], rest[0][:, :, halves[1]])
+        for h in range(2):
+            quantize(r_woven[0], r_codes[0], r_plane[0], E4M3, halves[h])
+        clear_page(2)
+        for i in range(ROW_TILES):
+            product(0, i, False)
+        quantize(q_woven[1], q_codes[1], q_plane[1], E5M2, whole)
+        read_back(1)
+        place(0, 0)
+        subtract(1)
+        weave(nc.scalar.copy, r_woven[1][:], rest[1][:])
+        place(0, 1)
+        quantize(r_woven[1], r_codes[1], r_plane[1], E4M3, whole)
+        place(0, 2)
+        clear_page(3)
+        place(0, 3)
+        for i in range(ROW_TILES):
+            product(1, i, True)
+            product(1, i, False)
+            place(1, i)

@@ -19,15 +19,14 @@ ALU = mybir.AluOpType
 
 P = 128
 PACK = 4
+GROUP = 16
+QUADRANTS = 4
 CHUNK = 512
 HALF = CHUNK // 2
 CHUNKS = J // CHUNK
 ROW_TILES = N // P
-RUN = 4
-
-
-def weave(copy, dst, src):
-    copy(out=dst.rearrange("p (c i) t -> p c t i", i=RUN), in_=src.rearrange("p t (c i) -> p c t i", i=RUN))
+SCALAR_TOKENS = 128
+MX_ALIGN = 64
 
 
 def tile_list_embg_tgq4_res_kernel(tc, dy, w_words, w_scales, res, wgo, offs, out):
@@ -35,19 +34,22 @@ def tile_list_embg_tgq4_res_kernel(tc, dy, w_words, w_scales, res, wgo, offs, ou
     with ExitStack() as ctx:
         keep = ctx.enter_context(tc.tile_pool(name="keep", bufs=1))
         ring = ctx.enter_context(tc.tile_pool(name="ring", bufs=3))
-        psum_back = ctx.enter_context(tc.psum_pool(name="psum_back", bufs=4))
-        psum_dx = ctx.enter_context(tc.psum_pool(name="psum_dx", bufs=4))
+        psum_back = ctx.enter_context(tc.psum_pool(name="psum_back", bufs=PACK))
+        psum_dx = ctx.enter_context(tc.psum_pool(name="psum_dx", bufs=ROW_TILES))
 
-        offsets = keep.tile([P, J // 16], U16, name="offsets")
-        w_codes = keep.tile([P, 2 * N], U8, name="w_codes", align_bytes=64)
-        w_plane = keep.tile([P, N], U8, name="w_plane", align_bytes=64)
+        def held_tile(shape, dtype, name, tag):
+            return keep.tile(shape, dtype, name=name, tag=tag, align_bytes=MX_ALIGN)
+
+        order = [(c, i) for c in range(CHUNKS) for i in range(ROW_TILES)]
+        halves = [slice(0, HALF), slice(HALF, CHUNK)]
+        whole = slice(0, CHUNK)
+
+        offsets = keep.tile([P, J // GROUP], U16, name="offsets")
+        w_codes = keep.tile([P, 2 * N], U8, name="w_codes", align_bytes=MX_ALIGN)
+        w_scale = keep.tile([P, N], U8, name="w_scale", align_bytes=MX_ALIGN)
         raw = [keep.tile([P, 2, PACK, HALF], F32, name=f"raw{c}") for c in range(CHUNKS)]
         weights = [keep.tile([P, CHUNK], F32, name=f"weights{c}") for c in range(CHUNKS)]
-        skips = {}
-        for c in range(CHUNKS):
-            for i in range(ROW_TILES):
-                tag = "page3" if (c, i) == (0, 2) else f"skip{c}{i}"
-                skips[c, i] = keep.tile([P, CHUNK], F32, name=f"skip{c}{i}", tag=tag, align_bytes=64)
+        residual = {(c, i): keep.tile([P, CHUNK], F32, name=f"residual{c}{i}") for c, i in order}
 
         dy_rows = dy.rearrange("(p t) j -> p t j", t=PACK)
 
@@ -56,71 +58,67 @@ def tile_list_embg_tgq4_res_kernel(tc, dy, w_words, w_scales, res, wgo, offs, ou
                 j0 = c * CHUNK + h * HALF
                 nc.sync.dma_start(out=raw[c][:, h], in_=dy_rows[:, :, j0 : j0 + HALF])
 
-        def load_skip(c, i):
-            nc.sync.dma_start(out=skips[c, i][:], in_=res[i * P : (i + 1) * P, c * CHUNK : (c + 1) * CHUNK])
+        def load_residual(c, i):
+            nc.sync.dma_start(out=residual[c, i][:], in_=res[i * P : (i + 1) * P, c * CHUNK : (c + 1) * CHUNK])
 
         def load_weights(c):
             nc.sync.dma_start(out=weights[c][:], in_=wgo[:, c * CHUNK : (c + 1) * CHUNK])
 
-        nc.vector.memset(w_plane[:].bitcast(I32), 0)
+        nc.vector.memset(w_scale[:].bitcast(I32), 0)
         load_dy(0)
         nc.sync.dma_start(out=w_codes[:].bitcast(I32), in_=w_words[0].bitcast(I32))
-        for q in range(4):
+        for q in range(QUADRANTS):
             nc.scalar.dma_start(
-                out=w_plane[32 * q : 32 * q + 4, :].bitcast(I32), in_=w_scales[0, 4 * q : 4 * q + 4, :].bitcast(I32)
+                out=w_scale[32 * q : 32 * q + 4, :].bitcast(I32), in_=w_scales[0, 4 * q : 4 * q + 4, :].bitcast(I32)
             )
         load_dy(1)
-        load_skip(0, 0)
+        load_residual(0, 0)
         load_weights(0)
         nc.sync.dma_start(offsets[:], offs)
         for i in range(1, ROW_TILES):
-            load_skip(0, i)
+            load_residual(0, i)
         load_weights(1)
         for i in range(ROW_TILES):
-            load_skip(1, i)
+            load_residual(1, i)
 
         eye = keep.tile([P, P], BF16, name="eye")
         make_identity(nc, eye[:])
         pitch = PACK * P + 1
-        eye_rows = keep.tile([P, PACK * pitch], BF16, name="eye_rows", align_bytes=64)
-        nc.vector.memset(eye_rows[:], 0.0)
-        nc.scalar.copy(
-            out=eye_rows[:].rearrange("p (t s) -> p t s", s=pitch)[:, :, 0 : PACK * P : PACK],
-            in_=eye[:].unsqueeze(1).to_broadcast([P, PACK, P]),
-        )
-        eye_codes = keep.tile([P, K], U32, name="eye_codes", align_bytes=64)
-        eye_plane = keep.tile([P, K], U8, name="eye_plane", align_bytes=64)
-        nc.vector.quantize_mx(out=eye_codes[:].bitcast(E4M3), scales=eye_plane[:], in_=eye_rows[:, 0 : PACK * K])
+        eye_woven = keep.tile([P, PACK * pitch], BF16, name="eye_woven", align_bytes=MX_ALIGN)
+        nc.vector.memset(eye_woven[:].bitcast(I32), 0)
+        pages = {i: keep.tile([P, T], F32, name=f"page{i}") for i in range(2)}
+        for i in range(2):
+            nc.vector.memset(pages[i][:].bitcast(I32), 0)
+        diagonals = eye_woven[:].rearrange("p (t s) -> p t s", s=pitch)[:, :, 0 : PACK * P : PACK]
+        nc.scalar.copy(out=diagonals, in_=eye[:].unsqueeze(1).to_broadcast([P, PACK, P]))
+        eye_codes = keep.tile([P, K], U32, name="eye_codes", align_bytes=MX_ALIGN)
+        eye_scale = keep.tile([P, K], U8, name="eye_scale", align_bytes=MX_ALIGN)
+        nc.vector.quantize_mx(out=eye_codes[:].bitcast(E4M3), scales=eye_scale[:], in_=eye_woven[:, 0 : PACK * K])
 
-        pages = {0: keep.tile([P, T], F32, name="page0", tag="page0")}
-        nc.vector.memset(pages[0][:], 0.0)
+        def chunk_tiles(dtype, name, chunks):
+            return {c: keep.tile([P, CHUNK], dtype, name=f"{name}{c}", align_bytes=MX_ALIGN) for c in chunks}
 
-        def clear_page(i):
-            pages[i] = keep.tile([P, T], F32, name=f"page{i}", tag=f"page{i}", align_bytes=64)
-            nc.gpsimd.memset(pages[i][:], 0.0)
+        woven_shape = [P, CHUNK, PACK]
+        q_woven = [held_tile(woven_shape, BF16, "q_woven0", "page2"), held_tile(woven_shape, BF16, "q_woven1", "q_woven1")]
+        r_woven = [held_tile(woven_shape, BF16, "r_woven0", "page3"), held_tile(woven_shape, BF16, "r_woven1", "r_woven1")]
+        q_codes = chunk_tiles(U32, "q_codes", range(CHUNKS))
+        q_scale = chunk_tiles(U8, "q_scale", range(CHUNKS))
+        r_codes = chunk_tiles(U32, "r_codes", range(1))
+        r_scale = chunk_tiles(U8, "r_scale", range(CHUNKS))
+        rest = [held_tile([P, 2, PACK, HALF], BF16, f"rest{c}", f"rest{c}") for c in range(CHUNKS)]
 
-        def mx_tiles(name, first_tag):
-            tags = [first_tag, f"{name}_woven1"]
-            woven = [
-                keep.tile([P, CHUNK, PACK], BF16, name=f"{name}_woven{c}", tag=tags[c], align_bytes=64) for c in range(CHUNKS)
-            ]
-            codes = [keep.tile([P, CHUNK], U32, name=f"{name}_codes{c}", align_bytes=64) for c in range(CHUNKS)]
-            plane = [keep.tile([P, CHUNK], U8, name=f"{name}_plane{c}", align_bytes=64) for c in range(CHUNKS)]
-            return woven, codes, plane
+        def weave(copy, woven, rows, h, j0, j1):
+            copy(out=woven[:, h * HALF + j0 : h * HALF + j1, :], in_=rows[:, h, :, j0:j1].rearrange("p t j -> p j t"))
 
-        q_woven, q_codes, q_plane = mx_tiles("q", "page1")
-        r_woven, r_codes, r_plane = mx_tiles("r", "page2")
-        rest = [keep.tile([P, PACK, CHUNK], BF16, name=f"rest{c}") for c in range(CHUNKS)]
-
-        def quantize(woven, codes, plane, fmt, cols):
+        def quantize(woven, codes, scale, fmt, cols):
             nc.vector.quantize_mx(
-                out=codes[:, cols].bitcast(fmt), scales=plane[:, cols], in_=woven[:, cols, :].rearrange("p j t -> p (j t)")
+                out=codes[:, cols].bitcast(fmt), scales=scale[:, cols], in_=woven[:, cols, :].rearrange("p j t -> p (j t)")
             )
 
-        halves = [slice(0, HALF), slice(HALF, CHUNK)]
-        whole = slice(0, CHUNK)
         back = {}
         dx = {}
+        dx_sbuf = {}
+        scaled = {}
 
         def read_back(c):
             for t in range(PACK):
@@ -129,80 +127,112 @@ def tile_list_embg_tgq4_res_kernel(tc, dy, w_words, w_scales, res, wgo, offs, ou
                 nc.tensor.matmul_mx(
                     out=back[c, t][:],
                     lhsT=eye_codes[:, cols].bitcast(E4M3),
-                    lhsT_scale=eye_plane[:, cols],
+                    lhsT_scale=eye_scale[:, cols],
                     rhs=q_codes[c][:].bitcast(E5M2),
-                    rhs_scale=q_plane[c][:],
+                    rhs_scale=q_scale[c][:],
                     start=True,
                     stop=True,
                 )
 
-        def subtract(c):
-            for t in range(PACK):
-                nc.vector.tensor_tensor(
-                    out=rest[c][:, t, :].rearrange("p (h j) -> p h j", h=2),
-                    in0=raw[c][:, :, t, :],
-                    in1=back[c, t][:].rearrange("p (h j) -> p h j", h=2),
-                    op=ALU.subtract,
-                )
+        def subtract(c, t):
+            nc.vector.tensor_tensor(
+                out=rest[c][:, :, t, :],
+                in0=raw[c][:, :, t, :],
+                in1=back[c, t][:].rearrange("p (h j) -> p h j", h=2),
+                op=ALU.subtract,
+            )
 
-        def product(c, i, first):
-            if first:
-                dx[c, i] = psum_dx.tile([P, CHUNK], F32, name="dx")
-            codes, plane, fmt = (q_codes, q_plane, E5M2) if first else (r_codes, r_plane, E4M3)
+        def subtract_half(c, t, h):
+            nc.vector.tensor_tensor(
+                out=rest[c][:, h, t, :], in0=raw[c][:, h, t, :], in1=back[c, t][:, halves[h]], op=ALU.subtract
+            )
+
+        def product(c, i, codes, scale, fmt, first):
             nc.tensor.matmul_mx(
                 out=dx[c, i][:],
                 lhsT=w_codes[:, 2 * P * i : 2 * P * (i + 1)].bitcast(E2M1),
-                lhsT_scale=w_plane[:, P * i : P * (i + 1)],
+                lhsT_scale=w_scale[:, P * i : P * (i + 1)],
                 rhs=codes[c][:].bitcast(fmt),
-                rhs_scale=plane[c][:],
+                rhs_scale=scale[c][:],
                 start=first,
                 stop=not first,
             )
 
-        def place(c, i):
+        def open_sum(c, i):
+            dx[c, i] = psum_dx.tile([P, CHUNK], F32, name="dx")
+            product(c, i, q_codes, q_scale, E5M2, True)
+
+        def close_sum(c, i):
+            product(c, i, r_codes, r_scale, E4M3, False)
+
+        def empty_bank(c, i):
+            dx_sbuf[c, i] = keep.tile([P, CHUNK], F32, name=f"dx_sbuf{c}{i}")
+            nc.scalar.copy(out=dx_sbuf[c, i][:], in_=dx[c, i][:])
+
+        product_tags = {order[1]: "r_codes1", order[2]: "rest1", order[3]: "r_woven1"}
+
+        def finish(c, i):
             total = ring.tile([P, CHUNK], F32, name="total")
-            scaled = ring.tile([P, CHUNK], F32, name="scaled")
-            if (c, i) == (0, 0):
-                nc.vector.tensor_tensor(out=total[:], in0=dx[c, i][:], in1=skips[c, i][:], op=ALU.add)
-                nc.vector.tensor_tensor(out=scaled[:], in0=total[:], in1=weights[c][:], op=ALU.mult)
+            if (c, i) in product_tags:
+                scaled[c, i] = held_tile([P, CHUNK], F32, f"scaled{c}{i}", product_tags[c, i])
             else:
-                sums = ring.tile([P, CHUNK], F32, name="sums")
-                nc.scalar.copy(out=sums[:], in_=dx[c, i][:])
-                nc.gpsimd.tensor_tensor(out=total[:], in0=sums[:], in1=skips[c, i][:], op=ALU.add)
-                nc.gpsimd.tensor_tensor(out=scaled[:], in0=total[:], in1=weights[c][:], op=ALU.mult)
-            entries = offsets[:, c * CHUNK // 16 : (c + 1) * CHUNK // 16]
-            nc.vector.tensor_copy(out=pages[i][:].indirect(entries), in_=scaled[:])
+                scaled[c, i] = ring.tile([P, CHUNK], F32, name="scaled")
+            engine, sums = (nc.vector, dx) if (c, i) == order[0] else (nc.gpsimd, dx_sbuf)
+            engine.tensor_tensor(out=total[:], in0=sums[c, i][:], in1=residual[c, i][:], op=ALU.add)
+            engine.tensor_tensor(out=scaled[c, i][:], in0=total[:], in1=weights[c][:], op=ALU.mult)
+
+        def place(c, i):
+            entries = offsets[:, c * CHUNK // GROUP : (c + 1) * CHUNK // GROUP]
+            nc.vector.tensor_copy(out=pages[i][:].indirect(entries), in_=scaled[c, i][:])
             if c == CHUNKS - 1:
                 nc.sync.dma_start(out=out[i * P : (i + 1) * P, :], in_=pages[i][:])
 
         for h in range(2):
-            weave(nc.vector.tensor_copy, q_woven[0][:, halves[h], :], raw[0][:, h])
-            quantize(q_woven[0], q_codes[0], q_plane[0], E5M2, halves[h])
-        clear_page(1)
+            weave(nc.vector.tensor_copy, q_woven[0], raw[0], h, 0, HALF)
+            quantize(q_woven[0], q_codes[0], q_scale[0], E5M2, halves[h])
+        pages[2] = held_tile([P, T], F32, "page2", "page2")
+        nc.vector.memset(pages[2][:].bitcast(I32), 0)
         read_back(0)
-        for i in range(ROW_TILES):
-            product(0, i, True)
         for h in range(2):
-            weave(nc.scalar.copy, q_woven[1][:, halves[h], :], raw[1][:, h])
-        subtract(0)
-        weave(nc.vector.tensor_copy, r_woven[0][:, halves[0], :], rest[0][:, :, halves[0]])
-        weave(nc.scalar.copy, r_woven[0][:, halves[1], :], rest[0][:, :, halves[1]])
-        for h in range(2):
-            quantize(r_woven[0], r_codes[0], r_plane[0], E4M3, halves[h])
-        clear_page(2)
+            weave(nc.scalar.copy, q_woven[1], raw[1], h, 0, HALF)
+
+        for t in range(PACK - 1):
+            subtract(0, t)
+        subtract_half(0, PACK - 1, 0)
+        weave(nc.scalar.copy, r_woven[0], rest[0], 0, 0, SCALAR_TOKENS)
+        subtract_half(0, PACK - 1, 1)
+        quantize(q_woven[1], q_codes[1], q_scale[1], E5M2, whole)
         for i in range(ROW_TILES):
-            product(0, i, False)
-        quantize(q_woven[1], q_codes[1], q_plane[1], E5M2, whole)
+            open_sum(0, i)
         read_back(1)
+        weave(nc.vector.tensor_copy, r_woven[0], rest[0], 0, SCALAR_TOKENS, HALF)
+        weave(nc.vector.tensor_copy, r_woven[0], rest[0], 1, 0, HALF)
+        for h in range(2):
+            quantize(r_woven[0], r_codes[0], r_scale[0], E4M3, halves[h])
+
+        pages[3] = held_tile([P, T], F32, "page3", "page3")
+        nc.gpsimd.memset(pages[3][:].bitcast(I32), 0)
+        close_sum(0, 0)
+        close_sum(0, 1)
+        finish(0, 0)
+        empty_bank(0, 1)
+        for t in range(PACK):
+            subtract(1, t)
         place(0, 0)
-        subtract(1)
-        weave(nc.scalar.copy, r_woven[1][:], rest[1][:])
+        for i in range(2, ROW_TILES):
+            close_sum(0, i)
+            empty_bank(0, i)
+        for h in range(2):
+            weave(nc.scalar.copy, r_woven[1], rest[1], h, 0, HALF)
+        finish(0, 1)
         place(0, 1)
-        quantize(r_woven[1], r_codes[1], r_plane[1], E4M3, whole)
-        place(0, 2)
-        clear_page(3)
-        place(0, 3)
+
+        r_codes[1] = held_tile([P, CHUNK], U32, "r_codes1", "r_codes1")
+        quantize(r_woven[1], r_codes[1], r_scale[1], E4M3, whole)
         for i in range(ROW_TILES):
-            product(1, i, True)
-            product(1, i, False)
-            place(1, i)
+            open_sum(1, i)
+            close_sum(1, i)
+            empty_bank(1, i)
+        for c, i in order[2:]:
+            finish(c, i)
+            place(c, i)

@@ -1,7 +1,6 @@
 from contextlib import ExitStack
 
 import concourse.mybir as mybir
-from concourse.masks import make_identity
 
 K, N, T, J = 512, 512, 2048, 1024
 FLOPS = 3 * 2 * K * N * J
@@ -16,6 +15,7 @@ E4M3 = mybir.dt.float8_e4m3fn_x4
 E5M2 = mybir.dt.float8_e5m2_x4
 E2M1 = mybir.dt.float4_e2m1fn_x4
 ALU = mybir.AluOpType
+COPY = mybir.ActivationFunctionType.Copy
 
 P = 128
 PACK = 4
@@ -25,7 +25,7 @@ CHUNK = 512
 HALF = CHUNK // 2
 CHUNKS = J // CHUNK
 ROW_TILES = N // P
-SCALAR_TOKENS = 128
+SCALAR_TOKENS = 192
 MX_ALIGN = 64
 
 
@@ -34,8 +34,10 @@ def tile_list_embg_tgq4_res_kernel(tc, dy, w_words, w_scales, res, wgo, offs, ou
     with ExitStack() as ctx:
         keep = ctx.enter_context(tc.tile_pool(name="keep", bufs=1))
         ring = ctx.enter_context(tc.tile_pool(name="ring", bufs=3))
-        psum_back = ctx.enter_context(tc.psum_pool(name="psum_back", bufs=PACK))
-        psum_dx = ctx.enter_context(tc.psum_pool(name="psum_dx", bufs=ROW_TILES))
+        psum = ctx.enter_context(tc.psum_pool(name="psum", bufs=1))
+
+        def bank(b, name):
+            return psum.tile([P, CHUNK], F32, name=name, tag=f"bank{b}")
 
         def held_tile(shape, dtype, name, tag):
             return keep.tile(shape, dtype, name=name, tag=tag, align_bytes=MX_ALIGN)
@@ -68,7 +70,7 @@ def tile_list_embg_tgq4_res_kernel(tc, dy, w_words, w_scales, res, wgo, offs, ou
         load_dy(0)
         nc.sync.dma_start(out=w_codes[:].bitcast(I32), in_=w_words[0].bitcast(I32))
         for q in range(QUADRANTS):
-            nc.scalar.dma_start(
+            nc.sync.dma_start(
                 out=w_scale[32 * q : 32 * q + 4, :].bitcast(I32), in_=w_scales[0, 4 * q : 4 * q + 4, :].bitcast(I32)
             )
         load_dy(1)
@@ -81,34 +83,44 @@ def tile_list_embg_tgq4_res_kernel(tc, dy, w_words, w_scales, res, wgo, offs, ou
         for i in range(ROW_TILES):
             load_residual(1, i)
 
-        eye = keep.tile([P, P], BF16, name="eye")
-        make_identity(nc, eye[:])
-        pitch = PACK * P + 1
-        eye_woven = keep.tile([P, PACK * pitch], BF16, name="eye_woven", align_bytes=MX_ALIGN)
-        nc.vector.memset(eye_woven[:].bitcast(I32), 0)
-        pages = {i: keep.tile([P, T], F32, name=f"page{i}") for i in range(2)}
-        for i in range(2):
-            nc.vector.memset(pages[i][:].bitcast(I32), 0)
-        diagonals = eye_woven[:].rearrange("p (t s) -> p t s", s=pitch)[:, :, 0 : PACK * P : PACK]
-        nc.scalar.copy(out=diagonals, in_=eye[:].unsqueeze(1).to_broadcast([P, PACK, P]))
+        ones_at = keep.tile([P, K + 2 * PACK], BF16, name="ones_at")
+        nc.gpsimd.memset(ones_at[:], 0.0)
+        nc.gpsimd.affine_select(
+            out=ones_at[:], in_=ones_at[:], compare_op=ALU.not_equal, fill=1.0, base=-(PACK - 1),
+            pattern=[[1, K + 2 * PACK]], channel_multiplier=-PACK,
+        )
+        eye_woven = keep.tile([P, PACK * K], BF16, name="eye_woven", align_bytes=MX_ALIGN)
+        pages = {0: keep.tile([P, T], F32, name="page0")}
+        nc.vector.memset(pages[0][:].bitcast(I32), 0)
+        for t in range(PACK):
+            nc.vector.tensor_copy(out=eye_woven[:, t * K : (t + 1) * K], in_=ones_at[:, PACK - 1 - t : PACK - 1 - t + K])
+        eye = keep.tile([P, P], F32, name="eye")
+        nc.scalar.copy(out=eye[:], in_=ones_at[:, PACK - 1 : K + PACK - 1 : PACK])
         eye_codes = keep.tile([P, K], U32, name="eye_codes", align_bytes=MX_ALIGN)
-        eye_scale = keep.tile([P, K], U8, name="eye_scale", align_bytes=MX_ALIGN)
-        nc.vector.quantize_mx(out=eye_codes[:].bitcast(E4M3), scales=eye_scale[:], in_=eye_woven[:, 0 : PACK * K])
+        first_scale = held_tile([P, P], U8, "first_scale", "page2")
+        eye_scale = keep.tile([P, K - P], U8, name="eye_scale", align_bytes=MX_ALIGN)
+        for t0, t1, scales in ((0, 1, first_scale[:]), (1, 2, eye_scale[:, 0:P]), (2, 4, eye_scale[:, P : 3 * P])):
+            nc.vector.quantize_mx(
+                out=eye_codes[:, t0 * P : t1 * P].bitcast(E4M3), scales=scales, in_=eye_woven[:, t0 * K : t1 * K]
+            )
 
         def chunk_tiles(dtype, name, chunks):
             return {c: keep.tile([P, CHUNK], dtype, name=f"{name}{c}", align_bytes=MX_ALIGN) for c in chunks}
 
         woven_shape = [P, CHUNK, PACK]
-        q_woven = [held_tile(woven_shape, BF16, "q_woven0", "page2"), held_tile(woven_shape, BF16, "q_woven1", "q_woven1")]
-        r_woven = [held_tile(woven_shape, BF16, "r_woven0", "page3"), held_tile(woven_shape, BF16, "r_woven1", "r_woven1")]
-        q_codes = chunk_tiles(U32, "q_codes", range(CHUNKS))
+        q_woven = [held_tile(woven_shape, BF16, "q_woven0", "page1"), held_tile(woven_shape, BF16, "q_woven1", "page3")]
+        r_woven = [held_tile(woven_shape, BF16, "r_woven0", "r_woven0"), held_tile(woven_shape, BF16, "r_woven1", "r_woven1")]
+        q_codes = chunk_tiles(U32, "q_codes", range(1))
         q_scale = chunk_tiles(U8, "q_scale", range(CHUNKS))
         r_codes = chunk_tiles(U32, "r_codes", range(1))
         r_scale = chunk_tiles(U8, "r_scale", range(CHUNKS))
-        rest = [held_tile([P, 2, PACK, HALF], BF16, f"rest{c}", f"rest{c}") for c in range(CHUNKS)]
+        rest = keep.tile([P, 2, PACK, HALF], BF16, name="rest")
 
         def weave(copy, woven, rows, h, j0, j1):
-            copy(out=woven[:, h * HALF + j0 : h * HALF + j1, :], in_=rows[:, h, :, j0:j1].rearrange("p t j -> p j t"))
+            copy(
+                out=woven[:, h * HALF + j0 : h * HALF + j1, :].rearrange("p (c i) t -> p c t i", i=PACK),
+                in_=rows[:, h, :, j0:j1].rearrange("p t (c i) -> p c t i", i=PACK),
+            )
 
         def quantize(woven, codes, scale, fmt, cols):
             nc.vector.quantize_mx(
@@ -122,29 +134,29 @@ def tile_list_embg_tgq4_res_kernel(tc, dy, w_words, w_scales, res, wgo, offs, ou
 
         def read_back(c):
             for t in range(PACK):
-                back[c, t] = psum_back.tile([P, CHUNK], F32, name="back")
+                back[c, t] = bank(t, f"back{c}{t}")
                 cols = slice(t * P, (t + 1) * P)
                 nc.tensor.matmul_mx(
                     out=back[c, t][:],
                     lhsT=eye_codes[:, cols].bitcast(E4M3),
-                    lhsT_scale=eye_scale[:, cols],
+                    lhsT_scale=first_scale[:] if (c, t) == (0, 0) else eye_scale[:, max(t - 1, 0) * P : max(t, 1) * P],
                     rhs=q_codes[c][:].bitcast(E5M2),
                     rhs_scale=q_scale[c][:],
                     start=True,
                     stop=True,
                 )
 
-        def subtract(c, t):
+        def subtract(t):
             nc.vector.tensor_tensor(
-                out=rest[c][:, :, t, :],
-                in0=raw[c][:, :, t, :],
-                in1=back[c, t][:].rearrange("p (h j) -> p h j", h=2),
+                out=rest[:, :, t, :],
+                in0=raw[0][:, :, t, :],
+                in1=back[0, t][:].rearrange("p (h j) -> p h j", h=2),
                 op=ALU.subtract,
             )
 
-        def subtract_half(c, t, h):
+        def subtract_half(t, h):
             nc.vector.tensor_tensor(
-                out=rest[c][:, h, t, :], in0=raw[c][:, h, t, :], in1=back[c, t][:, halves[h]], op=ALU.subtract
+                out=rest[:, h, t, :], in0=raw[0][:, h, t, :], in1=back[0, t][:, halves[h]], op=ALU.subtract
             )
 
         def product(c, i, codes, scale, fmt, first):
@@ -159,80 +171,135 @@ def tile_list_embg_tgq4_res_kernel(tc, dy, w_words, w_scales, res, wgo, offs, ou
             )
 
         def open_sum(c, i):
-            dx[c, i] = psum_dx.tile([P, CHUNK], F32, name="dx")
+            dx[c, i] = bank(PACK + i, f"dx{c}{i}")
             product(c, i, q_codes, q_scale, E5M2, True)
 
         def close_sum(c, i):
             product(c, i, r_codes, r_scale, E4M3, False)
 
-        def empty_bank(c, i):
+        def empty_bank(c, i, parts=(whole,)):
             dx_sbuf[c, i] = keep.tile([P, CHUNK], F32, name=f"dx_sbuf{c}{i}")
-            nc.scalar.copy(out=dx_sbuf[c, i][:], in_=dx[c, i][:])
+            for cols in parts:
+                nc.scalar.copy(out=dx_sbuf[c, i][:, cols], in_=dx[c, i][:, cols])
 
-        product_tags = {order[1]: "r_codes1", order[2]: "rest1", order[3]: "r_woven1"}
+        product_tags = {order[1]: "r_codes1", order[2]: "turned3", order[3]: "r_woven1"}
 
-        def finish(c, i):
+        def finish(c, i, parts=(whole,)):
             total = ring.tile([P, CHUNK], F32, name="total")
             if (c, i) in product_tags:
                 scaled[c, i] = held_tile([P, CHUNK], F32, f"scaled{c}{i}", product_tags[c, i])
             else:
                 scaled[c, i] = ring.tile([P, CHUNK], F32, name="scaled")
             engine, sums = (nc.vector, dx) if (c, i) == order[0] else (nc.gpsimd, dx_sbuf)
-            engine.tensor_tensor(out=total[:], in0=sums[c, i][:], in1=residual[c, i][:], op=ALU.add)
-            engine.tensor_tensor(out=scaled[c, i][:], in0=total[:], in1=weights[c][:], op=ALU.mult)
+            for cols in parts:
+                engine.tensor_tensor(out=total[:, cols], in0=sums[c, i][:, cols], in1=residual[c, i][:, cols], op=ALU.add)
+                engine.tensor_tensor(out=scaled[c, i][:, cols], in0=total[:, cols], in1=weights[c][:, cols], op=ALU.mult)
 
-        def place(c, i):
-            entries = offsets[:, c * CHUNK // GROUP : (c + 1) * CHUNK // GROUP]
-            nc.vector.tensor_copy(out=pages[i][:].indirect(entries), in_=scaled[c, i][:])
+        def place(c, i, parts=(whole,)):
+            for cols in parts:
+                entries = offsets[:, (c * CHUNK + cols.start) // GROUP : (c * CHUNK + cols.stop) // GROUP]
+                nc.vector.tensor_copy(out=pages[i][:].indirect(entries), in_=scaled[c, i][:, cols])
             if c == CHUNKS - 1:
                 nc.sync.dma_start(out=out[i * P : (i + 1) * P, :], in_=pages[i][:])
 
-        for h in range(2):
-            weave(nc.vector.tensor_copy, q_woven[0], raw[0], h, 0, HALF)
-            quantize(q_woven[0], q_codes[0], q_scale[0], E5M2, halves[h])
-        pages[2] = held_tile([P, T], F32, "page2", "page2")
-        nc.vector.memset(pages[2][:].bitcast(I32), 0)
+        def clear(i, q):
+            nc.gpsimd.memset(pages[i][:, q * CHUNK : (q + 1) * CHUNK].bitcast(I32), 0)
+
+        weave(nc.scalar.copy, q_woven[0], raw[0], 0, 0, 128)
+        weave(nc.vector.tensor_copy, q_woven[0], raw[0], 0, 128, HALF)
+        quantize(q_woven[0], q_codes[0], q_scale[0], E5M2, halves[0])
+        weave(nc.scalar.copy, q_woven[0], raw[0], 1, 0, 96)
+        weave(nc.vector.tensor_copy, q_woven[0], raw[0], 1, 96, HALF)
+        quantize(q_woven[0], q_codes[0], q_scale[0], E5M2, halves[1])
+        pages[1] = held_tile([P, T], F32, "page1", "page1")
+        nc.vector.memset(pages[1][:].bitcast(I32), 0)
         read_back(0)
+        pages[2] = held_tile([P, T], F32, "page2", "page2")
+        for q in range(4):
+            clear(2, q)
         for h in range(2):
             weave(nc.scalar.copy, q_woven[1], raw[1], h, 0, HALF)
 
         for t in range(PACK - 1):
-            subtract(0, t)
-        subtract_half(0, PACK - 1, 0)
-        weave(nc.scalar.copy, r_woven[0], rest[0], 0, 0, SCALAR_TOKENS)
-        subtract_half(0, PACK - 1, 1)
-        quantize(q_woven[1], q_codes[1], q_scale[1], E5M2, whole)
+            subtract(t)
+        subtract_half(PACK - 1, 0)
+        weave(nc.scalar.copy, r_woven[0], rest, 0, 0, SCALAR_TOKENS)
+        subtract_half(PACK - 1, 1)
         for i in range(ROW_TILES):
             open_sum(0, i)
-        read_back(1)
-        weave(nc.vector.tensor_copy, r_woven[0], rest[0], 0, SCALAR_TOKENS, HALF)
-        weave(nc.vector.tensor_copy, r_woven[0], rest[0], 1, 0, HALF)
+        weave(nc.vector.tensor_copy, r_woven[0], rest, 0, SCALAR_TOKENS, HALF)
+        weave(nc.vector.tensor_copy, r_woven[0], rest, 1, 0, HALF)
         for h in range(2):
             quantize(r_woven[0], r_codes[0], r_scale[0], E4M3, halves[h])
+        q_codes[1] = held_tile([P, CHUNK], U32, "q_codes1", "r_woven0")
+        quantize(q_woven[1], q_codes[1], q_scale[1], E5M2, whole)
 
-        pages[3] = held_tile([P, T], F32, "page3", "page3")
-        nc.gpsimd.memset(pages[3][:].bitcast(I32), 0)
         close_sum(0, 0)
         close_sum(0, 1)
         finish(0, 0)
-        empty_bank(0, 1)
-        for t in range(PACK):
-            subtract(1, t)
         place(0, 0)
+        empty_bank(0, 1)
+        read_back(1)
+        pages[3] = held_tile([P, T], F32, "page3", "page3")
+        clear(3, 0)
+        clear(3, 1)
+        finish(0, 1)
+        place(0, 1)
         for i in range(2, ROW_TILES):
             close_sum(0, i)
             empty_bank(0, i)
+
+        blocks = CHUNK // P
+        diff = {}
+        for b in range(blocks):
+            diff[b] = bank(PACK + b, f"diff{b}")
+            h, j0 = divmod(b * P, HALF)
+            for t in range(PACK):
+                nc.tensor.matmul(
+                    out=diff[b][:, t * P : (t + 1) * P], lhsT=raw[1][:, h, t, j0 : j0 + P], rhs=eye[:], start=t == 0, stop=False, is_transpose=True
+                )
+        minus = [keep.tile([P, PACK, HALF], F32, name=f"minus{h}") for h in range(2)]
         for h in range(2):
-            weave(nc.scalar.copy, r_woven[1], rest[1], h, 0, HALF)
-        finish(0, 1)
-        place(0, 1)
+            for t in range(PACK):
+                nc.scalar.activation(out=minus[h][:, t, :], in_=back[1, t][:, halves[h]], func=COPY, scale=-1.0)
+        clear(3, 2)
+        clear(3, 3)
+
+        turned = {}
+
+        def turn(b):
+            h, j0 = divmod(b * P, HALF)
+            for t in range(PACK):
+                nc.tensor.matmul(
+                    out=diff[b][:, t * P : (t + 1) * P], lhsT=minus[h][:, t, j0 : j0 + P], rhs=eye[:], start=False, stop=t == PACK - 1, is_transpose=True
+                )
+            turned[b] = held_tile([P, 2, P, 2], BF16, f"turned{b}", f"turned{b}")
+            nc.scalar.copy(out=turned[b][:], in_=diff[b][:].rearrange("j (u e p) -> j u p e", u=2, e=2))
+
+        def turn_back(b):
+            pairs = bank(b, f"pairs{b}")
+            words = turned[b][:].rearrange("j u p e -> j (u p e)").bitcast(F32)
+            for u in range(2):
+                nc.tensor.transpose(pairs[:, u * P : (u + 1) * P], words[:, u * P : (u + 1) * P], eye[:])
+            nc.scalar.copy(
+                out=r_woven[1][:, b * P : (b + 1) * P, :].rearrange("p j t -> p (j t)").bitcast(F32).rearrange("p (j u) -> p j u", u=2),
+                in_=pairs[:, 0 : 2 * P].rearrange("p (u j) -> p j u", u=2),
+            )
+
+        for b in range(blocks):
+            turn(b)
+        for b in range(blocks):
+            turn_back(b)
+        for i in range(ROW_TILES):
+            open_sum(1, i)
 
         r_codes[1] = held_tile([P, CHUNK], U32, "r_codes1", "r_codes1")
         quantize(r_woven[1], r_codes[1], r_scale[1], E4M3, whole)
+        for i in range(2, ROW_TILES):
+            finish(0, i)
+            place(0, i)
         for i in range(ROW_TILES):
-            open_sum(1, i)
             close_sum(1, i)
             empty_bank(1, i)
-        for c, i in order[2:]:
-            finish(c, i)
-            place(c, i)
+            finish(1, i)
+            place(1, i)

@@ -34,6 +34,12 @@ def tile_list_embg_tgq4_res_kernel(tc, dy, w_words, w_scales, res, wgo, offs, ou
     with ExitStack() as ctx:
         keep = ctx.enter_context(tc.tile_pool(name="keep", bufs=1))
         ring = ctx.enter_context(tc.tile_pool(name="ring", bufs=3))
+        shared = ctx.enter_context(tc.tile_pool(name="shared", bufs=1))
+        page_bytes = 4 * T
+
+        def placed_tile(shape, dtype, name, offset):
+            return shared.tile(shape, dtype, name=name, offset=offset, align_bytes=MX_ALIGN)
+
         psum = ctx.enter_context(tc.psum_pool(name="psum", bufs=1))
 
         def bank(b, name):
@@ -83,34 +89,31 @@ def tile_list_embg_tgq4_res_kernel(tc, dy, w_words, w_scales, res, wgo, offs, ou
         for i in range(ROW_TILES):
             load_residual(1, i)
 
-        ones_at = keep.tile([P, K + 2 * PACK], BF16, name="ones_at")
+        ones_at = placed_tile([P, K + 2 * PACK], BF16, "ones_at", page_bytes - K)
         nc.gpsimd.memset(ones_at[:], 0.0)
         nc.gpsimd.affine_select(
             out=ones_at[:], in_=ones_at[:], compare_op=ALU.not_equal, fill=1.0, base=-(PACK - 1),
             pattern=[[1, K + 2 * PACK]], channel_multiplier=-PACK,
         )
-        eye_woven = keep.tile([P, PACK * K], BF16, name="eye_woven", align_bytes=MX_ALIGN)
-        pages = {0: keep.tile([P, T], F32, name="page0")}
-        nc.vector.memset(pages[0][:].bitcast(I32), 0)
+        eye_woven = held_tile([P, PACK * K], BF16, "eye_woven", "q_codes0")
+        pages = {i: keep.tile([P, T], F32, name=f"page{i}") for i in (0, 2)}
+        for i in (0, 2):
+            nc.vector.memset(pages[i][:].bitcast(I32), 0)
         for t in range(PACK):
-            nc.vector.tensor_copy(out=eye_woven[:, t * K : (t + 1) * K], in_=ones_at[:, PACK - 1 - t : PACK - 1 - t + K])
+            nc.scalar.copy(out=eye_woven[:, t * K : (t + 1) * K], in_=ones_at[:, PACK - 1 - t : PACK - 1 - t + K])
         eye = keep.tile([P, P], F32, name="eye")
         nc.scalar.copy(out=eye[:], in_=ones_at[:, PACK - 1 : K + PACK - 1 : PACK])
         eye_codes = keep.tile([P, K], U32, name="eye_codes", align_bytes=MX_ALIGN)
-        first_scale = held_tile([P, P], U8, "first_scale", "page2")
-        eye_scale = keep.tile([P, K - P], U8, name="eye_scale", align_bytes=MX_ALIGN)
-        for t0, t1, scales in ((0, 1, first_scale[:]), (1, 2, eye_scale[:, 0:P]), (2, 4, eye_scale[:, P : 3 * P])):
-            nc.vector.quantize_mx(
-                out=eye_codes[:, t0 * P : t1 * P].bitcast(E4M3), scales=scales, in_=eye_woven[:, t0 * K : t1 * K]
-            )
+        eye_scale = keep.tile([P, K], U8, name="eye_scale", align_bytes=MX_ALIGN)
+        nc.vector.quantize_mx(out=eye_codes[:].bitcast(E4M3), scales=eye_scale[:], in_=eye_woven[:])
 
         def chunk_tiles(dtype, name, chunks):
             return {c: keep.tile([P, CHUNK], dtype, name=f"{name}{c}", align_bytes=MX_ALIGN) for c in chunks}
 
         woven_shape = [P, CHUNK, PACK]
-        q_woven = [held_tile(woven_shape, BF16, "q_woven0", "page1"), held_tile(woven_shape, BF16, "q_woven1", "page3")]
+        q_woven = [placed_tile(woven_shape, BF16, "q_woven0", page_bytes // 2), placed_tile(woven_shape, BF16, "q_woven1", page_bytes)]
         r_woven = [held_tile(woven_shape, BF16, "r_woven0", "r_woven0"), held_tile(woven_shape, BF16, "r_woven1", "r_woven1")]
-        q_codes = chunk_tiles(U32, "q_codes", range(1))
+        q_codes = {0: held_tile([P, CHUNK], U32, "q_codes0", "q_codes0")}
         q_scale = chunk_tiles(U8, "q_scale", range(CHUNKS))
         r_codes = chunk_tiles(U32, "r_codes", range(1))
         r_scale = chunk_tiles(U8, "r_scale", range(CHUNKS))
@@ -139,7 +142,7 @@ def tile_list_embg_tgq4_res_kernel(tc, dy, w_words, w_scales, res, wgo, offs, ou
                 nc.tensor.matmul_mx(
                     out=back[c, t][:],
                     lhsT=eye_codes[:, cols].bitcast(E4M3),
-                    lhsT_scale=first_scale[:] if (c, t) == (0, 0) else eye_scale[:, max(t - 1, 0) * P : max(t, 1) * P],
+                    lhsT_scale=eye_scale[:, cols],
                     rhs=q_codes[c][:].bitcast(E5M2),
                     rhs_scale=q_scale[c][:],
                     start=True,
@@ -193,6 +196,7 @@ def tile_list_embg_tgq4_res_kernel(tc, dy, w_words, w_scales, res, wgo, offs, ou
             engine, sums = (nc.vector, dx) if (c, i) == order[0] else (nc.gpsimd, dx_sbuf)
             for cols in parts:
                 engine.tensor_tensor(out=total[:, cols], in0=sums[c, i][:, cols], in1=residual[c, i][:, cols], op=ALU.add)
+            for cols in parts:
                 engine.tensor_tensor(out=scaled[c, i][:, cols], in0=total[:, cols], in1=weights[c][:, cols], op=ALU.mult)
 
         def place(c, i, parts=(whole,)):
@@ -205,18 +209,17 @@ def tile_list_embg_tgq4_res_kernel(tc, dy, w_words, w_scales, res, wgo, offs, ou
         def clear(i, q):
             nc.gpsimd.memset(pages[i][:, q * CHUNK : (q + 1) * CHUNK].bitcast(I32), 0)
 
-        weave(nc.scalar.copy, q_woven[0], raw[0], 0, 0, 128)
-        weave(nc.vector.tensor_copy, q_woven[0], raw[0], 0, 128, HALF)
+        weave(nc.scalar.copy, q_woven[0], raw[0], 0, 0, 160)
+        weave(nc.vector.tensor_copy, q_woven[0], raw[0], 0, 160, HALF)
         quantize(q_woven[0], q_codes[0], q_scale[0], E5M2, halves[0])
         weave(nc.scalar.copy, q_woven[0], raw[0], 1, 0, 96)
         weave(nc.vector.tensor_copy, q_woven[0], raw[0], 1, 96, HALF)
         quantize(q_woven[0], q_codes[0], q_scale[0], E5M2, halves[1])
-        pages[1] = held_tile([P, T], F32, "page1", "page1")
-        nc.vector.memset(pages[1][:].bitcast(I32), 0)
+        pages[1] = placed_tile([P, T], F32, "page1", 0)
+        nc.vector.memset(pages[1][:, 0 : T // 2].bitcast(I32), 0)
         read_back(0)
-        pages[2] = held_tile([P, T], F32, "page2", "page2")
-        for q in range(4):
-            clear(2, q)
+        clear(1, 2)
+        clear(1, 3)
         for h in range(2):
             weave(nc.scalar.copy, q_woven[1], raw[1], h, 0, HALF)
 
@@ -236,11 +239,11 @@ def tile_list_embg_tgq4_res_kernel(tc, dy, w_words, w_scales, res, wgo, offs, ou
 
         close_sum(0, 0)
         close_sum(0, 1)
-        finish(0, 0)
+        finish(0, 0, halves)
         place(0, 0)
         empty_bank(0, 1)
         read_back(1)
-        pages[3] = held_tile([P, T], F32, "page3", "page3")
+        pages[3] = placed_tile([P, T], F32, "page3", page_bytes)
         clear(3, 0)
         clear(3, 1)
         finish(0, 1)

@@ -16,6 +16,7 @@ E5M2 = mybir.dt.float8_e5m2_x4
 E2M1 = mybir.dt.float4_e2m1fn_x4
 ALU = mybir.AluOpType
 COPY = mybir.ActivationFunctionType.Copy
+IDENTITY = mybir.ActivationFunctionType.Identity
 
 P = 128
 PACK = 4
@@ -25,7 +26,7 @@ CHUNK = 512
 HALF = CHUNK // 2
 CHUNKS = J // CHUNK
 ROW_TILES = N // P
-SCALAR_TOKENS = 192
+SCALAR_TOKENS = 224
 MX_ALIGN = 64
 
 
@@ -72,7 +73,13 @@ def tile_list_embg_tgq4_res_kernel(tc, dy, w_words, w_scales, res, wgo, offs, ou
         def load_weights(c):
             nc.sync.dma_start(out=weights[c][:], in_=wgo[:, c * CHUNK : (c + 1) * CHUNK])
 
-        nc.vector.memset(w_scale[:].bitcast(I32), 0)
+        ones_at = placed_tile([P, K + 2 * PACK], BF16, "ones_at", page_bytes - K)
+        nc.gpsimd.memset(ones_at[:], 0.0)
+        nc.gpsimd.affine_select(
+            out=ones_at[:], in_=ones_at[:], compare_op=ALU.not_equal, fill=1.0, base=-(PACK - 1),
+            pattern=[[1, K + 2 * PACK]], channel_multiplier=-PACK,
+        )
+        nc.gpsimd.memset(w_scale[:].bitcast(I32), 0)
         load_dy(0)
         nc.sync.dma_start(out=w_codes[:].bitcast(I32), in_=w_words[0].bitcast(I32))
         for q in range(QUADRANTS):
@@ -89,18 +96,19 @@ def tile_list_embg_tgq4_res_kernel(tc, dy, w_words, w_scales, res, wgo, offs, ou
         for i in range(ROW_TILES):
             load_residual(1, i)
 
-        ones_at = placed_tile([P, K + 2 * PACK], BF16, "ones_at", page_bytes - K)
-        nc.gpsimd.memset(ones_at[:], 0.0)
-        nc.gpsimd.affine_select(
-            out=ones_at[:], in_=ones_at[:], compare_op=ALU.not_equal, fill=1.0, base=-(PACK - 1),
-            pattern=[[1, K + 2 * PACK]], channel_multiplier=-PACK,
-        )
         eye_woven = held_tile([P, PACK * K], BF16, "eye_woven", "q_codes0")
         pages = {i: keep.tile([P, T], F32, name=f"page{i}") for i in (0, 2)}
-        for i in (0, 2):
-            nc.vector.memset(pages[i][:].bitcast(I32), 0)
+
+        def clear(i, q):
+            nc.gpsimd.memset(pages[i][:, q * CHUNK : (q + 1) * CHUNK].bitcast(I32), 0)
+
+        for cols in (slice(0, T // 2 - 1), slice(T // 2 - 1, T)):
+            nc.vector.memset(pages[0][:, cols].bitcast(I32), 0)
+        clear(2, 0)
+        nc.gpsimd.memset(pages[2][:, CHUNK : 2 * CHUNK + 8].bitcast(I32), 0)
         for t in range(PACK):
-            nc.scalar.copy(out=eye_woven[:, t * K : (t + 1) * K], in_=ones_at[:, PACK - 1 - t : PACK - 1 - t + K])
+            copy = nc.vector.tensor_copy if t % 2 else nc.scalar.copy
+            copy(out=eye_woven[:, t * K : (t + 1) * K], in_=ones_at[:, PACK - 1 - t : PACK - 1 - t + K])
         eye = keep.tile([P, P], F32, name="eye")
         nc.scalar.copy(out=eye[:], in_=ones_at[:, PACK - 1 : K + PACK - 1 : PACK])
         eye_codes = keep.tile([P, K], U32, name="eye_codes", align_bytes=MX_ALIGN)
@@ -174,7 +182,7 @@ def tile_list_embg_tgq4_res_kernel(tc, dy, w_words, w_scales, res, wgo, offs, ou
             )
 
         def open_sum(c, i):
-            dx[c, i] = bank(PACK + i, f"dx{c}{i}")
+            dx[c, i] = bank(PACK + i if c == 0 else (6, 5, 0, 1)[i], f"dx{c}{i}")
             product(c, i, q_codes, q_scale, E5M2, True)
 
         def close_sum(c, i):
@@ -185,10 +193,14 @@ def tile_list_embg_tgq4_res_kernel(tc, dy, w_words, w_scales, res, wgo, offs, ou
             for cols in parts:
                 nc.scalar.copy(out=dx_sbuf[c, i][:, cols], in_=dx[c, i][:, cols])
 
-        product_tags = {order[1]: "r_codes1", order[2]: "turned3", order[3]: "r_woven1"}
+        product_tags = {order[1]: "r_codes1"}
+        sum_tags = {order[3]: "r_woven1"}
 
         def finish(c, i, parts=(whole,)):
-            total = ring.tile([P, CHUNK], F32, name="total")
+            if (c, i) in sum_tags:
+                total = held_tile([P, CHUNK], F32, f"total{c}{i}", sum_tags[c, i])
+            else:
+                total = ring.tile([P, CHUNK], F32, name="total")
             if (c, i) in product_tags:
                 scaled[c, i] = held_tile([P, CHUNK], F32, f"scaled{c}{i}", product_tags[c, i])
             else:
@@ -203,14 +215,14 @@ def tile_list_embg_tgq4_res_kernel(tc, dy, w_words, w_scales, res, wgo, offs, ou
             for cols in parts:
                 entries = offsets[:, (c * CHUNK + cols.start) // GROUP : (c * CHUNK + cols.stop) // GROUP]
                 nc.vector.tensor_copy(out=pages[i][:].indirect(entries), in_=scaled[c, i][:, cols])
-            if c == CHUNKS - 1:
+            if (c, i) == order[-1]:
+                for queue, cols in ((nc.sync, slice(0, T // 2)), (nc.scalar, slice(T // 2, T))):
+                    queue.dma_start(out=out[i * P : (i + 1) * P, cols], in_=pages[i][:, cols])
+            elif c == CHUNKS - 1:
                 nc.sync.dma_start(out=out[i * P : (i + 1) * P, :], in_=pages[i][:])
 
-        def clear(i, q):
-            nc.gpsimd.memset(pages[i][:, q * CHUNK : (q + 1) * CHUNK].bitcast(I32), 0)
-
-        weave(nc.scalar.copy, q_woven[0], raw[0], 0, 0, 160)
-        weave(nc.vector.tensor_copy, q_woven[0], raw[0], 0, 160, HALF)
+        weave(nc.scalar.copy, q_woven[0], raw[0], 0, 0, 128)
+        weave(nc.vector.tensor_copy, q_woven[0], raw[0], 0, 128, HALF)
         quantize(q_woven[0], q_codes[0], q_scale[0], E5M2, halves[0])
         weave(nc.scalar.copy, q_woven[0], raw[0], 1, 0, 96)
         weave(nc.vector.tensor_copy, q_woven[0], raw[0], 1, 96, HALF)
@@ -220,8 +232,14 @@ def tile_list_embg_tgq4_res_kernel(tc, dy, w_words, w_scales, res, wgo, offs, ou
         read_back(0)
         clear(1, 2)
         clear(1, 3)
-        for h in range(2):
-            weave(nc.scalar.copy, q_woven[1], raw[1], h, 0, HALF)
+
+        def copy_plus_zero(out, in_):
+            nc.scalar.activation(out=out, in_=in_, func=IDENTITY, bias=pages[2][:, T // 2 : T // 2 + 1])
+
+        weave(copy_plus_zero, q_woven[1], raw[1], 0, 0, HALF)
+        weave(nc.scalar.copy, q_woven[1], raw[1], 1, 0, HALF)
+        clear(2, 2)
+        clear(2, 3)
 
         for t in range(PACK - 1):
             subtract(t)
@@ -248,51 +266,68 @@ def tile_list_embg_tgq4_res_kernel(tc, dy, w_words, w_scales, res, wgo, offs, ou
         clear(3, 1)
         finish(0, 1)
         place(0, 1)
+        clear(3, 2)
+        clear(3, 3)
         for i in range(2, ROW_TILES):
             close_sum(0, i)
-            empty_bank(0, i)
 
         blocks = CHUNK // P
         diff = {}
-        for b in range(blocks):
-            diff[b] = bank(PACK + b, f"diff{b}")
+        minus = keep.tile([P, PACK, CHUNK], F32, name="minus")
+
+        def open_difference(b):
+            diff[b] = bank((4, 5, 0, 1)[b], f"diff{b}")
             h, j0 = divmod(b * P, HALF)
             for t in range(PACK):
                 nc.tensor.matmul(
                     out=diff[b][:, t * P : (t + 1) * P], lhsT=raw[1][:, h, t, j0 : j0 + P], rhs=eye[:], start=t == 0, stop=False, is_transpose=True
                 )
-        minus = [keep.tile([P, PACK, HALF], F32, name=f"minus{h}") for h in range(2)]
-        for h in range(2):
-            for t in range(PACK):
-                nc.scalar.activation(out=minus[h][:, t, :], in_=back[1, t][:, halves[h]], func=COPY, scale=-1.0)
-        clear(3, 2)
-        clear(3, 3)
+
+        def negate(t, cols):
+            nc.scalar.activation(out=minus[:, t, cols], in_=back[1, t][:, cols], func=COPY, scale=-1.0)
+
+        open_difference(0)
+        open_difference(1)
+        for t in range(PACK - 1):
+            negate(t, whole)
+        open_difference(2)
+        open_difference(3)
+        for cols in halves:
+            negate(PACK - 1, cols)
+        empty_bank(0, 2)
 
         turned = {}
 
         def turn(b):
-            h, j0 = divmod(b * P, HALF)
             for t in range(PACK):
                 nc.tensor.matmul(
-                    out=diff[b][:, t * P : (t + 1) * P], lhsT=minus[h][:, t, j0 : j0 + P], rhs=eye[:], start=False, stop=t == PACK - 1, is_transpose=True
+                    out=diff[b][:, t * P : (t + 1) * P], lhsT=minus[:, t, b * P : (b + 1) * P], rhs=eye[:], start=False, stop=t == PACK - 1, is_transpose=True
                 )
             turned[b] = held_tile([P, 2, P, 2], BF16, f"turned{b}", f"turned{b}")
             nc.scalar.copy(out=turned[b][:], in_=diff[b][:].rearrange("j (u e p) -> j u p e", u=2, e=2))
 
-        def turn_back(b):
-            pairs = bank(b, f"pairs{b}")
-            words = turned[b][:].rearrange("j u p e -> j (u p e)").bitcast(F32)
-            for u in range(2):
-                nc.tensor.transpose(pairs[:, u * P : (u + 1) * P], words[:, u * P : (u + 1) * P], eye[:])
+        def turn_back(bs, where):
+            n = len(bs)
+            pairs = bank(where, f"pairs{bs[0]}")
+            for k, b in enumerate(bs):
+                words = turned[b][:].rearrange("j u p e -> j (u p e)").bitcast(F32)
+                for u in range(2):
+                    at = (u * n + k) * P
+                    nc.tensor.transpose(pairs[:, at : at + P], words[:, u * P : (u + 1) * P], eye[:])
             nc.scalar.copy(
-                out=r_woven[1][:, b * P : (b + 1) * P, :].rearrange("p j t -> p (j t)").bitcast(F32).rearrange("p (j u) -> p j u", u=2),
-                in_=pairs[:, 0 : 2 * P].rearrange("p (u j) -> p j u", u=2),
+                out=r_woven[1][:, bs[0] * P : (bs[-1] + 1) * P, :].rearrange("p j t -> p (j t)").bitcast(F32).rearrange("p (j u) -> p j u", u=2),
+                in_=pairs[:, 0 : 2 * n * P].rearrange("p (u j) -> p j u", u=2),
             )
 
-        for b in range(blocks):
-            turn(b)
-        for b in range(blocks):
-            turn_back(b)
+        turn(0)
+        turn(1)
+        turn(2)
+        turn_back([0, 1], 2)
+        turn(3)
+        turn_back([2], 3)
+        turn_back([3], 4)
+        dx_sbuf[0, 3] = held_tile([P, CHUNK], F32, "dx_sbuf03", "turned3")
+        nc.scalar.activation(out=dx_sbuf[0, 3][:], in_=dx[0, 3][:], func=IDENTITY, bias=pages[2][:, 0:1])
         for i in range(ROW_TILES):
             open_sum(1, i)
 

@@ -1,6 +1,7 @@
 from contextlib import ExitStack
 
 import concourse.mybir as mybir
+from concourse.masks import make_identity
 
 K, N, T, J = 512, 512, 2048, 1024
 FLOPS = 3 * 2 * K * N * J
@@ -26,7 +27,7 @@ CHUNK = 512
 HALF = CHUNK // 2
 CHUNKS = J // CHUNK
 ROW_TILES = N // P
-SCALAR_TOKENS = 224
+SCALAR_TOKENS = 192
 MX_ALIGN = 64
 
 
@@ -73,20 +74,14 @@ def tile_list_embg_tgq4_res_kernel(tc, dy, w_words, w_scales, res, wgo, offs, ou
         def load_weights(c):
             nc.sync.dma_start(out=weights[c][:], in_=wgo[:, c * CHUNK : (c + 1) * CHUNK])
 
-        ones_at = placed_tile([P, K + 2 * PACK], BF16, "ones_at", page_bytes - K)
-        nc.gpsimd.memset(ones_at[:], 0.0)
-        nc.gpsimd.affine_select(
-            out=ones_at[:], in_=ones_at[:], compare_op=ALU.not_equal, fill=1.0, base=-(PACK - 1),
-            pattern=[[1, K + 2 * PACK]], channel_multiplier=-PACK,
-        )
-        nc.gpsimd.memset(w_scale[:].bitcast(I32), 0)
+        nc.vector.memset(w_scale[:].bitcast(I32), 0)
         load_dy(0)
+        load_dy(1)
         nc.sync.dma_start(out=w_codes[:].bitcast(I32), in_=w_words[0].bitcast(I32))
         for q in range(QUADRANTS):
             nc.sync.dma_start(
                 out=w_scale[32 * q : 32 * q + 4, :].bitcast(I32), in_=w_scales[0, 4 * q : 4 * q + 4, :].bitcast(I32)
             )
-        load_dy(1)
         load_residual(0, 0)
         load_weights(0)
         nc.sync.dma_start(offsets[:], offs)
@@ -96,24 +91,32 @@ def tile_list_embg_tgq4_res_kernel(tc, dy, w_words, w_scales, res, wgo, offs, ou
         for i in range(ROW_TILES):
             load_residual(1, i)
 
-        eye_woven = held_tile([P, PACK * K], BF16, "eye_woven", "q_codes0")
-        pages = {i: keep.tile([P, T], F32, name=f"page{i}") for i in (0, 2)}
+        pages = {0: keep.tile([P, T], F32, name="page0")}
 
         def clear(i, q):
             nc.gpsimd.memset(pages[i][:, q * CHUNK : (q + 1) * CHUNK].bitcast(I32), 0)
 
-        for cols in (slice(0, T // 2 - 1), slice(T // 2 - 1, T)):
-            nc.vector.memset(pages[0][:, cols].bitcast(I32), 0)
-        clear(2, 0)
-        nc.gpsimd.memset(pages[2][:, CHUNK : 2 * CHUNK + 8].bitcast(I32), 0)
+        seed = held_tile([P, P], BF16, "seed", "page2")
+        make_identity(nc, seed[:])
+        ones_at = placed_tile([P, K + 2 * PACK], BF16, "ones_at", page_bytes - K)
+        nc.vector.memset(ones_at[:].bitcast(I32), 0)
+        nc.vector.memset(pages[0][:].bitcast(I32), 0)
+        nc.vector.tensor_copy(out=ones_at[:, PACK - 1 : K + PACK - 1 : PACK], in_=seed[:])
+        eye_woven = held_tile([P, PACK * K], BF16, "eye_woven", "q_codes0")
         for t in range(PACK):
             copy = nc.vector.tensor_copy if t % 2 else nc.scalar.copy
             copy(out=eye_woven[:, t * K : (t + 1) * K], in_=ones_at[:, PACK - 1 - t : PACK - 1 - t + K])
+        pages[2] = held_tile([P, T], F32, "page2", "page2")
+        nc.vector.memset(pages[2][:].bitcast(I32), 0)
         eye = keep.tile([P, P], F32, name="eye")
         nc.scalar.copy(out=eye[:], in_=ones_at[:, PACK - 1 : K + PACK - 1 : PACK])
         eye_codes = keep.tile([P, K], U32, name="eye_codes", align_bytes=MX_ALIGN)
-        eye_scale = keep.tile([P, K], U8, name="eye_scale", align_bytes=MX_ALIGN)
-        nc.vector.quantize_mx(out=eye_codes[:].bitcast(E4M3), scales=eye_scale[:], in_=eye_woven[:])
+        first_scale = held_tile([P, P], U8, "first_scale", "page3")
+        eye_scale = keep.tile([P, K - P], U8, name="eye_scale", align_bytes=MX_ALIGN)
+        for t0, t1, scales in ((0, 1, first_scale[:]), (1, 2, eye_scale[:, 0:P]), (2, 4, eye_scale[:, P : 3 * P])):
+            nc.vector.quantize_mx(
+                out=eye_codes[:, t0 * P : t1 * P].bitcast(E4M3), scales=scales, in_=eye_woven[:, t0 * K : t1 * K]
+            )
 
         def chunk_tiles(dtype, name, chunks):
             return {c: keep.tile([P, CHUNK], dtype, name=f"{name}{c}", align_bytes=MX_ALIGN) for c in chunks}
@@ -145,12 +148,12 @@ def tile_list_embg_tgq4_res_kernel(tc, dy, w_words, w_scales, res, wgo, offs, ou
 
         def read_back(c):
             for t in range(PACK):
-                back[c, t] = bank(t, f"back{c}{t}")
+                back[c, t] = bank(t if c == 0 else (6, 7, 4, 5)[t], f"back{c}{t}")
                 cols = slice(t * P, (t + 1) * P)
                 nc.tensor.matmul_mx(
                     out=back[c, t][:],
                     lhsT=eye_codes[:, cols].bitcast(E4M3),
-                    lhsT_scale=eye_scale[:, cols],
+                    lhsT_scale=first_scale[:] if (c, t) == (0, 0) else eye_scale[:, max(t - 1, 0) * P : max(t, 1) * P],
                     rhs=q_codes[c][:].bitcast(E5M2),
                     rhs_scale=q_scale[c][:],
                     start=True,
@@ -182,7 +185,7 @@ def tile_list_embg_tgq4_res_kernel(tc, dy, w_words, w_scales, res, wgo, offs, ou
             )
 
         def open_sum(c, i):
-            dx[c, i] = bank(PACK + i if c == 0 else (6, 5, 0, 1)[i], f"dx{c}{i}")
+            dx[c, i] = bank(PACK + i if c == 0 else (5, 0, 7, 5)[i], f"dx{c}{i}")
             product(c, i, q_codes, q_scale, E5M2, True)
 
         def close_sum(c, i):
@@ -215,10 +218,7 @@ def tile_list_embg_tgq4_res_kernel(tc, dy, w_words, w_scales, res, wgo, offs, ou
             for cols in parts:
                 entries = offsets[:, (c * CHUNK + cols.start) // GROUP : (c * CHUNK + cols.stop) // GROUP]
                 nc.vector.tensor_copy(out=pages[i][:].indirect(entries), in_=scaled[c, i][:, cols])
-            if (c, i) == order[-1]:
-                for queue, cols in ((nc.sync, slice(0, T // 2)), (nc.scalar, slice(T // 2, T))):
-                    queue.dma_start(out=out[i * P : (i + 1) * P, cols], in_=pages[i][:, cols])
-            elif c == CHUNKS - 1:
+            if c == CHUNKS - 1:
                 nc.sync.dma_start(out=out[i * P : (i + 1) * P, :], in_=pages[i][:])
 
         weave(nc.scalar.copy, q_woven[0], raw[0], 0, 0, 128)
@@ -228,26 +228,34 @@ def tile_list_embg_tgq4_res_kernel(tc, dy, w_words, w_scales, res, wgo, offs, ou
         weave(nc.vector.tensor_copy, q_woven[0], raw[0], 1, 96, HALF)
         quantize(q_woven[0], q_codes[0], q_scale[0], E5M2, halves[1])
         pages[1] = placed_tile([P, T], F32, "page1", 0)
-        nc.vector.memset(pages[1][:, 0 : T // 2].bitcast(I32), 0)
+        nc.vector.memset(pages[1][:].bitcast(I32), 0)
         read_back(0)
-        clear(1, 2)
-        clear(1, 3)
-
-        def copy_plus_zero(out, in_):
-            nc.scalar.activation(out=out, in_=in_, func=IDENTITY, bias=pages[2][:, T // 2 : T // 2 + 1])
-
-        weave(copy_plus_zero, q_woven[1], raw[1], 0, 0, HALF)
-        weave(nc.scalar.copy, q_woven[1], raw[1], 1, 0, HALF)
-        clear(2, 2)
-        clear(2, 3)
+        pages[3] = held_tile([P, T], F32, "page3", "page3")
+        nc.vector.memset(pages[3][:, 0:264].bitcast(I32), 0)
+        nc.gpsimd.memset(pages[3][:, 256:].bitcast(I32), 0)
+        for h in range(2):
+            weave(nc.scalar.copy, q_woven[1], raw[1], h, 0, HALF)
 
         for t in range(PACK - 1):
             subtract(t)
         subtract_half(PACK - 1, 0)
         weave(nc.scalar.copy, r_woven[0], rest, 0, 0, SCALAR_TOKENS)
         subtract_half(PACK - 1, 1)
-        for i in range(ROW_TILES):
+        diff = {}
+        minus = keep.tile([P, PACK, CHUNK], F32, name="minus")
+
+        def open_difference(b):
+            diff[b] = bank(b, f"diff{b}")
+            h, j0 = divmod(b * P, HALF)
+            for t in range(PACK):
+                nc.tensor.matmul(
+                    out=diff[b][:, t * P : (t + 1) * P], lhsT=raw[1][:, h, t, j0 : j0 + P], rhs=eye[:], start=t == 0, stop=False, is_transpose=True
+                )
+
+        for i in range(2):
             open_sum(0, i)
+        for b in range(PACK):
+            open_difference(b)
         weave(nc.vector.tensor_copy, r_woven[0], rest, 0, SCALAR_TOKENS, HALF)
         weave(nc.vector.tensor_copy, r_woven[0], rest, 1, 0, HALF)
         for h in range(2):
@@ -261,37 +269,17 @@ def tile_list_embg_tgq4_res_kernel(tc, dy, w_words, w_scales, res, wgo, offs, ou
         place(0, 0)
         empty_bank(0, 1)
         read_back(1)
-        pages[3] = placed_tile([P, T], F32, "page3", page_bytes)
-        clear(3, 0)
-        clear(3, 1)
         finish(0, 1)
         place(0, 1)
-        clear(3, 2)
-        clear(3, 3)
-        for i in range(2, ROW_TILES):
-            close_sum(0, i)
-
         blocks = CHUNK // P
-        diff = {}
-        minus = keep.tile([P, PACK, CHUNK], F32, name="minus")
-
-        def open_difference(b):
-            diff[b] = bank((4, 5, 0, 1)[b], f"diff{b}")
-            h, j0 = divmod(b * P, HALF)
-            for t in range(PACK):
-                nc.tensor.matmul(
-                    out=diff[b][:, t * P : (t + 1) * P], lhsT=raw[1][:, h, t, j0 : j0 + P], rhs=eye[:], start=t == 0, stop=False, is_transpose=True
-                )
-
         def negate(t, cols):
             nc.scalar.activation(out=minus[:, t, cols], in_=back[1, t][:, cols], func=COPY, scale=-1.0)
 
-        open_difference(0)
-        open_difference(1)
         for t in range(PACK - 1):
             negate(t, whole)
-        open_difference(2)
-        open_difference(3)
+        for i in range(2, ROW_TILES):
+            open_sum(0, i)
+            close_sum(0, i)
         for cols in halves:
             negate(PACK - 1, cols)
         empty_bank(0, 2)
@@ -322,13 +310,13 @@ def tile_list_embg_tgq4_res_kernel(tc, dy, w_words, w_scales, res, wgo, offs, ou
         turn(0)
         turn(1)
         turn(2)
-        turn_back([0, 1], 2)
+        turn_back([0, 1], 4)
         turn(3)
-        turn_back([2], 3)
-        turn_back([3], 4)
+        turn_back([2], 5)
+        turn_back([3], 0)
         dx_sbuf[0, 3] = held_tile([P, CHUNK], F32, "dx_sbuf03", "turned3")
         nc.scalar.activation(out=dx_sbuf[0, 3][:], in_=dx[0, 3][:], func=IDENTITY, bias=pages[2][:, 0:1])
-        for i in range(ROW_TILES):
+        for i in range(ROW_TILES - 1):
             open_sum(1, i)
 
         r_codes[1] = held_tile([P, CHUNK], U32, "r_codes1", "r_codes1")
@@ -337,6 +325,8 @@ def tile_list_embg_tgq4_res_kernel(tc, dy, w_words, w_scales, res, wgo, offs, ou
             finish(0, i)
             place(0, i)
         for i in range(ROW_TILES):
+            if i == ROW_TILES - 1:
+                open_sum(1, i)
             close_sum(1, i)
             empty_bank(1, i)
             finish(1, i)

@@ -27,8 +27,20 @@ CHUNK = 512
 HALF = CHUNK // 2
 CHUNKS = J // CHUNK
 ROW_TILES = N // P
-SCALAR_TOKENS = 192
+TOKEN_TILES = CHUNK // P
 MX_ALIGN = 64
+PAGE_BYTES = 4 * T
+WOVEN_BYTES = 2 * PACK * CHUNK
+
+SCALAR_FIRST_HALF = 192
+SCALAR_SECOND_HALF = 96
+SCALAR_REST = 192
+VECTOR_CLEARS = 256
+OVERLAP = 8
+
+BACK_BANKS = ((0, 1, 2, 3), (6, 7, 2, 3))
+DX_BANKS = ((2, 3, 6, 7), (3, 0, 7, 3))
+DIFFERENCE_BANKS = (0, 1, 4, 5)
 
 
 def tile_list_embg_tgq4_res_kernel(tc, dy, w_words, w_scales, res, wgo, offs, out):
@@ -37,18 +49,16 @@ def tile_list_embg_tgq4_res_kernel(tc, dy, w_words, w_scales, res, wgo, offs, ou
         keep = ctx.enter_context(tc.tile_pool(name="keep", bufs=1))
         ring = ctx.enter_context(tc.tile_pool(name="ring", bufs=3))
         shared = ctx.enter_context(tc.tile_pool(name="shared", bufs=1))
-        page_bytes = 4 * T
+        psum = ctx.enter_context(tc.psum_pool(name="psum", bufs=1))
+
+        def held_tile(shape, dtype, name, tag):
+            return keep.tile(shape, dtype, name=name, tag=tag, align_bytes=MX_ALIGN)
 
         def placed_tile(shape, dtype, name, offset):
             return shared.tile(shape, dtype, name=name, offset=offset, align_bytes=MX_ALIGN)
 
-        psum = ctx.enter_context(tc.psum_pool(name="psum", bufs=1))
-
         def bank(b, name):
             return psum.tile([P, CHUNK], F32, name=name, tag=f"bank{b}")
-
-        def held_tile(shape, dtype, name, tag):
-            return keep.tile(shape, dtype, name=name, tag=tag, align_bytes=MX_ALIGN)
 
         order = [(c, i) for c in range(CHUNKS) for i in range(ROW_TILES)]
         halves = [slice(0, HALF), slice(HALF, CHUNK)]
@@ -63,11 +73,6 @@ def tile_list_embg_tgq4_res_kernel(tc, dy, w_words, w_scales, res, wgo, offs, ou
 
         dy_rows = dy.rearrange("(p t) j -> p t j", t=PACK)
 
-        def load_dy(c):
-            for h in range(2):
-                j0 = c * CHUNK + h * HALF
-                nc.sync.dma_start(out=raw[c][:, h], in_=dy_rows[:, :, j0 : j0 + HALF])
-
         def load_residual(c, i):
             nc.sync.dma_start(out=residual[c, i][:], in_=res[i * P : (i + 1) * P, c * CHUNK : (c + 1) * CHUNK])
 
@@ -75,8 +80,10 @@ def tile_list_embg_tgq4_res_kernel(tc, dy, w_words, w_scales, res, wgo, offs, ou
             nc.sync.dma_start(out=weights[c][:], in_=wgo[:, c * CHUNK : (c + 1) * CHUNK])
 
         nc.vector.memset(w_scale[:].bitcast(I32), 0)
-        load_dy(0)
-        load_dy(1)
+        for c in range(CHUNKS):
+            for h in range(2):
+                j0 = c * CHUNK + h * HALF
+                nc.sync.dma_start(out=raw[c][:, h], in_=dy_rows[:, :, j0 : j0 + HALF])
         nc.sync.dma_start(out=w_codes[:].bitcast(I32), in_=w_words[0].bitcast(I32))
         for q in range(QUADRANTS):
             nc.sync.dma_start(
@@ -91,49 +98,50 @@ def tile_list_embg_tgq4_res_kernel(tc, dy, w_words, w_scales, res, wgo, offs, ou
         for i in range(ROW_TILES):
             load_residual(1, i)
 
+        eye_bytes = 4 * P
+        across_border = PAGE_BYTES - WOVEN_BYTES // 2
+        behind_pages = 2 * PAGE_BYTES + eye_bytes
+
         pages = {0: keep.tile([P, T], F32, name="page0")}
-
-        def clear(i, q):
-            nc.gpsimd.memset(pages[i][:, q * CHUNK : (q + 1) * CHUNK].bitcast(I32), 0)
-
         seed = held_tile([P, P], BF16, "seed", "page2")
         make_identity(nc, seed[:])
-        ones_at = placed_tile([P, K + 2 * PACK], BF16, "ones_at", page_bytes - K)
+        ones_at = placed_tile([P, K + 2 * PACK], BF16, "ones_at", across_border)
+        every_fourth = ones_at[:, PACK - 1 : K + PACK - 1 : PACK]
         nc.vector.memset(ones_at[:].bitcast(I32), 0)
         nc.vector.memset(pages[0][:].bitcast(I32), 0)
-        nc.vector.tensor_copy(out=ones_at[:, PACK - 1 : K + PACK - 1 : PACK], in_=seed[:])
-        eye_woven = held_tile([P, PACK * K], BF16, "eye_woven", "q_codes0")
+        nc.vector.tensor_copy(out=every_fourth, in_=seed[:])
+        eye_woven = placed_tile([P, PACK * K], BF16, "eye_woven", behind_pages)
         for t in range(PACK):
             copy = nc.vector.tensor_copy if t % 2 else nc.scalar.copy
             copy(out=eye_woven[:, t * K : (t + 1) * K], in_=ones_at[:, PACK - 1 - t : PACK - 1 - t + K])
         pages[2] = held_tile([P, T], F32, "page2", "page2")
         nc.vector.memset(pages[2][:].bitcast(I32), 0)
-        eye = keep.tile([P, P], F32, name="eye")
-        nc.scalar.copy(out=eye[:], in_=ones_at[:, PACK - 1 : K + PACK - 1 : PACK])
+        kept_eye = keep.tile([P, P], BF16, name="kept_eye")
+        nc.scalar.copy(out=kept_eye[:], in_=every_fourth)
         eye_codes = keep.tile([P, K], U32, name="eye_codes", align_bytes=MX_ALIGN)
-        first_scale = held_tile([P, P], U8, "first_scale", "page3")
-        eye_scale = keep.tile([P, K - P], U8, name="eye_scale", align_bytes=MX_ALIGN)
-        for t0, t1, scales in ((0, 1, first_scale[:]), (1, 2, eye_scale[:, 0:P]), (2, 4, eye_scale[:, P : 3 * P])):
-            nc.vector.quantize_mx(
-                out=eye_codes[:, t0 * P : t1 * P].bitcast(E4M3), scales=scales, in_=eye_woven[:, t0 * K : t1 * K]
-            )
+        eye_scale = keep.tile([P, K], U8, name="eye_scale", align_bytes=MX_ALIGN)
+        nc.vector.quantize_mx(out=eye_codes[:].bitcast(E4M3), scales=eye_scale[:], in_=eye_woven[:])
 
         def chunk_tiles(dtype, name, chunks):
             return {c: keep.tile([P, CHUNK], dtype, name=f"{name}{c}", align_bytes=MX_ALIGN) for c in chunks}
 
         woven_shape = [P, CHUNK, PACK]
-        q_woven = [placed_tile(woven_shape, BF16, "q_woven0", page_bytes // 2), placed_tile(woven_shape, BF16, "q_woven1", page_bytes)]
-        r_woven = [held_tile(woven_shape, BF16, "r_woven0", "r_woven0"), held_tile(woven_shape, BF16, "r_woven1", "r_woven1")]
-        q_codes = {0: held_tile([P, CHUNK], U32, "q_codes0", "q_codes0")}
+        q_woven = [
+            placed_tile(woven_shape, BF16, "q_woven0", across_border),
+            placed_tile(woven_shape, BF16, "q_woven1", behind_pages + WOVEN_BYTES // 2),
+        ]
+        r_woven = [held_tile(woven_shape, BF16, f"r_woven{c}", f"r_woven{c}") for c in range(CHUNKS)]
+        q_codes = {0: placed_tile([P, CHUNK], U32, "q_codes0", behind_pages)}
         q_scale = chunk_tiles(U8, "q_scale", range(CHUNKS))
         r_codes = chunk_tiles(U32, "r_codes", range(1))
         r_scale = chunk_tiles(U8, "r_scale", range(CHUNKS))
         rest = keep.tile([P, 2, PACK, HALF], BF16, name="rest")
+        minus = keep.tile([P, PACK, CHUNK], F32, name="minus")
 
         def weave(copy, woven, rows, h, j0, j1):
             copy(
-                out=woven[:, h * HALF + j0 : h * HALF + j1, :].rearrange("p (c i) t -> p c t i", i=PACK),
-                in_=rows[:, h, :, j0:j1].rearrange("p t (c i) -> p c t i", i=PACK),
+                out=woven[:, h * HALF + j0 : h * HALF + j1, :].rearrange("p (g i) t -> p g t i", i=PACK),
+                in_=rows[:, h, :, j0:j1].rearrange("p t (g i) -> p g t i", i=PACK),
             )
 
         def quantize(woven, codes, scale, fmt, cols):
@@ -145,15 +153,17 @@ def tile_list_embg_tgq4_res_kernel(tc, dy, w_words, w_scales, res, wgo, offs, ou
         dx = {}
         dx_sbuf = {}
         scaled = {}
+        difference = {}
+        turned = {}
 
         def read_back(c):
             for t in range(PACK):
-                back[c, t] = bank(t if c == 0 else (6, 7, 4, 5)[t], f"back{c}{t}")
+                back[c, t] = bank(BACK_BANKS[c][t], f"back{c}{t}")
                 cols = slice(t * P, (t + 1) * P)
                 nc.tensor.matmul_mx(
                     out=back[c, t][:],
                     lhsT=eye_codes[:, cols].bitcast(E4M3),
-                    lhsT_scale=first_scale[:] if (c, t) == (0, 0) else eye_scale[:, max(t - 1, 0) * P : max(t, 1) * P],
+                    lhsT_scale=eye_scale[:, cols],
                     rhs=q_codes[c][:].bitcast(E5M2),
                     rhs_scale=q_scale[c][:],
                     start=True,
@@ -185,95 +195,109 @@ def tile_list_embg_tgq4_res_kernel(tc, dy, w_words, w_scales, res, wgo, offs, ou
             )
 
         def open_sum(c, i):
-            dx[c, i] = bank(PACK + i if c == 0 else (5, 0, 7, 5)[i], f"dx{c}{i}")
+            dx[c, i] = bank(DX_BANKS[c][i], f"dx{c}{i}")
             product(c, i, q_codes, q_scale, E5M2, True)
 
         def close_sum(c, i):
             product(c, i, r_codes, r_scale, E4M3, False)
 
-        def empty_bank(c, i, parts=(whole,)):
+        def empty_bank(c, i):
             dx_sbuf[c, i] = keep.tile([P, CHUNK], F32, name=f"dx_sbuf{c}{i}")
-            for cols in parts:
-                nc.scalar.copy(out=dx_sbuf[c, i][:, cols], in_=dx[c, i][:, cols])
+            nc.scalar.copy(out=dx_sbuf[c, i][:], in_=dx[c, i][:])
 
-        product_tags = {order[1]: "r_codes1"}
-        sum_tags = {order[3]: "r_woven1"}
-
-        def finish(c, i, parts=(whole,)):
-            if (c, i) in sum_tags:
-                total = held_tile([P, CHUNK], F32, f"total{c}{i}", sum_tags[c, i])
+        def finish(c, i):
+            if (c, i) == order[3]:
+                total = held_tile([P, CHUNK], F32, "total03", "r_woven1")
             else:
                 total = ring.tile([P, CHUNK], F32, name="total")
-            if (c, i) in product_tags:
-                scaled[c, i] = held_tile([P, CHUNK], F32, f"scaled{c}{i}", product_tags[c, i])
+            if (c, i) == order[1]:
+                scaled[c, i] = held_tile([P, CHUNK], F32, "scaled01", "r_codes1")
             else:
                 scaled[c, i] = ring.tile([P, CHUNK], F32, name="scaled")
-            engine, sums = (nc.vector, dx) if (c, i) == order[0] else (nc.gpsimd, dx_sbuf)
+            engine, sums, parts = (nc.vector, dx, halves) if (c, i) == order[0] else (nc.gpsimd, dx_sbuf, [whole])
             for cols in parts:
                 engine.tensor_tensor(out=total[:, cols], in0=sums[c, i][:, cols], in1=residual[c, i][:, cols], op=ALU.add)
             for cols in parts:
                 engine.tensor_tensor(out=scaled[c, i][:, cols], in0=total[:, cols], in1=weights[c][:, cols], op=ALU.mult)
 
-        def place(c, i, parts=(whole,)):
-            for cols in parts:
-                entries = offsets[:, (c * CHUNK + cols.start) // GROUP : (c * CHUNK + cols.stop) // GROUP]
-                nc.vector.tensor_copy(out=pages[i][:].indirect(entries), in_=scaled[c, i][:, cols])
+        def place(c, i):
+            entries = offsets[:, c * CHUNK // GROUP : (c + 1) * CHUNK // GROUP]
+            nc.vector.tensor_copy(out=pages[i][:].indirect(entries), in_=scaled[c, i][:])
             if c == CHUNKS - 1:
                 nc.sync.dma_start(out=out[i * P : (i + 1) * P, :], in_=pages[i][:])
 
-        weave(nc.scalar.copy, q_woven[0], raw[0], 0, 0, 128)
-        weave(nc.vector.tensor_copy, q_woven[0], raw[0], 0, 128, HALF)
-        quantize(q_woven[0], q_codes[0], q_scale[0], E5M2, halves[0])
-        weave(nc.scalar.copy, q_woven[0], raw[0], 1, 0, 96)
-        weave(nc.vector.tensor_copy, q_woven[0], raw[0], 1, 96, HALF)
-        quantize(q_woven[0], q_codes[0], q_scale[0], E5M2, halves[1])
+        def add_transposed(b, t, rows, start, stop):
+            nc.tensor.matmul(
+                out=difference[b][:, t * P : (t + 1) * P], lhsT=rows, rhs=eye[:], start=start, stop=stop, is_transpose=True
+            )
+
+        def open_difference(b):
+            difference[b] = bank(DIFFERENCE_BANKS[b], f"difference{b}")
+            h, j0 = divmod(b * P, HALF)
+            for t in range(PACK):
+                add_transposed(b, t, raw[1][:, h, t, j0 : j0 + P], t == 0, False)
+
+        def negate(t, cols):
+            nc.scalar.activation(out=minus[:, t, cols], in_=back[1, t][:, cols], func=COPY, scale=-1.0)
+
+        def close_difference(b):
+            for t in range(PACK):
+                add_transposed(b, t, minus[:, t, b * P : (b + 1) * P], False, t == PACK - 1)
+            turned[b] = held_tile([P, 2, P, 2], BF16, f"turned{b}", f"turned{b}")
+            nc.scalar.copy(out=turned[b][:], in_=difference[b][:].rearrange("j (u e p) -> j u p e", u=2, e=2))
+
+        def turn_back(first, count, where):
+            pairs = bank(where, f"pairs{first}")
+            for b in range(count):
+                words = turned[first + b][:].rearrange("j u p e -> j (u p e)").bitcast(F32)
+                for u in range(2):
+                    at = (u * count + b) * P
+                    nc.tensor.transpose(pairs[:, at : at + P], words[:, u * P : (u + 1) * P], eye[:])
+            woven_words = r_woven[1][:, first * P : (first + count) * P, :].rearrange("p j t -> p (j t)").bitcast(F32)
+            nc.scalar.copy(
+                out=woven_words.rearrange("p (j u) -> p j u", u=2),
+                in_=pairs[:, 0 : 2 * count * P].rearrange("p (u j) -> p j u", u=2),
+            )
+
+        for h, share in enumerate((SCALAR_FIRST_HALF, SCALAR_SECOND_HALF)):
+            weave(nc.scalar.copy, q_woven[0], raw[0], h, 0, share)
+            weave(nc.vector.tensor_copy, q_woven[0], raw[0], h, share, HALF)
+            quantize(q_woven[0], q_codes[0], q_scale[0], E5M2, halves[h])
         pages[1] = placed_tile([P, T], F32, "page1", 0)
         nc.vector.memset(pages[1][:].bitcast(I32), 0)
         read_back(0)
-        pages[3] = held_tile([P, T], F32, "page3", "page3")
-        nc.vector.memset(pages[3][:, 0:264].bitcast(I32), 0)
-        nc.gpsimd.memset(pages[3][:, 256:].bitcast(I32), 0)
+        eye = placed_tile([P, P], F32, "eye", PAGE_BYTES)
+        nc.scalar.copy(out=eye[:], in_=kept_eye[:])
+        pages[3] = placed_tile([P, T], F32, "page3", PAGE_BYTES + eye_bytes)
+        nc.vector.memset(pages[3][:, 0 : VECTOR_CLEARS + OVERLAP].bitcast(I32), 0)
+        nc.gpsimd.memset(pages[3][:, VECTOR_CLEARS:].bitcast(I32), 0)
         for h in range(2):
             weave(nc.scalar.copy, q_woven[1], raw[1], h, 0, HALF)
 
         for t in range(PACK - 1):
             subtract(t)
         subtract_half(PACK - 1, 0)
-        weave(nc.scalar.copy, r_woven[0], rest, 0, 0, SCALAR_TOKENS)
+        weave(nc.scalar.copy, r_woven[0], rest, 0, 0, SCALAR_REST)
         subtract_half(PACK - 1, 1)
-        diff = {}
-        minus = keep.tile([P, PACK, CHUNK], F32, name="minus")
-
-        def open_difference(b):
-            diff[b] = bank(b, f"diff{b}")
-            h, j0 = divmod(b * P, HALF)
-            for t in range(PACK):
-                nc.tensor.matmul(
-                    out=diff[b][:, t * P : (t + 1) * P], lhsT=raw[1][:, h, t, j0 : j0 + P], rhs=eye[:], start=t == 0, stop=False, is_transpose=True
-                )
-
+        for b in range(TOKEN_TILES):
+            open_difference(b)
         for i in range(2):
             open_sum(0, i)
-        for b in range(PACK):
-            open_difference(b)
-        weave(nc.vector.tensor_copy, r_woven[0], rest, 0, SCALAR_TOKENS, HALF)
+        weave(nc.vector.tensor_copy, r_woven[0], rest, 0, SCALAR_REST, HALF)
         weave(nc.vector.tensor_copy, r_woven[0], rest, 1, 0, HALF)
         for h in range(2):
             quantize(r_woven[0], r_codes[0], r_scale[0], E4M3, halves[h])
+
         q_codes[1] = held_tile([P, CHUNK], U32, "q_codes1", "r_woven0")
         quantize(q_woven[1], q_codes[1], q_scale[1], E5M2, whole)
-
         close_sum(0, 0)
         close_sum(0, 1)
-        finish(0, 0, halves)
+        finish(0, 0)
         place(0, 0)
         empty_bank(0, 1)
         read_back(1)
         finish(0, 1)
         place(0, 1)
-        blocks = CHUNK // P
-        def negate(t, cols):
-            nc.scalar.activation(out=minus[:, t, cols], in_=back[1, t][:, cols], func=COPY, scale=-1.0)
 
         for t in range(PACK - 1):
             negate(t, whole)
@@ -283,47 +307,23 @@ def tile_list_embg_tgq4_res_kernel(tc, dy, w_words, w_scales, res, wgo, offs, ou
         for cols in halves:
             negate(PACK - 1, cols)
         empty_bank(0, 2)
+        for b in range(TOKEN_TILES - 1):
+            close_difference(b)
+        turn_back(0, 2, BACK_BANKS[1][2])
+        close_difference(TOKEN_TILES - 1)
+        turn_back(2, 1, BACK_BANKS[1][3])
+        turn_back(3, 1, DIFFERENCE_BANKS[0])
 
-        turned = {}
-
-        def turn(b):
-            for t in range(PACK):
-                nc.tensor.matmul(
-                    out=diff[b][:, t * P : (t + 1) * P], lhsT=minus[:, t, b * P : (b + 1) * P], rhs=eye[:], start=False, stop=t == PACK - 1, is_transpose=True
-                )
-            turned[b] = held_tile([P, 2, P, 2], BF16, f"turned{b}", f"turned{b}")
-            nc.scalar.copy(out=turned[b][:], in_=diff[b][:].rearrange("j (u e p) -> j u p e", u=2, e=2))
-
-        def turn_back(bs, where):
-            n = len(bs)
-            pairs = bank(where, f"pairs{bs[0]}")
-            for k, b in enumerate(bs):
-                words = turned[b][:].rearrange("j u p e -> j (u p e)").bitcast(F32)
-                for u in range(2):
-                    at = (u * n + k) * P
-                    nc.tensor.transpose(pairs[:, at : at + P], words[:, u * P : (u + 1) * P], eye[:])
-            nc.scalar.copy(
-                out=r_woven[1][:, bs[0] * P : (bs[-1] + 1) * P, :].rearrange("p j t -> p (j t)").bitcast(F32).rearrange("p (j u) -> p j u", u=2),
-                in_=pairs[:, 0 : 2 * n * P].rearrange("p (u j) -> p j u", u=2),
-            )
-
-        turn(0)
-        turn(1)
-        turn(2)
-        turn_back([0, 1], 4)
-        turn(3)
-        turn_back([2], 5)
-        turn_back([3], 0)
-        dx_sbuf[0, 3] = held_tile([P, CHUNK], F32, "dx_sbuf03", "turned3")
+        dx_sbuf[0, 3] = held_tile([P, CHUNK], F32, "dx_sbuf03", f"turned{TOKEN_TILES - 1}")
         nc.scalar.activation(out=dx_sbuf[0, 3][:], in_=dx[0, 3][:], func=IDENTITY, bias=pages[2][:, 0:1])
         for i in range(ROW_TILES - 1):
             open_sum(1, i)
-
         r_codes[1] = held_tile([P, CHUNK], U32, "r_codes1", "r_codes1")
         quantize(r_woven[1], r_codes[1], r_scale[1], E4M3, whole)
         for i in range(2, ROW_TILES):
             finish(0, i)
             place(0, i)
+
         for i in range(ROW_TILES):
             if i == ROW_TILES - 1:
                 open_sum(1, i)

@@ -35,7 +35,8 @@ WOVEN_BYTES = 2 * PACK * CHUNK
 SCALAR_FIRST_HALF = 192
 SCALAR_SECOND_HALF = 96
 SCALAR_REST = 192
-VECTOR_CLEARS = 256
+VECTOR_CLEARS = 128
+VECTOR_CLEARS_LAST = 1200
 OVERLAP = 8
 
 BACK_BANKS = ((0, 1, 2, 3), (6, 7, 2, 3))
@@ -183,23 +184,23 @@ def tile_list_embg_tgq4_res_kernel(tc, dy, w_words, w_scales, res, wgo, offs, ou
                 out=rest[:, h, t, :], in0=raw[0][:, h, t, :], in1=back[0, t][:, halves[h]], op=ALU.subtract
             )
 
-        def product(c, i, codes, scale, fmt, first):
+        def product(c, i, codes, scale, fmt, cols, start, stop):
             nc.tensor.matmul_mx(
-                out=dx[c, i][:],
+                out=dx[c, i][:, cols],
                 lhsT=w_codes[:, 2 * P * i : 2 * P * (i + 1)].bitcast(E2M1),
                 lhsT_scale=w_scale[:, P * i : P * (i + 1)],
-                rhs=codes[c][:].bitcast(fmt),
-                rhs_scale=scale[c][:],
-                start=first,
-                stop=not first,
+                rhs=codes[c][:, cols].bitcast(fmt),
+                rhs_scale=scale[c][:, cols],
+                start=start,
+                stop=stop,
             )
 
         def open_sum(c, i):
             dx[c, i] = bank(DX_BANKS[c][i], f"dx{c}{i}")
-            product(c, i, q_codes, q_scale, E5M2, True)
+            product(c, i, q_codes, q_scale, E5M2, whole, True, False)
 
         def close_sum(c, i):
-            product(c, i, r_codes, r_scale, E4M3, False)
+            product(c, i, r_codes, r_scale, E4M3, whole, False, True)
 
         def empty_bank(c, i):
             dx_sbuf[c, i] = keep.tile([P, CHUNK], F32, name=f"dx_sbuf{c}{i}")
@@ -263,14 +264,14 @@ def tile_list_embg_tgq4_res_kernel(tc, dy, w_words, w_scales, res, wgo, offs, ou
             weave(nc.scalar.copy, q_woven[0], raw[0], h, 0, share)
             weave(nc.vector.tensor_copy, q_woven[0], raw[0], h, share, HALF)
             quantize(q_woven[0], q_codes[0], q_scale[0], E5M2, halves[h])
-        pages[1] = placed_tile([P, T], F32, "page1", 0)
-        nc.vector.memset(pages[1][:].bitcast(I32), 0)
+        pages[3] = placed_tile([P, T], F32, "page3", 0)
+        nc.vector.memset(pages[3][:, 0:VECTOR_CLEARS_LAST].bitcast(I32), 0)
         read_back(0)
         eye = placed_tile([P, P], F32, "eye", PAGE_BYTES)
         nc.scalar.copy(out=eye[:], in_=kept_eye[:])
-        pages[3] = placed_tile([P, T], F32, "page3", PAGE_BYTES + eye_bytes)
-        nc.vector.memset(pages[3][:, 0 : VECTOR_CLEARS + OVERLAP].bitcast(I32), 0)
-        nc.gpsimd.memset(pages[3][:, VECTOR_CLEARS:].bitcast(I32), 0)
+        pages[1] = placed_tile([P, T], F32, "page1", PAGE_BYTES + eye_bytes)
+        nc.vector.memset(pages[1][:, 0 : VECTOR_CLEARS + OVERLAP].bitcast(I32), 0)
+        nc.gpsimd.memset(pages[1][:, VECTOR_CLEARS:].bitcast(I32), 0)
         for h in range(2):
             weave(nc.scalar.copy, q_woven[1], raw[1], h, 0, HALF)
 
@@ -290,7 +291,8 @@ def tile_list_embg_tgq4_res_kernel(tc, dy, w_words, w_scales, res, wgo, offs, ou
 
         q_codes[1] = held_tile([P, CHUNK], U32, "q_codes1", "r_woven0")
         quantize(q_woven[1], q_codes[1], q_scale[1], E5M2, whole)
-        close_sum(0, 0)
+        for b in range(TOKEN_TILES):
+            product(0, 0, r_codes, r_scale, E4M3, slice(b * P, (b + 1) * P), False, b == TOKEN_TILES - 1)
         close_sum(0, 1)
         finish(0, 0)
         place(0, 0)
@@ -306,7 +308,9 @@ def tile_list_embg_tgq4_res_kernel(tc, dy, w_words, w_scales, res, wgo, offs, ou
             close_sum(0, i)
         for cols in halves:
             negate(PACK - 1, cols)
-        empty_bank(0, 2)
+        dx_sbuf[0, 2] = keep.tile([P, CHUNK], F32, name="dx_sbuf02")
+        last_cleared = pages[3][:, VECTOR_CLEARS_LAST - 1 : VECTOR_CLEARS_LAST]
+        nc.scalar.activation(out=dx_sbuf[0, 2][:], in_=dx[0, 2][:], func=IDENTITY, bias=last_cleared)
         for b in range(TOKEN_TILES - 1):
             close_difference(b)
         turn_back(0, 2, BACK_BANKS[1][2])
@@ -320,9 +324,11 @@ def tile_list_embg_tgq4_res_kernel(tc, dy, w_words, w_scales, res, wgo, offs, ou
             open_sum(1, i)
         r_codes[1] = held_tile([P, CHUNK], U32, "r_codes1", "r_codes1")
         quantize(r_woven[1], r_codes[1], r_scale[1], E4M3, whole)
-        for i in range(2, ROW_TILES):
-            finish(0, i)
-            place(0, i)
+        finish(0, 2)
+        nc.gpsimd.memset(pages[3][:, VECTOR_CLEARS_LAST - OVERLAP :].bitcast(I32), 0)
+        place(0, 2)
+        finish(0, 3)
+        place(0, 3)
 
         for i in range(ROW_TILES):
             if i == ROW_TILES - 1:

@@ -34,9 +34,9 @@ WOVEN_BYTES = 2 * PACK * CHUNK
 
 SCALAR_FIRST_HALF = 192
 SCALAR_SECOND_HALF = 96
-SCALAR_REST = 192
-VECTOR_CLEARS = 128
-VECTOR_CLEARS_LAST = 1200
+SCALAR_REST = 128
+VECTOR_CLEARS = 448
+VECTOR_CLEARS_LAST = 1088
 OVERLAP = 8
 
 BACK_BANKS = ((0, 1, 2, 3), (6, 7, 2, 3))
@@ -80,7 +80,7 @@ def tile_list_embg_tgq4_res_kernel(tc, dy, w_words, w_scales, res, wgo, offs, ou
         def load_weights(c):
             nc.sync.dma_start(out=weights[c][:], in_=wgo[:, c * CHUNK : (c + 1) * CHUNK])
 
-        nc.vector.memset(w_scale[:].bitcast(I32), 0)
+        nc.gpsimd.memset(w_scale[:].bitcast(I32), 0)
         for c in range(CHUNKS):
             for h in range(2):
                 j0 = c * CHUNK + h * HALF
@@ -113,7 +113,7 @@ def tile_list_embg_tgq4_res_kernel(tc, dy, w_words, w_scales, res, wgo, offs, ou
         nc.vector.tensor_copy(out=every_fourth, in_=seed[:])
         eye_woven = placed_tile([P, PACK * K], BF16, "eye_woven", behind_pages)
         for t in range(PACK):
-            copy = nc.vector.tensor_copy if t % 2 else nc.scalar.copy
+            copy = nc.vector.tensor_copy if t else nc.scalar.copy
             copy(out=eye_woven[:, t * K : (t + 1) * K], in_=ones_at[:, PACK - 1 - t : PACK - 1 - t + K])
         pages[2] = held_tile([P, T], F32, "page2", "page2")
         nc.vector.memset(pages[2][:].bitcast(I32), 0)

@@ -34,12 +34,13 @@ WOVEN_BYTES = 2 * PACK * CHUNK
 
 SCALAR_FIRST_HALF = 192
 SCALAR_SECOND_HALF = 96
-SCALAR_REST = 128
-VECTOR_CLEARS = 448
-VECTOR_CLEARS_LAST = 1088
+SCALAR_REST = 96
+VECTOR_CLEARS = 256
+VECTOR_CLEARS_LAST = 1152
 OVERLAP = 8
 
-BACK_BANKS = ((0, 1, 2, 3), (6, 7, 2, 3))
+BACK_BANKS = ((3, 0, 1, 2), (6, 7, 2, 3))
+EARLY_BANK = 4
 DX_BANKS = ((2, 3, 6, 7), (3, 0, 7, 3))
 DIFFERENCE_BANKS = (0, 1, 4, 5)
 
@@ -100,8 +101,8 @@ def tile_list_embg_tgq4_res_kernel(tc, dy, w_words, w_scales, res, wgo, offs, ou
             load_residual(1, i)
 
         eye_bytes = 4 * P
-        across_border = PAGE_BYTES - WOVEN_BYTES // 2
-        behind_pages = 2 * PAGE_BYTES + eye_bytes
+        across_border = PAGE_BYTES - eye_bytes
+        behind_pages = 2 * PAGE_BYTES + eye_bytes + WOVEN_BYTES
 
         pages = {0: keep.tile([P, T], F32, name="page0")}
         seed = held_tile([P, P], BF16, "seed", "page2")
@@ -113,30 +114,32 @@ def tile_list_embg_tgq4_res_kernel(tc, dy, w_words, w_scales, res, wgo, offs, ou
         nc.vector.tensor_copy(out=every_fourth, in_=seed[:])
         eye_woven = placed_tile([P, PACK * K], BF16, "eye_woven", behind_pages)
         for t in range(PACK):
-            copy = nc.vector.tensor_copy if t else nc.scalar.copy
+            copy = nc.vector.tensor_copy if t == PACK - 1 else nc.scalar.copy
             copy(out=eye_woven[:, t * K : (t + 1) * K], in_=ones_at[:, PACK - 1 - t : PACK - 1 - t + K])
         pages[2] = held_tile([P, T], F32, "page2", "page2")
         nc.vector.memset(pages[2][:].bitcast(I32), 0)
         kept_eye = keep.tile([P, P], BF16, name="kept_eye")
         nc.scalar.copy(out=kept_eye[:], in_=every_fourth)
-        eye_codes = keep.tile([P, K], U32, name="eye_codes", align_bytes=MX_ALIGN)
-        eye_scale = keep.tile([P, K], U8, name="eye_scale", align_bytes=MX_ALIGN)
-        nc.vector.quantize_mx(out=eye_codes[:].bitcast(E4M3), scales=eye_scale[:], in_=eye_woven[:])
+        first_codes = keep.tile([P, K + CHUNK], U32, name="first_codes", align_bytes=MX_ALIGN)
+        first_scale = keep.tile([P, K + CHUNK], U8, name="first_scale", align_bytes=MX_ALIGN)
+        eye_codes = first_codes[:, 0:K]
+        eye_scale = first_scale[:, 0:K]
+        nc.vector.quantize_mx(out=eye_codes.bitcast(E4M3), scales=eye_scale, in_=eye_woven[:])
 
         def chunk_tiles(dtype, name, chunks):
             return {c: keep.tile([P, CHUNK], dtype, name=f"{name}{c}", align_bytes=MX_ALIGN) for c in chunks}
 
         woven_shape = [P, CHUNK, PACK]
         q_woven = [
-            placed_tile(woven_shape, BF16, "q_woven0", across_border),
+            placed_tile([P, CHUNK + HALF, PACK], BF16, "q_woven0", across_border),
             placed_tile(woven_shape, BF16, "q_woven1", behind_pages + WOVEN_BYTES // 2),
         ]
         r_woven = [held_tile(woven_shape, BF16, f"r_woven{c}", f"r_woven{c}") for c in range(CHUNKS)]
-        q_codes = {0: placed_tile([P, CHUNK], U32, "q_codes0", behind_pages)}
-        q_scale = chunk_tiles(U8, "q_scale", range(CHUNKS))
+        q_codes = {0: first_codes[:, K:]}
+        q_scale = chunk_tiles(U8, "q_scale", range(1, CHUNKS))
+        q_scale[0] = first_scale[:, K:]
         r_codes = chunk_tiles(U32, "r_codes", range(1))
         r_scale = chunk_tiles(U8, "r_scale", range(CHUNKS))
-        rest = keep.tile([P, 2, PACK, HALF], BF16, name="rest")
         minus = keep.tile([P, PACK, CHUNK], F32, name="minus")
 
         def weave(copy, woven, rows, h, j0, j1):
@@ -157,16 +160,16 @@ def tile_list_embg_tgq4_res_kernel(tc, dy, w_words, w_scales, res, wgo, offs, ou
         difference = {}
         turned = {}
 
-        def read_back(c):
-            for t in range(PACK):
+        def read_back(c, rows):
+            for t in rows:
                 back[c, t] = bank(BACK_BANKS[c][t], f"back{c}{t}")
                 cols = slice(t * P, (t + 1) * P)
                 nc.tensor.matmul_mx(
                     out=back[c, t][:],
                     lhsT=eye_codes[:, cols].bitcast(E4M3),
                     lhsT_scale=eye_scale[:, cols],
-                    rhs=q_codes[c][:].bitcast(E5M2),
-                    rhs_scale=q_scale[c][:],
+                    rhs=q_codes[c][:, whole].bitcast(E5M2),
+                    rhs_scale=q_scale[c][:, whole],
                     start=True,
                     stop=True,
                 )
@@ -264,28 +267,41 @@ def tile_list_embg_tgq4_res_kernel(tc, dy, w_words, w_scales, res, wgo, offs, ou
             weave(nc.scalar.copy, q_woven[0], raw[0], h, 0, share)
             weave(nc.vector.tensor_copy, q_woven[0], raw[0], h, share, HALF)
             quantize(q_woven[0], q_codes[0], q_scale[0], E5M2, halves[h])
+            if h == 0:
+                early = bank(EARLY_BANK, "early")
+                window = slice(K - HALF, K + HALF)
+                nc.tensor.matmul_mx(
+                    out=early[:],
+                    lhsT=eye_codes[:, 0:P].bitcast(E4M3),
+                    lhsT_scale=eye_scale[:, 0:P],
+                    rhs=first_codes[:, window].bitcast(E5M2),
+                    rhs_scale=first_scale[:, window],
+                    start=True,
+                    stop=True,
+                )
         pages[3] = placed_tile([P, T], F32, "page3", 0)
         nc.vector.memset(pages[3][:, 0:VECTOR_CLEARS_LAST].bitcast(I32), 0)
-        read_back(0)
+        read_back(0, (1, 2, 3, 0))
         eye = placed_tile([P, P], F32, "eye", PAGE_BYTES)
-        nc.scalar.copy(out=eye[:], in_=kept_eye[:])
-        pages[1] = placed_tile([P, T], F32, "page1", PAGE_BYTES + eye_bytes)
+        nc.vector.tensor_copy(out=eye[:], in_=kept_eye[:])
+        pages[1] = placed_tile([P, T], F32, "page1", PAGE_BYTES + eye_bytes + WOVEN_BYTES)
         nc.vector.memset(pages[1][:, 0 : VECTOR_CLEARS + OVERLAP].bitcast(I32), 0)
         nc.gpsimd.memset(pages[1][:, VECTOR_CLEARS:].bitcast(I32), 0)
         for h in range(2):
             weave(nc.scalar.copy, q_woven[1], raw[1], h, 0, HALF)
 
-        for t in range(PACK - 1):
+        rest = placed_tile([P, 2, PACK, HALF], BF16, "rest", PAGE_BYTES + eye_bytes)
+        nc.vector.tensor_tensor(out=rest[:, 0, 0, :], in0=raw[0][:, 0, 0, :], in1=early[:, halves[1]], op=ALU.subtract)
+        for t in range(1, PACK):
             subtract(t)
-        subtract_half(PACK - 1, 0)
-        weave(nc.scalar.copy, r_woven[0], rest, 0, 0, SCALAR_REST)
-        subtract_half(PACK - 1, 1)
+        subtract_half(0, 1)
+        weave(nc.scalar.copy, r_woven[0], rest, 1, HALF - SCALAR_REST, HALF)
         for b in range(TOKEN_TILES):
             open_difference(b)
         for i in range(2):
             open_sum(0, i)
-        weave(nc.vector.tensor_copy, r_woven[0], rest, 0, SCALAR_REST, HALF)
-        weave(nc.vector.tensor_copy, r_woven[0], rest, 1, 0, HALF)
+        weave(nc.vector.tensor_copy, r_woven[0], rest, 0, 0, HALF)
+        weave(nc.vector.tensor_copy, r_woven[0], rest, 1, 0, HALF - SCALAR_REST)
         for h in range(2):
             quantize(r_woven[0], r_codes[0], r_scale[0], E4M3, halves[h])
 
@@ -297,7 +313,7 @@ def tile_list_embg_tgq4_res_kernel(tc, dy, w_words, w_scales, res, wgo, offs, ou
         finish(0, 0)
         place(0, 0)
         empty_bank(0, 1)
-        read_back(1)
+        read_back(1, range(PACK))
         finish(0, 1)
         place(0, 1)
 

@@ -17,218 +17,251 @@ E5M2 = mybir.dt.float8_e5m2_x4
 E2M1 = mybir.dt.float4_e2m1fn_x4
 ALU = mybir.AluOpType
 COPY = mybir.ActivationFunctionType.Copy
-IDENTITY = mybir.ActivationFunctionType.Identity
 
 P = 128
 PACK = 4
 GROUP = 16
 QUADRANTS = 4
-CHUNK = 512
-HALF = CHUNK // 2
-CHUNKS = J // CHUNK
+BANK = 512
+QUARTER = 256
+QUARTERS = J // QUARTER
 ROW_TILES = N // P
-TOKEN_TILES = CHUNK // P
 MX_ALIGN = 64
 PAGE_BYTES = 4 * T
-WOVEN_BYTES = 2 * PACK * CHUNK
+WOVEN_BYTES = 2 * PACK * QUARTER
 
-SCALAR_FIRST_HALF = 192
-SCALAR_SECOND_HALF = 96
-SCALAR_REST = 96
-VECTOR_CLEARS = 256
-VECTOR_CLEARS_LAST = 1152
-OVERLAP = 8
-
-BACK_BANKS = ((3, 0, 1, 2), (6, 7, 2, 3))
-EARLY_BANK = 4
-DX_BANKS = ((2, 3, 6, 7), (3, 0, 7, 3))
-DIFFERENCE_BANKS = (0, 1, 4, 5)
+UNITS = (
+    ((0, 0, 256), (1, 0, 256)),
+    ((2, 0, 256), (3, 0, 256)),
+    ((0, 256, 256), (1, 256, 256)),
+    ((2, 256, 256), (3, 256, 256)),
+    ((0, 512, 256), (1, 512, 256)),
+    ((2, 512, 256), (0, 768, 256)),
+    ((1, 768, 256), (2, 768, 256)),
+    ((3, 512, 256), (3, 768, 256)),
+)
+BACK_BANKS = (0, 1, 2, 3, 0, 1, 2, 6)
+DIFFERENCE_BANKS = {4: 3, 5: 4, 6: 3, 7: 4}
+DX_BANKS = (4, 5, 0, 1, 2, 3, 4, 2)
+PAIRS_BANKS = {4: 7, 6: 2}
 
 
 def tile_list_embg_tgq4_res_kernel(tc, dy, w_words, w_scales, res, wgo, offs, out):
     nc = tc.nc
     with ExitStack() as ctx:
         keep = ctx.enter_context(tc.tile_pool(name="keep", bufs=1))
-        ring = ctx.enter_context(tc.tile_pool(name="ring", bufs=3))
         shared = ctx.enter_context(tc.tile_pool(name="shared", bufs=1))
         psum = ctx.enter_context(tc.psum_pool(name="psum", bufs=1))
 
         def held_tile(shape, dtype, name, tag):
             return keep.tile(shape, dtype, name=name, tag=tag, align_bytes=MX_ALIGN)
 
+        def own_tile(shape, dtype, name):
+            return keep.tile(shape, dtype, name=name, align_bytes=MX_ALIGN)
+
         def placed_tile(shape, dtype, name, offset):
             return shared.tile(shape, dtype, name=name, offset=offset, align_bytes=MX_ALIGN)
 
         def bank(b, name):
-            return psum.tile([P, CHUNK], F32, name=name, tag=f"bank{b}")
-
-        order = [(c, i) for c in range(CHUNKS) for i in range(ROW_TILES)]
-        halves = [slice(0, HALF), slice(HALF, CHUNK)]
-        whole = slice(0, CHUNK)
+            return psum.tile([P, BANK], F32, name=name, tag=f"bank{b}")
 
         offsets = keep.tile([P, J // GROUP], U16, name="offsets")
-        w_codes = keep.tile([P, 2 * N], U8, name="w_codes", align_bytes=MX_ALIGN)
-        w_scale = keep.tile([P, N], U8, name="w_scale", align_bytes=MX_ALIGN)
-        raw = [keep.tile([P, 2, PACK, HALF], F32, name=f"raw{c}") for c in range(CHUNKS)]
-        weights = [keep.tile([P, CHUNK], F32, name=f"weights{c}") for c in range(CHUNKS)]
-        residual = {(c, i): keep.tile([P, CHUNK], F32, name=f"residual{c}{i}") for c, i in order}
+        w_codes = own_tile([P, 2 * N], U8, "w_codes")
+        w_scale = own_tile([P, N], U8, "w_scale")
+        raw = [keep.tile([P, PACK, QUARTER], F32, name=f"raw{h}") for h in range(QUARTERS)]
+        weights = [keep.tile([P, BANK], F32, name=f"weights{c}") for c in range(2)]
+        residual = [keep.tile([P, BANK], F32, name=f"residual{u}") for u in range(len(UNITS))]
 
         dy_rows = dy.rearrange("(p t) j -> p t j", t=PACK)
 
-        def load_residual(c, i):
-            nc.sync.dma_start(out=residual[c, i][:], in_=res[i * P : (i + 1) * P, c * CHUNK : (c + 1) * CHUNK])
+        def load_dy(h):
+            nc.sync.dma_start(out=raw[h][:], in_=dy_rows[:, :, h * QUARTER : (h + 1) * QUARTER])
+
+        def load_residual(u):
+            pieces = UNITS[u]
+            first, j0, width = pieces[0]
+            if all(piece[1] == j0 for piece in pieces):
+                rows = res[first * P : (first + len(pieces)) * P, j0 : j0 + width]
+                nc.sync.dma_start(
+                    out=residual[u][:].rearrange("p (i j) -> p i j", j=width), in_=rows.rearrange("(i p) j -> p i j", p=P)
+                )
+            elif all(piece[0] == first for piece in pieces):
+                nc.sync.dma_start(out=residual[u][:], in_=res[first * P : (first + 1) * P, j0 : j0 + BANK])
+            else:
+                for n, (i, j, width) in enumerate(pieces):
+                    nc.sync.dma_start(
+                        out=residual[u][:, n * width : (n + 1) * width], in_=res[i * P : (i + 1) * P, j : j + width]
+                    )
 
         def load_weights(c):
-            nc.sync.dma_start(out=weights[c][:], in_=wgo[:, c * CHUNK : (c + 1) * CHUNK])
+            nc.sync.dma_start(out=weights[c][:], in_=wgo[:, c * BANK : (c + 1) * BANK])
 
         nc.gpsimd.memset(w_scale[:].bitcast(I32), 0)
-        for c in range(CHUNKS):
-            for h in range(2):
-                j0 = c * CHUNK + h * HALF
-                nc.sync.dma_start(out=raw[c][:, h], in_=dy_rows[:, :, j0 : j0 + HALF])
+        load_dy(0)
+        load_dy(1)
+        load_dy(2)
         nc.sync.dma_start(out=w_codes[:].bitcast(I32), in_=w_words[0].bitcast(I32))
         for q in range(QUADRANTS):
             nc.sync.dma_start(
                 out=w_scale[32 * q : 32 * q + 4, :].bitcast(I32), in_=w_scales[0, 4 * q : 4 * q + 4, :].bitcast(I32)
             )
-        load_residual(0, 0)
+        load_dy(3)
+        load_residual(0)
         load_weights(0)
         nc.sync.dma_start(offsets[:], offs)
-        for i in range(1, ROW_TILES):
-            load_residual(0, i)
+        for u in range(1, 4):
+            load_residual(u)
         load_weights(1)
-        for i in range(ROW_TILES):
-            load_residual(1, i)
-
-        eye_bytes = 4 * P
-        across_border = PAGE_BYTES - eye_bytes
-        behind_pages = 2 * PAGE_BYTES + eye_bytes + WOVEN_BYTES
+        for u in range(4, len(UNITS)):
+            load_residual(u)
 
         pages = {0: keep.tile([P, T], F32, name="page0")}
-        seed = held_tile([P, P], BF16, "seed", "page2")
+        seed = held_tile([P, P], BF16, "seed", "page1")
         make_identity(nc, seed[:])
-        ones_at = placed_tile([P, K + 2 * PACK], BF16, "ones_at", across_border)
+        ones_at = placed_tile([P, K + 2 * PACK], BF16, "ones_at", 0)
         every_fourth = ones_at[:, PACK - 1 : K + PACK - 1 : PACK]
         nc.vector.memset(ones_at[:].bitcast(I32), 0)
         nc.vector.memset(pages[0][:].bitcast(I32), 0)
         nc.vector.tensor_copy(out=every_fourth, in_=seed[:])
-        eye_woven = placed_tile([P, PACK * K], BF16, "eye_woven", behind_pages)
+        eye_woven = placed_tile([P, PACK * K], BF16, "eye_woven", 2 * PAGE_BYTES - MX_ALIGN)
         for t in range(PACK):
             copy = nc.vector.tensor_copy if t == PACK - 1 else nc.scalar.copy
             copy(out=eye_woven[:, t * K : (t + 1) * K], in_=ones_at[:, PACK - 1 - t : PACK - 1 - t + K])
-        pages[2] = held_tile([P, T], F32, "page2", "page2")
-        nc.vector.memset(pages[2][:].bitcast(I32), 0)
-        kept_eye = keep.tile([P, P], BF16, name="kept_eye")
-        nc.scalar.copy(out=kept_eye[:], in_=every_fourth)
-        first_codes = keep.tile([P, K + CHUNK], U32, name="first_codes", align_bytes=MX_ALIGN)
-        first_scale = keep.tile([P, K + CHUNK], U8, name="first_scale", align_bytes=MX_ALIGN)
-        eye_codes = first_codes[:, 0:K]
-        eye_scale = first_scale[:, 0:K]
-        nc.vector.quantize_mx(out=eye_codes.bitcast(E4M3), scales=eye_scale, in_=eye_woven[:])
+        pages[1] = held_tile([P, T], F32, "page1", "page1")
+        nc.vector.memset(pages[1][:].bitcast(I32), 0)
+        eye = keep.tile([P, P], F32, name="eye")
+        nc.scalar.copy(out=eye[:], in_=every_fourth)
+        eye_codes = own_tile([P, K], U32, "eye_codes")
+        eye_scale = own_tile([P, K], U8, "eye_scale")
+        nc.vector.quantize_mx(out=eye_codes[:].bitcast(E4M3), scales=eye_scale[:], in_=eye_woven[:])
 
-        def chunk_tiles(dtype, name, chunks):
-            return {c: keep.tile([P, CHUNK], dtype, name=f"{name}{c}", align_bytes=MX_ALIGN) for c in chunks}
-
-        woven_shape = [P, CHUNK, PACK]
+        quarter_shape = [P, QUARTER, PACK]
         q_woven = [
-            placed_tile([P, CHUNK + HALF, PACK], BF16, "q_woven0", across_border),
-            placed_tile(woven_shape, BF16, "q_woven1", behind_pages + WOVEN_BYTES // 2),
+            placed_tile(quarter_shape, BF16, "q_woven0", 0),
+            placed_tile(quarter_shape, BF16, "q_woven1", 2 * PAGE_BYTES - WOVEN_BYTES),
+            placed_tile(quarter_shape, BF16, "q_woven2", 2 * PAGE_BYTES),
+            placed_tile(quarter_shape, BF16, "q_woven3", 2 * PAGE_BYTES + WOVEN_BYTES),
         ]
-        r_woven = [held_tile(woven_shape, BF16, f"r_woven{c}", f"r_woven{c}") for c in range(CHUNKS)]
-        q_codes = {0: first_codes[:, K:]}
-        q_scale = chunk_tiles(U8, "q_scale", range(1, CHUNKS))
-        q_scale[0] = first_scale[:, K:]
-        r_codes = chunk_tiles(U32, "r_codes", range(1))
-        r_scale = chunk_tiles(U8, "r_scale", range(CHUNKS))
-        minus = keep.tile([P, PACK, CHUNK], F32, name="minus")
 
-        def weave(copy, woven, rows, h, j0, j1):
-            copy(
-                out=woven[:, h * HALF + j0 : h * HALF + j1, :].rearrange("p (g i) t -> p g t i", i=PACK),
-                in_=rows[:, h, :, j0:j1].rearrange("p t (g i) -> p g t i", i=PACK),
-            )
-
-        def quantize(woven, codes, scale, fmt, cols):
-            nc.vector.quantize_mx(
-                out=codes[:, cols].bitcast(fmt), scales=scale[:, cols], in_=woven[:, cols, :].rearrange("p j t -> p (j t)")
-            )
-
+        q_operand = {}
+        r_operand = {}
         back = {}
         dx = {}
-        dx_sbuf = {}
         scaled = {}
+        minus = {}
         difference = {}
         turned = {}
+        r_woven = {}
 
-        def read_back(c, rows):
-            for t in rows:
-                back[c, t] = bank(BACK_BANKS[c][t], f"back{c}{t}")
+        def weave(copy, h, j0, j1):
+            copy(
+                out=q_woven[h][:, j0:j1, :].rearrange("p (g i) t -> p g t i", i=PACK),
+                in_=raw[h][:, :, j0:j1].rearrange("p t (g i) -> p g t i", i=PACK),
+            )
+
+        def quantize(operand, woven, j0, width, fmt, codes):
+            scale = own_tile([P, width], U8, f"scale_{len(q_operand)}_{len(r_operand)}")
+            nc.vector.quantize_mx(
+                out=codes[:, 0:width].bitcast(fmt), scales=scale[:], in_=woven[:].rearrange("p j t -> p (j t)")
+            )
+            for j in range(0, width, P):
+                operand[j0 + j] = (codes[:, j:width], scale[:, j:width])
+
+        def first_tier(h):
+            quantize(q_operand, q_woven[h], h * QUARTER, QUARTER, E5M2, own_tile([P, QUARTER], U32, f"q_codes{h}"))
+
+        def second_tier(j0, width, codes):
+            quantize(r_operand, r_woven[j0], j0, width, E4M3, codes)
+
+        def read_back(b):
+            back[b] = bank(BACK_BANKS[b], f"back{b}")
+            codes, scale = q_operand[b * P]
+            for t in range(PACK):
                 cols = slice(t * P, (t + 1) * P)
                 nc.tensor.matmul_mx(
-                    out=back[c, t][:],
+                    out=back[b][:, cols],
                     lhsT=eye_codes[:, cols].bitcast(E4M3),
                     lhsT_scale=eye_scale[:, cols],
-                    rhs=q_codes[c][:, whole].bitcast(E5M2),
-                    rhs_scale=q_scale[c][:, whole],
+                    rhs=codes[:, 0:P].bitcast(E5M2),
+                    rhs_scale=scale[:, 0:P],
                     start=True,
                     stop=True,
                 )
 
-        def subtract(t):
+        def raw_tile(b):
+            h, j0 = divmod(b * P, QUARTER)
+            return raw[h][:, :, j0 : j0 + P]
+
+        def subtract(b, woven):
             nc.vector.tensor_tensor(
-                out=rest[:, :, t, :],
-                in0=raw[0][:, :, t, :],
-                in1=back[0, t][:].rearrange("p (h j) -> p h j", h=2),
+                out=woven.rearrange("p (g i) t -> p g t i", i=2),
+                in0=raw_tile(b).rearrange("p t (g i) -> p g t i", i=2),
+                in1=back[b][:].rearrange("p (t g i) -> p g t i", t=PACK, i=2),
                 op=ALU.subtract,
             )
 
-        def subtract_half(t, h):
-            nc.vector.tensor_tensor(
-                out=rest[:, h, t, :], in0=raw[0][:, h, t, :], in1=back[0, t][:, halves[h]], op=ALU.subtract
+        def products(u, operand, fmt, opening):
+            pieces = list(enumerate(UNITS[u]))
+            if not opening:
+                pieces = sorted(pieces, key=lambda piece: -piece[1][1])
+            for step, (n, (i, j0, width)) in enumerate(pieces):
+                codes, scale = operand[j0]
+                nc.tensor.matmul_mx(
+                    out=dx[u][:, n * width : (n + 1) * width],
+                    lhsT=w_codes[:, 2 * P * i : 2 * P * (i + 1)].bitcast(E2M1),
+                    lhsT_scale=w_scale[:, P * i : P * (i + 1)],
+                    rhs=codes[:, 0:width].bitcast(fmt),
+                    rhs_scale=scale[:, 0:width],
+                    start=opening and step == 0,
+                    stop=not opening and step == len(pieces) - 1,
+                )
+
+        def open_sum(u):
+            dx[u] = bank(DX_BANKS[u], f"dx{u}")
+            products(u, q_operand, E5M2, True)
+
+        def close_sum(u):
+            products(u, r_operand, E4M3, False)
+
+        def unit_weights(u):
+            pieces = UNITS[u]
+            c, j0 = divmod(pieces[0][1], BANK)
+            width = pieces[0][2]
+            if pieces[1][1] != pieces[0][1]:
+                return weights[c][:].rearrange("p (i j) -> p i j", j=width)
+            return weights[c][:, j0 : j0 + width].unsqueeze(1).to_broadcast([P, len(pieces), width])
+
+        def empty_bank(u):
+            sums = keep.tile([P, BANK], F32, name=f"dx_sbuf{u}")
+            nc.scalar.copy(out=sums[:], in_=dx[u][:])
+            return sums
+
+        def finish(u, sums, total):
+            scaled[u] = held_tile([P, BANK], F32, f"scaled{u}", f"scaled{u}")
+            width = UNITS[u][0][2]
+            nc.gpsimd.tensor_tensor(out=total[:], in0=sums[:], in1=residual[u][:], op=ALU.add)
+            nc.gpsimd.tensor_tensor(
+                out=scaled[u][:].rearrange("p (i j) -> p i j", j=width),
+                in0=total[:].rearrange("p (i j) -> p i j", j=width),
+                in1=unit_weights(u),
+                op=ALU.mult,
             )
 
-        def product(c, i, codes, scale, fmt, cols, start, stop):
-            nc.tensor.matmul_mx(
-                out=dx[c, i][:, cols],
-                lhsT=w_codes[:, 2 * P * i : 2 * P * (i + 1)].bitcast(E2M1),
-                lhsT_scale=w_scale[:, P * i : P * (i + 1)],
-                rhs=codes[c][:, cols].bitcast(fmt),
-                rhs_scale=scale[c][:, cols],
-                start=start,
-                stop=stop,
-            )
-
-        def open_sum(c, i):
-            dx[c, i] = bank(DX_BANKS[c][i], f"dx{c}{i}")
-            product(c, i, q_codes, q_scale, E5M2, whole, True, False)
-
-        def close_sum(c, i):
-            product(c, i, r_codes, r_scale, E4M3, whole, False, True)
-
-        def empty_bank(c, i):
-            dx_sbuf[c, i] = keep.tile([P, CHUNK], F32, name=f"dx_sbuf{c}{i}")
-            nc.scalar.copy(out=dx_sbuf[c, i][:], in_=dx[c, i][:])
-
-        def finish(c, i):
-            if (c, i) == order[3]:
-                total = held_tile([P, CHUNK], F32, "total03", "r_woven1")
-            else:
-                total = ring.tile([P, CHUNK], F32, name="total")
-            if (c, i) == order[1]:
-                scaled[c, i] = held_tile([P, CHUNK], F32, "scaled01", "r_codes1")
-            else:
-                scaled[c, i] = ring.tile([P, CHUNK], F32, name="scaled")
-            engine, sums, parts = (nc.vector, dx, halves) if (c, i) == order[0] else (nc.gpsimd, dx_sbuf, [whole])
-            for cols in parts:
-                engine.tensor_tensor(out=total[:, cols], in0=sums[c, i][:, cols], in1=residual[c, i][:, cols], op=ALU.add)
-            for cols in parts:
-                engine.tensor_tensor(out=scaled[c, i][:, cols], in0=total[:, cols], in1=weights[c][:, cols], op=ALU.mult)
-
-        def place(c, i):
-            entries = offsets[:, c * CHUNK // GROUP : (c + 1) * CHUNK // GROUP]
-            nc.vector.tensor_copy(out=pages[i][:].indirect(entries), in_=scaled[c, i][:])
-            if c == CHUNKS - 1:
-                nc.sync.dma_start(out=out[i * P : (i + 1) * P, :], in_=pages[i][:])
+        def place(u, fused=False):
+            pieces = list(enumerate(UNITS[u]))
+            if u == len(UNITS) - 1:
+                pieces = [(0, (ROW_TILES - 1, BANK, BANK))]
+            for n, (i, j0, width) in sorted(pieces, key=lambda piece: piece[1][0]):
+                entries = offsets[:, j0 // GROUP : (j0 + width) // GROUP]
+                values = scaled[u][:, n * width : (n + 1) * width]
+                if fused:
+                    nc.vector.tensor_tensor(
+                        out=pages[i][:].indirect(entries), in0=values, in1=weights[0][:, j0 : j0 + width], op=ALU.mult
+                    )
+                else:
+                    nc.vector.tensor_copy(out=pages[i][:].indirect(entries), in_=values)
+                if j0 + width == J:
+                    nc.sync.dma_start(out=out[i * P : (i + 1) * P, :], in_=pages[i][:])
 
         def add_transposed(b, t, rows, start, stop):
             nc.tensor.matmul(
@@ -237,119 +270,120 @@ def tile_list_embg_tgq4_res_kernel(tc, dy, w_words, w_scales, res, wgo, offs, ou
 
         def open_difference(b):
             difference[b] = bank(DIFFERENCE_BANKS[b], f"difference{b}")
-            h, j0 = divmod(b * P, HALF)
             for t in range(PACK):
-                add_transposed(b, t, raw[1][:, h, t, j0 : j0 + P], t == 0, False)
+                add_transposed(b, t, raw_tile(b)[:, t, :], t == 0, False)
 
-        def negate(t, cols):
-            nc.scalar.activation(out=minus[:, t, cols], in_=back[1, t][:, cols], func=COPY, scale=-1.0)
+        def negate(b):
+            minus[b] = keep.tile([P, BANK], F32, name=f"minus{b}")
+            nc.scalar.activation(out=minus[b][:], in_=back[b][:], func=COPY, scale=-1.0)
 
         def close_difference(b):
             for t in range(PACK):
-                add_transposed(b, t, minus[:, t, b * P : (b + 1) * P], False, t == PACK - 1)
-            turned[b] = held_tile([P, 2, P, 2], BF16, f"turned{b}", f"turned{b}")
+                add_transposed(b, t, minus[b][:, t * P : (t + 1) * P], False, t == PACK - 1)
+            if b in turned_at:
+                turned[b] = placed_tile([P, 2, P, 2], BF16, f"turned{b}", turned_at[b])
+            else:
+                turned[b] = keep.tile([P, 2, P, 2], BF16, name=f"turned{b}")
             nc.scalar.copy(out=turned[b][:], in_=difference[b][:].rearrange("j (u e p) -> j u p e", u=2, e=2))
 
-        def turn_back(first, count, where):
-            pairs = bank(where, f"pairs{first}")
+        def turn_back(first, count, woven):
+            pairs = bank(PAIRS_BANKS[first], f"pairs{first}")
             for b in range(count):
                 words = turned[first + b][:].rearrange("j u p e -> j (u p e)").bitcast(F32)
                 for u in range(2):
                     at = (u * count + b) * P
                     nc.tensor.transpose(pairs[:, at : at + P], words[:, u * P : (u + 1) * P], eye[:])
-            woven_words = r_woven[1][:, first * P : (first + count) * P, :].rearrange("p j t -> p (j t)").bitcast(F32)
+            r_woven[first * P] = woven
+            woven_words = r_woven[first * P][:].rearrange("p j t -> p (j t)").bitcast(F32)
             nc.scalar.copy(
                 out=woven_words.rearrange("p (j u) -> p j u", u=2),
                 in_=pairs[:, 0 : 2 * count * P].rearrange("p (u j) -> p j u", u=2),
             )
 
-        for h, share in enumerate((SCALAR_FIRST_HALF, SCALAR_SECOND_HALF)):
-            weave(nc.scalar.copy, q_woven[0], raw[0], h, 0, share)
-            weave(nc.vector.tensor_copy, q_woven[0], raw[0], h, share, HALF)
-            quantize(q_woven[0], q_codes[0], q_scale[0], E5M2, halves[h])
-            if h == 0:
-                early = bank(EARLY_BANK, "early")
-                window = slice(K - HALF, K + HALF)
-                nc.tensor.matmul_mx(
-                    out=early[:],
-                    lhsT=eye_codes[:, 0:P].bitcast(E4M3),
-                    lhsT_scale=eye_scale[:, 0:P],
-                    rhs=first_codes[:, window].bitcast(E5M2),
-                    rhs_scale=first_scale[:, window],
-                    start=True,
-                    stop=True,
-                )
-        pages[3] = placed_tile([P, T], F32, "page3", 0)
-        nc.vector.memset(pages[3][:, 0:VECTOR_CLEARS_LAST].bitcast(I32), 0)
-        read_back(0, (1, 2, 3, 0))
-        eye = placed_tile([P, P], F32, "eye", PAGE_BYTES)
-        nc.vector.tensor_copy(out=eye[:], in_=kept_eye[:])
-        pages[1] = placed_tile([P, T], F32, "page1", PAGE_BYTES + eye_bytes + WOVEN_BYTES)
-        nc.vector.memset(pages[1][:, 0 : VECTOR_CLEARS + OVERLAP].bitcast(I32), 0)
-        nc.gpsimd.memset(pages[1][:, VECTOR_CLEARS:].bitcast(I32), 0)
+        halves = [slice(0, QUARTER), slice(QUARTER, BANK)]
+
+        def add_residual(u, total):
+            for cols in halves:
+                nc.vector.tensor_tensor(out=total[:, cols], in0=dx[u][:, cols], in1=residual[u][:, cols], op=ALU.add)
+
+        holds_at = 2 * WOVEN_BYTES + 2 * PAGE_BYTES
+        half = WOVEN_BYTES // 2
+        turned_at = {5: holds_at + 2 * half, 7: holds_at + 5 * half}
+
+        weave(nc.scalar.copy, 0, 0, P)
+        weave(nc.vector.tensor_copy, 0, P, QUARTER)
+        first_tier(0)
+        pages[2] = placed_tile([P, T], F32, "page2", 0)
+        nc.vector.memset(pages[2][:].bitcast(I32), 0)
+        read_back(0)
+        read_back(1)
+        weave(nc.scalar.copy, 1, 0, QUARTER)
+        first_tier(1)
+        pages[3] = placed_tile([P, T], F32, "page3", PAGE_BYTES)
+        nc.gpsimd.memset(pages[3][:].bitcast(I32), 0)
+        read_back(2)
+        read_back(3)
+        open_sum(0)
+        open_sum(1)
+        weave(nc.scalar.copy, 2, 0, QUARTER)
+        weave(nc.scalar.copy, 3, 0, QUARTER)
         for h in range(2):
-            weave(nc.scalar.copy, q_woven[1], raw[1], h, 0, HALF)
-
-        rest = placed_tile([P, 2, PACK, HALF], BF16, "rest", PAGE_BYTES + eye_bytes)
-        nc.vector.tensor_tensor(out=rest[:, 0, 0, :], in0=raw[0][:, 0, 0, :], in1=early[:, halves[1]], op=ALU.subtract)
-        for t in range(1, PACK):
-            subtract(t)
-        subtract_half(0, 1)
-        weave(nc.scalar.copy, r_woven[0], rest, 1, HALF - SCALAR_REST, HALF)
-        for b in range(TOKEN_TILES):
-            open_difference(b)
-        for i in range(2):
-            open_sum(0, i)
-        weave(nc.vector.tensor_copy, r_woven[0], rest, 0, 0, HALF)
-        weave(nc.vector.tensor_copy, r_woven[0], rest, 1, 0, HALF - SCALAR_REST)
-        for h in range(2):
-            quantize(r_woven[0], r_codes[0], r_scale[0], E4M3, halves[h])
-
-        q_codes[1] = held_tile([P, CHUNK], U32, "q_codes1", "r_woven0")
-        quantize(q_woven[1], q_codes[1], q_scale[1], E5M2, whole)
-        for b in range(TOKEN_TILES):
-            product(0, 0, r_codes, r_scale, E4M3, slice(b * P, (b + 1) * P), False, b == TOKEN_TILES - 1)
-        close_sum(0, 1)
-        finish(0, 0)
-        place(0, 0)
-        empty_bank(0, 1)
-        read_back(1, range(PACK))
-        finish(0, 1)
-        place(0, 1)
-
-        for t in range(PACK - 1):
-            negate(t, whole)
-        for i in range(2, ROW_TILES):
-            open_sum(0, i)
-            close_sum(0, i)
+            r_woven[h * QUARTER] = own_tile(quarter_shape, BF16, f"r_woven{2 * h}")
+            for b in range(2):
+                subtract(2 * h + b, r_woven[h * QUARTER][:, b * P : (b + 1) * P, :])
+        second_tier(0, QUARTER, own_tile([P, QUARTER], U32, "r_codes0"))
+        close_sum(0)
+        close_sum(1)
+        first_tier(2)
+        second_tier(QUARTER, QUARTER, own_tile([P, QUARTER], U32, "r_codes2"))
+        first_tier(3)
+        total = held_tile([P, BANK], F32, "total0", "total0")
+        add_residual(0, total)
+        scaled[0] = keep.tile([P, BANK], F32, name="scaled0")
         for cols in halves:
-            negate(PACK - 1, cols)
-        dx_sbuf[0, 2] = keep.tile([P, CHUNK], F32, name="dx_sbuf02")
-        last_cleared = pages[3][:, VECTOR_CLEARS_LAST - 1 : VECTOR_CLEARS_LAST]
-        nc.scalar.activation(out=dx_sbuf[0, 2][:], in_=dx[0, 2][:], func=IDENTITY, bias=last_cleared)
-        for b in range(TOKEN_TILES - 1):
-            close_difference(b)
-        turn_back(0, 2, BACK_BANKS[1][2])
-        close_difference(TOKEN_TILES - 1)
-        turn_back(2, 1, BACK_BANKS[1][3])
-        turn_back(3, 1, DIFFERENCE_BANKS[0])
+            nc.vector.tensor_tensor(out=scaled[0][:, cols], in0=total[:, cols], in1=weights[0][:, 0:QUARTER], op=ALU.mult)
+        place(0)
+        finish(1, empty_bank(1), held_tile([P, BANK], F32, "total1", "total0"))
 
-        dx_sbuf[0, 3] = held_tile([P, CHUNK], F32, "dx_sbuf03", f"turned{TOKEN_TILES - 1}")
-        nc.scalar.activation(out=dx_sbuf[0, 3][:], in_=dx[0, 3][:], func=IDENTITY, bias=pages[2][:, 0:1])
-        for i in range(ROW_TILES - 1):
-            open_sum(1, i)
-        r_codes[1] = held_tile([P, CHUNK], U32, "r_codes1", "r_codes1")
-        quantize(r_woven[1], r_codes[1], r_scale[1], E4M3, whole)
-        finish(0, 2)
-        nc.gpsimd.memset(pages[3][:, VECTOR_CLEARS_LAST - OVERLAP :].bitcast(I32), 0)
-        place(0, 2)
-        finish(0, 3)
-        place(0, 3)
+        read_back(4)
+        read_back(5)
+        negate(4)
+        open_difference(4)
+        negate(5)
+        open_difference(5)
+        close_difference(4)
+        close_difference(5)
+        open_sum(2)
+        close_sum(2)
+        sums = {2: empty_bank(2)}
+        turn_back(4, 2, placed_tile(quarter_shape, BF16, "r_woven4", holds_at + 3 * half))
+        read_back(6)
+        read_back(7)
+        open_sum(3)
+        close_sum(3)
+        sums[3] = empty_bank(3)
+        place(1)
 
-        for i in range(ROW_TILES):
-            if i == ROW_TILES - 1:
-                open_sum(1, i)
-            close_sum(1, i)
-            empty_bank(1, i)
-            finish(1, i)
-            place(1, i)
+        negate(6)
+        open_difference(6)
+        negate(7)
+        open_difference(7)
+        finish(2, sums[2], placed_tile([P, BANK], F32, "total2", holds_at + half))
+        second_tier(4 * P, QUARTER, held_tile([P, QUARTER], U32, "r_codes4", "scaled1"))
+        place(2)
+        close_difference(6)
+        close_difference(7)
+        turn_back(6, 2, held_tile(quarter_shape, BF16, "r_woven6", "r_woven6"))
+        finish(3, sums[3], placed_tile([P, BANK], F32, "total3", holds_at + 4 * half))
+        open_sum(4)
+        close_sum(4)
+        sums = empty_bank(4)
+        second_tier(6 * P, QUARTER, held_tile([P, QUARTER], U32, "r_codes6", "scaled2"))
+        place(3)
+        finish(4, sums, held_tile([P, BANK], F32, "total4", "r_woven6"))
+        place(4)
+        for u in range(5, len(UNITS)):
+            open_sum(u)
+            close_sum(u)
+            finish(u, empty_bank(u), held_tile([P, BANK], F32, f"total{u}", "r_woven6"))
+            place(u)

@@ -40,10 +40,10 @@ UNITS = (
     ((1, 768, 256), (2, 768, 256)),
     ((3, 512, 256), (3, 768, 256)),
 )
-BACK_BANKS = (0, 1, 2, 3, 0, 1, 2, 6)
-DIFFERENCE_BANKS = {4: 3, 5: 4, 6: 3, 7: 4}
-DX_BANKS = (4, 5, 0, 1, 2, 3, 4, 2)
-PAIRS_BANKS = {4: 7, 6: 2}
+BACK_BANKS = (0, 1, 2, 3, 2, 3, 2, 3)
+DIFFERENCE_BANKS = {4: 0, 5: 1, 6: 0, 7: 1}
+DX_BANKS = (4, 5, 6, 7, 5, 0, 1, 5)
+PAIRS_BANKS = {4: 4, 6: 5}
 
 
 def tile_list_embg_tgq4_res_kernel(tc, dy, w_words, w_scales, res, wgo, offs, out):
@@ -68,7 +68,7 @@ def tile_list_embg_tgq4_res_kernel(tc, dy, w_words, w_scales, res, wgo, offs, ou
         offsets = keep.tile([P, J // GROUP], U16, name="offsets")
         w_codes = own_tile([P, 2 * N], U8, "w_codes")
         w_scale = own_tile([P, N], U8, "w_scale")
-        raw = [keep.tile([P, PACK, QUARTER], F32, name=f"raw{h}") for h in range(QUARTERS)]
+        raw = [held_tile([P, PACK, QUARTER], F32, f"raw{h}", f"raw{h}") for h in range(QUARTERS)]
         weights = [keep.tile([P, BANK], F32, name=f"weights{c}") for c in range(2)]
         residual = [keep.tile([P, BANK], F32, name=f"residual{u}") for u in range(len(UNITS))]
 
@@ -118,29 +118,30 @@ def tile_list_embg_tgq4_res_kernel(tc, dy, w_words, w_scales, res, wgo, offs, ou
         pages = {0: keep.tile([P, T], F32, name="page0")}
         seed = held_tile([P, P], BF16, "seed", "page1")
         make_identity(nc, seed[:])
-        ones_at = placed_tile([P, K + 2 * PACK], BF16, "ones_at", 0)
-        every_fourth = ones_at[:, PACK - 1 : K + PACK - 1 : PACK]
-        nc.vector.memset(ones_at[:].bitcast(I32), 0)
+        eye_woven = placed_tile([P, 2 * K + MX_ALIGN], BF16, "eye_woven", PAGE_BYTES - MX_ALIGN)
+        eye_words = own_tile([P, 2 * QUARTER + 16], U32, "eye_words")
+        eye_scale = own_tile([P, QUARTER], U8, "eye_scale")
+        nc.gpsimd.memset(eye_words[:, QUARTER : QUARTER + 16].bitcast(I32), 0)
+        nc.vector.memset(eye_woven[:, 0 : 2 * K].bitcast(I32), 0)
         nc.vector.memset(pages[0][:].bitcast(I32), 0)
-        nc.vector.tensor_copy(out=every_fourth, in_=seed[:])
-        eye_woven = placed_tile([P, PACK * K], BF16, "eye_woven", 2 * PAGE_BYTES - MX_ALIGN)
-        for t in range(PACK):
-            copy = nc.vector.tensor_copy if t == PACK - 1 else nc.scalar.copy
-            copy(out=eye_woven[:, t * K : (t + 1) * K], in_=ones_at[:, PACK - 1 - t : PACK - 1 - t + K])
+        ones = eye_woven[:, 2 : 2 + 2 * (K + 1)].rearrange("p (a c) -> p a c", a=2)[:, :, 0:K:PACK]
+        nc.vector.tensor_copy(out=ones, in_=seed[:].unsqueeze(1).to_broadcast([P, 2, P]))
         pages[1] = held_tile([P, T], F32, "page1", "page1")
-        nc.vector.memset(pages[1][:].bitcast(I32), 0)
+        nc.vector.memset(pages[1][:, 0 : T // 4].bitcast(I32), 0)
+        nc.vector.quantize_mx(out=eye_words[:, 0:QUARTER].bitcast(E4M3), scales=eye_scale[:], in_=eye_woven[:, 0 : 2 * K])
+        nc.vector.memset(pages[1][:, T // 4 :].bitcast(I32), 0)
+        eye_halves = eye_words[:].bitcast(U16)
+        nc.scalar.copy(out=eye_halves[:, K + 32 : 2 * K + 32], in_=eye_halves[:, 1 : K + 1])
         eye = keep.tile([P, P], F32, name="eye")
-        nc.scalar.copy(out=eye[:], in_=every_fourth)
-        eye_codes = own_tile([P, K], U32, "eye_codes")
-        eye_scale = own_tile([P, K], U8, "eye_scale")
-        nc.vector.quantize_mx(out=eye_codes[:].bitcast(E4M3), scales=eye_scale[:], in_=eye_woven[:])
+        nc.scalar.copy(out=eye[:], in_=eye_woven[:, 2 : K + 2 : PACK])
+        eye_part = [eye_words[:, at : at + P] for at in (QUARTER + 16, QUARTER + 16 + P, 0, P)]
 
         quarter_shape = [P, QUARTER, PACK]
         q_woven = [
-            placed_tile(quarter_shape, BF16, "q_woven0", 0),
-            placed_tile(quarter_shape, BF16, "q_woven1", 2 * PAGE_BYTES - WOVEN_BYTES),
-            placed_tile(quarter_shape, BF16, "q_woven2", 2 * PAGE_BYTES),
-            placed_tile(quarter_shape, BF16, "q_woven3", 2 * PAGE_BYTES + WOVEN_BYTES),
+            placed_tile(quarter_shape, BF16, "q_woven0", PAGE_BYTES - WOVEN_BYTES),
+            placed_tile(quarter_shape, BF16, "q_woven1", PAGE_BYTES + WOVEN_BYTES),
+            placed_tile(quarter_shape, BF16, "q_woven2", PAGE_BYTES),
+            held_tile(quarter_shape, BF16, "q_woven3", "raw0"),
         ]
 
         q_operand = {}
@@ -180,8 +181,8 @@ def tile_list_embg_tgq4_res_kernel(tc, dy, w_words, w_scales, res, wgo, offs, ou
                 cols = slice(t * P, (t + 1) * P)
                 nc.tensor.matmul_mx(
                     out=back[b][:, cols],
-                    lhsT=eye_codes[:, cols].bitcast(E4M3),
-                    lhsT_scale=eye_scale[:, cols],
+                    lhsT=eye_part[t].bitcast(E4M3),
+                    lhsT_scale=eye_scale[:, 0:P],
                     rhs=codes[:, 0:P].bitcast(E5M2),
                     rhs_scale=scale[:, 0:P],
                     start=True,
@@ -319,21 +320,25 @@ def tile_list_embg_tgq4_res_kernel(tc, dy, w_words, w_scales, res, wgo, offs, ou
         read_back(1)
         weave(nc.scalar.copy, 1, 0, QUARTER)
         first_tier(1)
-        pages[3] = placed_tile([P, T], F32, "page3", PAGE_BYTES)
+        pages[3] = placed_tile([P, T], F32, "page3", PAGE_BYTES + WOVEN_BYTES)
         nc.gpsimd.memset(pages[3][:].bitcast(I32), 0)
         read_back(2)
         read_back(3)
         open_sum(0)
         open_sum(1)
         weave(nc.scalar.copy, 2, 0, QUARTER)
-        weave(nc.scalar.copy, 3, 0, QUARTER)
         for h in range(2):
             r_woven[h * QUARTER] = own_tile(quarter_shape, BF16, f"r_woven{2 * h}")
             for b in range(2):
                 subtract(2 * h + b, r_woven[h * QUARTER][:, b * P : (b + 1) * P, :])
+        weave(nc.scalar.copy, 3, 0, QUARTER)
         second_tier(0, QUARTER, own_tile([P, QUARTER], U32, "r_codes0"))
         close_sum(0)
         close_sum(1)
+        open_sum(2)
+        open_sum(3)
+        open_difference(4)
+        open_difference(5)
         first_tier(2)
         second_tier(QUARTER, QUARTER, own_tile([P, QUARTER], U32, "r_codes2"))
         first_tier(3)
@@ -348,18 +353,14 @@ def tile_list_embg_tgq4_res_kernel(tc, dy, w_words, w_scales, res, wgo, offs, ou
         read_back(4)
         read_back(5)
         negate(4)
-        open_difference(4)
         negate(5)
-        open_difference(5)
         close_difference(4)
         close_difference(5)
-        open_sum(2)
         close_sum(2)
         sums = {2: empty_bank(2)}
         turn_back(4, 2, placed_tile(quarter_shape, BF16, "r_woven4", holds_at + 3 * half))
         read_back(6)
         read_back(7)
-        open_sum(3)
         close_sum(3)
         sums[3] = empty_bank(3)
         place(1)

@@ -36,8 +36,8 @@ UNITS = (
     ((0, 256, 256), (1, 256, 256)),
     ((2, 256, 256), (3, 256, 256)),
     ((0, 512, 256), (1, 512, 256)),
-    ((2, 512, 256), (0, 768, 256)),
-    ((1, 768, 256), (2, 768, 256)),
+    ((0, 768, 256), (1, 768, 256)),
+    ((2, 512, 256), (2, 768, 256)),
     ((3, 512, 256), (3, 768, 256)),
 )
 BACK_BANKS = (0, 1, 2, 3, 2, 3, 2, 3)
@@ -250,8 +250,8 @@ def tile_list_embg_tgq4_res_kernel(tc, dy, w_words, w_scales, res, wgo, offs, ou
 
         def place(u, fused=False):
             pieces = list(enumerate(UNITS[u]))
-            if u == len(UNITS) - 1:
-                pieces = [(0, (ROW_TILES - 1, BANK, BANK))]
+            if pieces[0][1][0] == pieces[1][1][0]:
+                pieces = [(0, (pieces[0][1][0], pieces[0][1][1], BANK))]
             for n, (i, j0, width) in sorted(pieces, key=lambda piece: piece[1][0]):
                 entries = offsets[:, j0 // GROUP : (j0 + width) // GROUP]
                 values = scaled[u][:, n * width : (n + 1) * width]
@@ -308,8 +308,11 @@ def tile_list_embg_tgq4_res_kernel(tc, dy, w_words, w_scales, res, wgo, offs, ou
                 nc.vector.tensor_tensor(out=total[:, cols], in0=dx[u][:, cols], in1=residual[u][:, cols], op=ALU.add)
 
         holds_at = 2 * WOVEN_BYTES + 2 * PAGE_BYTES
-        half = WOVEN_BYTES // 2
-        turned_at = {5: holds_at + 2 * half, 7: holds_at + 5 * half}
+        step = WOVEN_BYTES // 4
+        turned_at = {5: holds_at + 7 * step, 7: holds_at + 4 * step}
+
+        def total_tile(u):
+            return placed_tile([P, BANK], F32, f"total{u}", holds_at + (3 if u in (0, 1, 3) else 6) * step)
 
         weave(nc.scalar.copy, 0, 0, P)
         weave(nc.vector.tensor_copy, 0, P, QUARTER)
@@ -342,13 +345,13 @@ def tile_list_embg_tgq4_res_kernel(tc, dy, w_words, w_scales, res, wgo, offs, ou
         first_tier(2)
         second_tier(QUARTER, QUARTER, own_tile([P, QUARTER], U32, "r_codes2"))
         first_tier(3)
-        total = held_tile([P, BANK], F32, "total0", "total0")
+        total = total_tile(0)
         add_residual(0, total)
         scaled[0] = keep.tile([P, BANK], F32, name="scaled0")
         for cols in halves:
             nc.vector.tensor_tensor(out=scaled[0][:, cols], in0=total[:, cols], in1=weights[0][:, 0:QUARTER], op=ALU.mult)
         place(0)
-        finish(1, empty_bank(1), held_tile([P, BANK], F32, "total1", "total0"))
+        finish(1, empty_bank(1), total_tile(1))
 
         read_back(4)
         read_back(5)
@@ -358,7 +361,7 @@ def tile_list_embg_tgq4_res_kernel(tc, dy, w_words, w_scales, res, wgo, offs, ou
         close_difference(5)
         close_sum(2)
         sums = {2: empty_bank(2)}
-        turn_back(4, 2, placed_tile(quarter_shape, BF16, "r_woven4", holds_at + 3 * half))
+        turn_back(4, 2, placed_tile(quarter_shape, BF16, "r_woven4", holds_at))
         read_back(6)
         read_back(7)
         close_sum(3)
@@ -369,22 +372,22 @@ def tile_list_embg_tgq4_res_kernel(tc, dy, w_words, w_scales, res, wgo, offs, ou
         open_difference(6)
         negate(7)
         open_difference(7)
-        finish(2, sums[2], placed_tile([P, BANK], F32, "total2", holds_at + half))
-        second_tier(4 * P, QUARTER, held_tile([P, QUARTER], U32, "r_codes4", "scaled1"))
+        finish(2, sums[2], total_tile(2))
+        second_tier(4 * P, QUARTER, own_tile([P, QUARTER], U32, "r_codes4"))
         place(2)
         close_difference(6)
         close_difference(7)
-        turn_back(6, 2, held_tile(quarter_shape, BF16, "r_woven6", "r_woven6"))
-        finish(3, sums[3], placed_tile([P, BANK], F32, "total3", holds_at + 4 * half))
+        turn_back(6, 2, placed_tile(quarter_shape, BF16, "r_woven6", holds_at + 9 * step))
+        finish(3, sums[3], total_tile(3))
         open_sum(4)
         close_sum(4)
         sums = empty_bank(4)
-        second_tier(6 * P, QUARTER, held_tile([P, QUARTER], U32, "r_codes6", "scaled2"))
+        second_tier(6 * P, QUARTER, own_tile([P, QUARTER], U32, "r_codes6"))
         place(3)
-        finish(4, sums, held_tile([P, BANK], F32, "total4", "r_woven6"))
+        finish(4, sums, total_tile(4))
         place(4)
         for u in range(5, len(UNITS)):
             open_sum(u)
             close_sum(u)
-            finish(u, empty_bank(u), held_tile([P, BANK], F32, f"total{u}", "r_woven6"))
+            finish(u, empty_bank(u), total_tile(u))
             place(u)

@@ -1,7 +1,6 @@
 from contextlib import ExitStack
 
 import concourse.mybir as mybir
-from concourse.masks import make_identity
 
 K, N, T, J = 512, 512, 2048, 1024
 FLOPS = 3 * 2 * K * N * J
@@ -96,7 +95,15 @@ def tile_list_embg_tgq4_res_kernel(tc, dy, w_words, w_scales, res, wgo, offs, ou
         def load_weights(c):
             nc.sync.dma_start(out=weights[c][:], in_=wgo[:, c * BANK : (c + 1) * BANK])
 
-        nc.gpsimd.memset(w_scale[:].bitcast(I32), 0)
+        early = ctx.enter_context(tc.tile_pool(name="early", bufs=1))
+        diagonal = early.tile([P, P], I32, name="diagonal", offset=PAGE_BYTES - 2 * P)
+        nc.gpsimd.iota(diagonal[:], pattern=[[1, P]], base=0, channel_multiplier=-1)
+        eye_woven = placed_tile([P, 2 * K + MX_ALIGN], BF16, "eye_woven", PAGE_BYTES - MX_ALIGN)
+        eye_words = own_tile([P, 2 * QUARTER + 16], U32, "eye_words")
+        eye_scale = own_tile([P, QUARTER], U8, "eye_scale")
+        nc.vector.memset(eye_woven[:, 0 : 2 * K].bitcast(I32), 0)
+        nc.vector.memset(w_scale[:].bitcast(I32), 0)
+        nc.vector.memset(eye_words[:, QUARTER : QUARTER + 16].bitcast(I32), 0)
         load_dy(0)
         load_dy(1)
         load_dy(2)
@@ -115,25 +122,22 @@ def tile_list_embg_tgq4_res_kernel(tc, dy, w_words, w_scales, res, wgo, offs, ou
         for u in range(4, len(UNITS)):
             load_residual(u)
 
-        pages = {0: keep.tile([P, T], F32, name="page0")}
-        seed = held_tile([P, P], BF16, "seed", "page1")
-        make_identity(nc, seed[:])
-        eye_woven = placed_tile([P, 2 * K + MX_ALIGN], BF16, "eye_woven", PAGE_BYTES - MX_ALIGN)
-        eye_words = own_tile([P, 2 * QUARTER + 16], U32, "eye_words")
-        eye_scale = own_tile([P, QUARTER], U8, "eye_scale")
-        nc.gpsimd.memset(eye_words[:, QUARTER : QUARTER + 16].bitcast(I32), 0)
-        nc.vector.memset(eye_woven[:, 0 : 2 * K].bitcast(I32), 0)
-        nc.vector.memset(pages[0][:].bitcast(I32), 0)
         ones = eye_woven[:, 2 : 2 + 2 * (K + 1)].rearrange("p (a c) -> p a c", a=2)[:, :, 0:K:PACK]
-        nc.vector.tensor_copy(out=ones, in_=seed[:].unsqueeze(1).to_broadcast([P, 2, P]))
-        pages[1] = held_tile([P, T], F32, "page1", "page1")
-        nc.vector.memset(pages[1][:, 0 : T // 4].bitcast(I32), 0)
+        nc.vector.tensor_scalar(
+            out=ones, in0=diagonal[:].unsqueeze(1).to_broadcast([P, 2, P]), scalar1=0.0, scalar2=None, op0=ALU.is_equal
+        )
+        eye = keep.tile([P, P], F32, name="eye")
+        nc.vector.tensor_scalar(out=eye[:], in0=diagonal[:], scalar1=0.0, scalar2=None, op0=ALU.is_equal)
         nc.vector.quantize_mx(out=eye_words[:, 0:QUARTER].bitcast(E4M3), scales=eye_scale[:], in_=eye_woven[:, 0 : 2 * K])
-        nc.vector.memset(pages[1][:, T // 4 :].bitcast(I32), 0)
+        pages = {i: early.tile([P, T], F32, name=f"page{i}", offset=i * PAGE_BYTES) for i in range(2)}
+
+        def clear(i, first, last):
+            nc.vector.memset(pages[i][:, first:last].bitcast(I32), 0)
+
+        clear(0, 0, T)
+        clear(1, 0, 2 * BANK)
         eye_halves = eye_words[:].bitcast(U16)
         nc.scalar.copy(out=eye_halves[:, K + 32 : 2 * K + 32], in_=eye_halves[:, 1 : K + 1])
-        eye = keep.tile([P, P], F32, name="eye")
-        nc.scalar.copy(out=eye[:], in_=eye_woven[:, 2 : K + 2 : PACK])
         eye_part = [eye_words[:, at : at + P] for at in (QUARTER + 16, QUARTER + 16 + P, 0, P)]
 
         quarter_shape = [P, QUARTER, PACK]
@@ -316,9 +320,11 @@ def tile_list_embg_tgq4_res_kernel(tc, dy, w_words, w_scales, res, wgo, offs, ou
 
         weave(nc.scalar.copy, 0, 0, P)
         weave(nc.vector.tensor_copy, 0, P, QUARTER)
+        clear(1, 2 * BANK, 3 * BANK)
         first_tier(0)
+        clear(1, 3 * BANK, T)
         pages[2] = placed_tile([P, T], F32, "page2", 0)
-        nc.vector.memset(pages[2][:].bitcast(I32), 0)
+        clear(2, 0, T)
         read_back(0)
         read_back(1)
         weave(nc.scalar.copy, 1, 0, QUARTER)

@@ -312,11 +312,12 @@ def tile_list_embg_tgq4_res_kernel(tc, dy, w_words, w_scales, res, wgo, offs, ou
                 nc.vector.tensor_tensor(out=total[:, cols], in0=dx[u][:, cols], in1=residual[u][:, cols], op=ALU.add)
 
         holds_at = 2 * WOVEN_BYTES + 2 * PAGE_BYTES
-        step = WOVEN_BYTES // 4
-        turned_at = {5: holds_at + 7 * step, 7: holds_at + 4 * step}
+        step = WOVEN_BYTES // 8
+        turned_at = {5: holds_at + 8 * step, 7: holds_at + 15 * step}
+        total_at = (0, 0, 7, 14, 20, 20, 20, 20)
 
         def total_tile(u):
-            return placed_tile([P, BANK], F32, f"total{u}", holds_at + (3 if u in (0, 1, 3) else 6) * step)
+            return placed_tile([P, BANK], F32, f"total{u}", holds_at + total_at[u] * step)
 
         weave(nc.scalar.copy, 0, 0, P)
         weave(nc.vector.tensor_copy, 0, P, QUARTER)
@@ -367,7 +368,7 @@ def tile_list_embg_tgq4_res_kernel(tc, dy, w_words, w_scales, res, wgo, offs, ou
         close_difference(5)
         close_sum(2)
         sums = {2: empty_bank(2)}
-        turn_back(4, 2, placed_tile(quarter_shape, BF16, "r_woven4", holds_at))
+        turn_back(4, 2, placed_tile(quarter_shape, BF16, "r_woven4", holds_at + 21 * step))
         read_back(6)
         read_back(7)
         close_sum(3)
@@ -379,16 +380,16 @@ def tile_list_embg_tgq4_res_kernel(tc, dy, w_words, w_scales, res, wgo, offs, ou
         negate(7)
         open_difference(7)
         finish(2, sums[2], total_tile(2))
-        second_tier(4 * P, QUARTER, own_tile([P, QUARTER], U32, "r_codes4"))
+        second_tier(4 * P, QUARTER, placed_tile([P, QUARTER], U32, "r_codes4", turned_at[5]))
         place(2)
         close_difference(6)
         close_difference(7)
-        turn_back(6, 2, placed_tile(quarter_shape, BF16, "r_woven6", holds_at + 9 * step))
+        turn_back(6, 2, placed_tile(quarter_shape, BF16, "r_woven6", holds_at + 27 * step))
         finish(3, sums[3], total_tile(3))
         open_sum(4)
         close_sum(4)
         sums = empty_bank(4)
-        second_tier(6 * P, QUARTER, own_tile([P, QUARTER], U32, "r_codes6"))
+        second_tier(6 * P, QUARTER, placed_tile([P, QUARTER], U32, "r_codes6", turned_at[7]))
         place(3)
         finish(4, sums, total_tile(4))
         place(4)

@@ -23,104 +23,111 @@ GROUP = 16
 QUADRANTS = 4
 BANK = 512
 QUARTER = 256
-QUARTERS = J // QUARTER
-ROW_TILES = N // P
 MX_ALIGN = 64
+PAD_WORDS = MX_ALIGN // 4
 PAGE_BYTES = 4 * T
 WOVEN_BYTES = 2 * PACK * QUARTER
 
-UNITS = (
-    ((0, 0, 256), (1, 0, 256)),
-    ((2, 0, 256), (3, 0, 256)),
-    ((0, 256, 256), (1, 256, 256)),
-    ((2, 256, 256), (3, 256, 256)),
-    ((0, 512, 256), (1, 512, 256)),
-    ((0, 768, 256), (1, 768, 256)),
-    ((2, 512, 256), (2, 768, 256)),
-    ((3, 512, 256), (3, 768, 256)),
-)
+UNITS = [
+    unit
+    for half in (0, BANK)
+    for unit in (
+        [((0, j0), (1, j0)) for j0 in (half, half + QUARTER)] + [((i, half), (i, half + QUARTER)) for i in (2, 3)]
+    )
+]
 BACK_BANKS = (0, 1, 2, 3, 2, 3, 2, 3)
 DIFFERENCE_BANKS = {4: 0, 5: 1, 6: 0, 7: 1}
+PAIRS_BANKS = {2: 4, 3: 5}
 DX_BANKS = (4, 5, 6, 7, 5, 0, 1, 5)
-PAIRS_BANKS = {4: 4, 6: 5}
 
 
 def tile_list_embg_tgq4_res_kernel(tc, dy, w_words, w_scales, res, wgo, offs, out):
     nc = tc.nc
     with ExitStack() as ctx:
         keep = ctx.enter_context(tc.tile_pool(name="keep", bufs=1))
-        shared = ctx.enter_context(tc.tile_pool(name="shared", bufs=1))
+        early = ctx.enter_context(tc.tile_pool(name="early", bufs=1))
+        head = ctx.enter_context(tc.tile_pool(name="head", bufs=1))
+        late = ctx.enter_context(tc.tile_pool(name="late", bufs=1))
         psum = ctx.enter_context(tc.psum_pool(name="psum", bufs=1))
-
-        def held_tile(shape, dtype, name, tag):
-            return keep.tile(shape, dtype, name=name, tag=tag, align_bytes=MX_ALIGN)
 
         def own_tile(shape, dtype, name):
             return keep.tile(shape, dtype, name=name, align_bytes=MX_ALIGN)
 
-        def placed_tile(shape, dtype, name, offset):
-            return shared.tile(shape, dtype, name=name, offset=offset, align_bytes=MX_ALIGN)
+        def placed_tile(pool, shape, dtype, name, offset):
+            return pool.tile(shape, dtype, name=name, offset=offset, align_bytes=MX_ALIGN)
 
         def bank(b, name):
             return psum.tile([P, BANK], F32, name=name, tag=f"bank{b}")
 
+        def one_row_tile(u):
+            return UNITS[u][0][0] == UNITS[u][1][0]
+
+        diagonal_at = PAGE_BYTES - 2 * P
+        q_woven_at = (PAGE_BYTES - WOVEN_BYTES // 2, PAGE_BYTES + WOVEN_BYTES, PAGE_BYTES)
+        eye_woven_at = q_woven_at[0] + WOVEN_BYTES - MX_ALIGN
+        page_at = {2: 0, 3: q_woven_at[1]}
+        step = WOVEN_BYTES // 8
+        total_at = [step * 7 * max(u - 1, 0) for u in range(4)] + [step * 20] * 4
+        turned_at = {2 * h + 1: total_at[h] + step for h in (2, 3)}
+        r_woven_at = {h: total_at[h + 1] + 7 * step for h in (2, 3)}
+
         offsets = keep.tile([P, J // GROUP], U16, name="offsets")
         w_codes = own_tile([P, 2 * N], U8, "w_codes")
         w_scale = own_tile([P, N], U8, "w_scale")
-        raw = [held_tile([P, PACK, QUARTER], F32, f"raw{h}", f"raw{h}") for h in range(QUARTERS)]
         weights = [keep.tile([P, BANK], F32, name=f"weights{c}") for c in range(2)]
-        residual = [keep.tile([P, BANK], F32, name=f"residual{u}") for u in range(len(UNITS))]
-
+        residual = {}
         dy_rows = dy.rearrange("(p t) j -> p t j", t=PACK)
+        raw = {}
 
-        def load_dy(h):
-            nc.sync.dma_start(out=raw[h][:], in_=dy_rows[:, :, h * QUARTER : (h + 1) * QUARTER])
+        def load_dy(first, count):
+            rows = keep.tile([P, PACK, count * P], F32, name=f"raw{first}", tag=f"raw{first}", align_bytes=MX_ALIGN)
+            nc.sync.dma_start(out=rows[:], in_=dy_rows[:, :, first * P : (first + count) * P])
+            for b in range(count):
+                raw[first + b] = rows[:, :, b * P : (b + 1) * P]
+            return rows
 
-        def load_residual(u):
-            pieces = UNITS[u]
-            first, j0, width = pieces[0]
-            if all(piece[1] == j0 for piece in pieces):
-                rows = res[first * P : (first + len(pieces)) * P, j0 : j0 + width]
-                nc.sync.dma_start(
-                    out=residual[u][:].rearrange("p (i j) -> p i j", j=width), in_=rows.rearrange("(i p) j -> p i j", p=P)
-                )
-            elif all(piece[0] == first for piece in pieces):
-                nc.sync.dma_start(out=residual[u][:], in_=res[first * P : (first + 1) * P, j0 : j0 + BANK])
-            else:
-                for n, (i, j, width) in enumerate(pieces):
-                    nc.sync.dma_start(
-                        out=residual[u][:, n * width : (n + 1) * width], in_=res[i * P : (i + 1) * P, j : j + width]
-                    )
+        def load_residual(u, units=1):
+            i, j0 = UNITS[u][0]
+            row_tiles, width = (units, BANK) if one_row_tile(u) else (2, QUARTER)
+            rows = keep.tile([P, units * BANK], F32, name=f"residual{u}")
+            nc.sync.dma_start(
+                out=rows[:].rearrange("p (i j) -> p i j", i=row_tiles),
+                in_=res[i * P : (i + row_tiles) * P, j0 : j0 + width].rearrange("(i p) j -> p i j", p=P),
+            )
+            for n in range(units):
+                residual[u + n] = rows[:, n * BANK : (n + 1) * BANK]
 
         def load_weights(c):
             nc.sync.dma_start(out=weights[c][:], in_=wgo[:, c * BANK : (c + 1) * BANK])
 
-        early = ctx.enter_context(tc.tile_pool(name="early", bufs=1))
-        diagonal = early.tile([P, P], I32, name="diagonal", offset=PAGE_BYTES - 2 * P)
+        diagonal = placed_tile(early, [P, P], I32, "diagonal", diagonal_at)
         nc.gpsimd.iota(diagonal[:], pattern=[[1, P]], base=0, channel_multiplier=-1)
-        eye_woven = placed_tile([P, 2 * K + MX_ALIGN], BF16, "eye_woven", PAGE_BYTES - MX_ALIGN)
-        eye_words = own_tile([P, 2 * QUARTER + 16], U32, "eye_words")
+        eye_woven = placed_tile(head, [P, 2 * K + MX_ALIGN // 2], BF16, "eye_woven", eye_woven_at)
+        eye_words = own_tile([P, 2 * QUARTER + PAD_WORDS], U32, "eye_words")
         eye_scale = own_tile([P, QUARTER], U8, "eye_scale")
         nc.vector.memset(eye_woven[:, 0 : 2 * K].bitcast(I32), 0)
         nc.vector.memset(w_scale[:].bitcast(I32), 0)
-        nc.vector.memset(eye_words[:, QUARTER : QUARTER + 16].bitcast(I32), 0)
-        load_dy(0)
-        load_dy(1)
-        load_dy(2)
+        nc.vector.memset(eye_words[:, QUARTER : QUARTER + PAD_WORDS].bitcast(I32), 0)
+
+        load_dy(0, 2)
+        load_dy(2, 1)
+        load_dy(3, 1)
+        third = load_dy(4, 2)
         nc.sync.dma_start(out=w_codes[:].bitcast(I32), in_=w_words[0].bitcast(I32))
         for q in range(QUADRANTS):
             nc.sync.dma_start(
                 out=w_scale[32 * q : 32 * q + 4, :].bitcast(I32), in_=w_scales[0, 4 * q : 4 * q + 4, :].bitcast(I32)
             )
-        load_dy(3)
+        fourth = load_dy(6, 2)
         load_residual(0)
         load_weights(0)
         nc.sync.dma_start(offsets[:], offs)
         for u in range(1, 4):
             load_residual(u)
         load_weights(1)
-        for u in range(4, len(UNITS)):
-            load_residual(u)
+        load_residual(4)
+        load_residual(5)
+        load_residual(6, units=2)
 
         ones = eye_woven[:, 2 : 2 + 2 * (K + 1)].rearrange("p (a c) -> p a c", a=2)[:, :, 0:K:PACK]
         nc.vector.tensor_scalar(
@@ -129,62 +136,63 @@ def tile_list_embg_tgq4_res_kernel(tc, dy, w_words, w_scales, res, wgo, offs, ou
         eye = keep.tile([P, P], F32, name="eye")
         nc.vector.tensor_scalar(out=eye[:], in0=diagonal[:], scalar1=0.0, scalar2=None, op0=ALU.is_equal)
         nc.vector.quantize_mx(out=eye_words[:, 0:QUARTER].bitcast(E4M3), scales=eye_scale[:], in_=eye_woven[:, 0 : 2 * K])
-        pages = {i: early.tile([P, T], F32, name=f"page{i}", offset=i * PAGE_BYTES) for i in range(2)}
+        pages = {i: placed_tile(early, [P, T], F32, f"page{i}", i * PAGE_BYTES) for i in range(2)}
 
         def clear(i, first, last):
             nc.vector.memset(pages[i][:, first:last].bitcast(I32), 0)
 
         clear(0, 0, T)
         clear(1, 0, 2 * BANK)
+        moved_at = QUARTER + PAD_WORDS
         eye_halves = eye_words[:].bitcast(U16)
-        nc.scalar.copy(out=eye_halves[:, K + 32 : 2 * K + 32], in_=eye_halves[:, 1 : K + 1])
-        eye_part = [eye_words[:, at : at + P] for at in (QUARTER + 16, QUARTER + 16 + P, 0, P)]
+        nc.scalar.copy(out=eye_halves[:, 2 * moved_at : 2 * moved_at + K], in_=eye_halves[:, 1 : K + 1])
+        eye_part = [eye_words[:, at : at + P] for at in (moved_at, moved_at + P, 0, P)]
 
         quarter_shape = [P, QUARTER, PACK]
-        q_woven = [
-            placed_tile(quarter_shape, BF16, "q_woven0", PAGE_BYTES - WOVEN_BYTES),
-            placed_tile(quarter_shape, BF16, "q_woven1", PAGE_BYTES + WOVEN_BYTES),
-            placed_tile(quarter_shape, BF16, "q_woven2", PAGE_BYTES),
-            held_tile(quarter_shape, BF16, "q_woven3", "raw0"),
-        ]
+        q_woven = [placed_tile(head, quarter_shape, BF16, f"q_woven{h}", q_woven_at[h]) for h in range(3)]
+        q_woven.append(keep.tile(quarter_shape, BF16, name="q_woven3", tag="raw0", align_bytes=MX_ALIGN))
 
         q_operand = {}
         r_operand = {}
+        r_woven = {}
         back = {}
-        dx = {}
-        scaled = {}
         minus = {}
         difference = {}
         turned = {}
-        r_woven = {}
+        dx = {}
+        scaled = {}
 
-        def weave(copy, h, j0, j1):
+        def weave(copy, woven, rows):
             copy(
-                out=q_woven[h][:, j0:j1, :].rearrange("p (g i) t -> p g t i", i=PACK),
-                in_=raw[h][:, :, j0:j1].rearrange("p t (g i) -> p g t i", i=PACK),
+                out=woven.rearrange("p (g i) t -> p g t i", i=PACK),
+                in_=rows.rearrange("p t (g i) -> p g t i", i=PACK),
             )
 
-        def quantize(operand, woven, j0, width, fmt, codes):
-            scale = own_tile([P, width], U8, f"scale_{len(q_operand)}_{len(r_operand)}")
-            nc.vector.quantize_mx(
-                out=codes[:, 0:width].bitcast(fmt), scales=scale[:], in_=woven[:].rearrange("p j t -> p (j t)")
-            )
-            for j in range(0, width, P):
-                operand[j0 + j] = (codes[:, j:width], scale[:, j:width])
+        def weave_tile(copy, b):
+            weave(copy, q_woven[b // 2][:, b % 2 * P : (b % 2 + 1) * P, :], raw[b])
+
+        def quantize(operand, woven, h, fmt, codes, name):
+            scale = own_tile([P, QUARTER], U8, name)
+            nc.vector.quantize_mx(out=codes[:].bitcast(fmt), scales=scale[:], in_=woven[:].rearrange("p j t -> p (j t)"))
+            for j in (0, P):
+                operand[h * QUARTER + j] = (codes[:, j:QUARTER], scale[:, j:QUARTER])
 
         def first_tier(h):
-            quantize(q_operand, q_woven[h], h * QUARTER, QUARTER, E5M2, own_tile([P, QUARTER], U32, f"q_codes{h}"))
+            quantize(q_operand, q_woven[h], h, E5M2, own_tile([P, QUARTER], U32, f"q_codes{h}"), f"q_scale{h}")
 
-        def second_tier(j0, width, codes):
-            quantize(r_operand, r_woven[j0], j0, width, E4M3, codes)
+        def second_tier(h):
+            if h in r_woven_at:
+                codes = placed_tile(late, [P, QUARTER], U32, f"r_codes{h}", turned_at[2 * h + 1])
+            else:
+                codes = own_tile([P, QUARTER], U32, f"r_codes{h}")
+            quantize(r_operand, r_woven[h], h, E4M3, codes, f"r_scale{h}")
 
         def read_back(b):
             back[b] = bank(BACK_BANKS[b], f"back{b}")
             codes, scale = q_operand[b * P]
             for t in range(PACK):
-                cols = slice(t * P, (t + 1) * P)
                 nc.tensor.matmul_mx(
-                    out=back[b][:, cols],
+                    out=back[b][:, t * P : (t + 1) * P],
                     lhsT=eye_part[t].bitcast(E4M3),
                     lhsT_scale=eye_scale[:, 0:P],
                     rhs=codes[:, 0:P].bitcast(E5M2),
@@ -193,78 +201,69 @@ def tile_list_embg_tgq4_res_kernel(tc, dy, w_words, w_scales, res, wgo, offs, ou
                     stop=True,
                 )
 
-        def raw_tile(b):
-            h, j0 = divmod(b * P, QUARTER)
-            return raw[h][:, :, j0 : j0 + P]
-
-        def subtract(b, woven):
-            nc.vector.tensor_tensor(
-                out=woven.rearrange("p (g i) t -> p g t i", i=2),
-                in0=raw_tile(b).rearrange("p t (g i) -> p g t i", i=2),
-                in1=back[b][:].rearrange("p (t g i) -> p g t i", t=PACK, i=2),
-                op=ALU.subtract,
-            )
-
-        def products(u, operand, fmt, opening):
-            pieces = list(enumerate(UNITS[u]))
-            if not opening:
-                pieces = sorted(pieces, key=lambda piece: -piece[1][1])
-            for step, (n, (i, j0, width)) in enumerate(pieces):
-                codes, scale = operand[j0]
-                nc.tensor.matmul_mx(
-                    out=dx[u][:, n * width : (n + 1) * width],
-                    lhsT=w_codes[:, 2 * P * i : 2 * P * (i + 1)].bitcast(E2M1),
-                    lhsT_scale=w_scale[:, P * i : P * (i + 1)],
-                    rhs=codes[:, 0:width].bitcast(fmt),
-                    rhs_scale=scale[:, 0:width],
-                    start=opening and step == 0,
-                    stop=not opening and step == len(pieces) - 1,
+        def subtract(h):
+            r_woven[h] = own_tile(quarter_shape, BF16, f"r_woven{h}")
+            for b in (2 * h, 2 * h + 1):
+                nc.vector.tensor_tensor(
+                    out=r_woven[h][:, b % 2 * P : (b % 2 + 1) * P, :].rearrange("p (g i) t -> p g t i", i=2),
+                    in0=raw[b].rearrange("p t (g i) -> p g t i", i=2),
+                    in1=back[b][:].rearrange("p (t g i) -> p g t i", t=PACK, i=2),
+                    op=ALU.subtract,
                 )
+
+        def product(u, n, operand, fmt, start, stop):
+            i, j0 = UNITS[u][n]
+            codes, scale = operand[j0]
+            nc.tensor.matmul_mx(
+                out=dx[u][:, n * QUARTER : (n + 1) * QUARTER],
+                lhsT=w_codes[:, 2 * P * i : 2 * P * (i + 1)].bitcast(E2M1),
+                lhsT_scale=w_scale[:, P * i : P * (i + 1)],
+                rhs=codes.bitcast(fmt),
+                rhs_scale=scale,
+                start=start,
+                stop=stop,
+            )
 
         def open_sum(u):
             dx[u] = bank(DX_BANKS[u], f"dx{u}")
-            products(u, q_operand, E5M2, True)
+            for n in range(2):
+                product(u, n, q_operand, E5M2, n == 0, False)
 
         def close_sum(u):
-            products(u, r_operand, E4M3, False)
+            for n in range(2):
+                product(u, n, r_operand, E4M3, False, n == 1)
 
-        def unit_weights(u):
-            pieces = UNITS[u]
-            c, j0 = divmod(pieces[0][1], BANK)
-            width = pieces[0][2]
-            if pieces[1][1] != pieces[0][1]:
-                return weights[c][:].rearrange("p (i j) -> p i j", j=width)
-            return weights[c][:, j0 : j0 + width].unsqueeze(1).to_broadcast([P, len(pieces), width])
+        def total_tile(u):
+            return placed_tile(late, [P, BANK], F32, f"total{u}", total_at[u])
 
         def empty_bank(u):
-            sums = keep.tile([P, BANK], F32, name=f"dx_sbuf{u}")
+            sums = keep.tile([P, BANK], F32, name=f"sums{u}")
             nc.scalar.copy(out=sums[:], in_=dx[u][:])
             return sums
 
-        def finish(u, sums, total):
-            scaled[u] = held_tile([P, BANK], F32, f"scaled{u}", f"scaled{u}")
-            width = UNITS[u][0][2]
-            nc.gpsimd.tensor_tensor(out=total[:], in0=sums[:], in1=residual[u][:], op=ALU.add)
-            nc.gpsimd.tensor_tensor(
-                out=scaled[u][:].rearrange("p (i j) -> p i j", j=width),
-                in0=total[:].rearrange("p (i j) -> p i j", j=width),
-                in1=unit_weights(u),
-                op=ALU.mult,
-            )
+        def finish(u, sums):
+            total = total_tile(u)
+            scaled[u] = keep.tile([P, BANK], F32, name=f"scaled{u}")
+            c, j0 = divmod(UNITS[u][0][1], BANK)
+            nc.gpsimd.tensor_tensor(out=total[:], in0=sums[:], in1=residual[u], op=ALU.add)
+            if one_row_tile(u):
+                nc.gpsimd.tensor_tensor(out=scaled[u][:], in0=total[:], in1=weights[c][:], op=ALU.mult)
+            else:
+                nc.gpsimd.tensor_tensor(
+                    out=scaled[u][:].rearrange("p (i j) -> p i j", i=2),
+                    in0=total[:].rearrange("p (i j) -> p i j", i=2),
+                    in1=weights[c][:, j0 : j0 + QUARTER].unsqueeze(1).to_broadcast([P, 2, QUARTER]),
+                    op=ALU.mult,
+                )
 
-        def place(u, fused=False):
-            pieces = list(enumerate(UNITS[u]))
-            if pieces[0][1][0] == pieces[1][1][0]:
-                pieces = [(0, (pieces[0][1][0], pieces[0][1][1], BANK))]
-            for n, (i, j0, width) in sorted(pieces, key=lambda piece: piece[1][0]):
-                entries = offsets[:, j0 // GROUP : (j0 + width) // GROUP]
-                values = scaled[u][:, n * width : (n + 1) * width]
-                if fused:
-                    nc.vector.tensor_tensor(
-                        out=pages[i][:].indirect(entries), in0=values, in1=weights[0][:, j0 : j0 + width], op=ALU.mult
-                    )
-                else:
-                    nc.vector.tensor_copy(out=pages[i][:].indirect(entries), in_=values)
+        def place(u):
+            width = BANK if one_row_tile(u) else QUARTER
+            for n in range(BANK // width):
+                i, j0 = UNITS[u][n]
+                nc.vector.tensor_copy(
+                    out=pages[i][:].indirect(offsets[:, j0 // GROUP : (j0 + width) // GROUP]),
+                    in_=scaled[u][:, n * width : (n + 1) * width],
+                )
                 if j0 + width == J:
                     nc.sync.dma_start(out=out[i * P : (i + 1) * P, :], in_=pages[i][:])
 
@@ -276,7 +275,7 @@ def tile_list_embg_tgq4_res_kernel(tc, dy, w_words, w_scales, res, wgo, offs, ou
         def open_difference(b):
             difference[b] = bank(DIFFERENCE_BANKS[b], f"difference{b}")
             for t in range(PACK):
-                add_transposed(b, t, raw_tile(b)[:, t, :], t == 0, False)
+                add_transposed(b, t, raw[b][:, t, :], t == 0, False)
 
         def negate(b):
             minus[b] = keep.tile([P, BANK], F32, name=f"minus{b}")
@@ -286,63 +285,48 @@ def tile_list_embg_tgq4_res_kernel(tc, dy, w_words, w_scales, res, wgo, offs, ou
             for t in range(PACK):
                 add_transposed(b, t, minus[b][:, t * P : (t + 1) * P], False, t == PACK - 1)
             if b in turned_at:
-                turned[b] = placed_tile([P, 2, P, 2], BF16, f"turned{b}", turned_at[b])
+                turned[b] = placed_tile(late, [P, 2, P, 2], BF16, f"turned{b}", turned_at[b])
             else:
                 turned[b] = keep.tile([P, 2, P, 2], BF16, name=f"turned{b}")
-            nc.scalar.copy(out=turned[b][:], in_=difference[b][:].rearrange("j (u e p) -> j u p e", u=2, e=2))
+            nc.scalar.copy(out=turned[b][:], in_=difference[b][:].rearrange("j (v e p) -> j v p e", v=2, e=2))
 
-        def turn_back(first, count, woven):
-            pairs = bank(PAIRS_BANKS[first], f"pairs{first}")
-            for b in range(count):
-                words = turned[first + b][:].rearrange("j u p e -> j (u p e)").bitcast(F32)
-                for u in range(2):
-                    at = (u * count + b) * P
-                    nc.tensor.transpose(pairs[:, at : at + P], words[:, u * P : (u + 1) * P], eye[:])
-            r_woven[first * P] = woven
-            woven_words = r_woven[first * P][:].rearrange("p j t -> p (j t)").bitcast(F32)
+        def turn_back(h):
+            pairs = bank(PAIRS_BANKS[h], f"pairs{h}")
+            for b in range(2):
+                words = turned[2 * h + b][:].rearrange("j v p e -> j (v p e)").bitcast(F32)
+                for v in range(2):
+                    at = v * QUARTER + b * P
+                    nc.tensor.transpose(pairs[:, at : at + P], words[:, v * P : (v + 1) * P], eye[:])
+            r_woven[h] = placed_tile(late, quarter_shape, BF16, f"r_woven{h}", r_woven_at[h])
+            woven_words = r_woven[h][:].rearrange("p j t -> p (j t)").bitcast(F32)
             nc.scalar.copy(
-                out=woven_words.rearrange("p (j u) -> p j u", u=2),
-                in_=pairs[:, 0 : 2 * count * P].rearrange("p (u j) -> p j u", u=2),
+                out=woven_words.rearrange("p (j v) -> p j v", v=2), in_=pairs[:].rearrange("p (v j) -> p j v", v=2)
             )
 
-        halves = [slice(0, QUARTER), slice(QUARTER, BANK)]
-
-        def add_residual(u, total):
-            for cols in halves:
-                nc.vector.tensor_tensor(out=total[:, cols], in0=dx[u][:, cols], in1=residual[u][:, cols], op=ALU.add)
-
-        holds_at = 2 * WOVEN_BYTES + 2 * PAGE_BYTES
-        step = WOVEN_BYTES // 8
-        turned_at = {5: holds_at + 8 * step, 7: holds_at + 15 * step}
-        total_at = (0, 0, 7, 14, 20, 20, 20, 20)
-
-        def total_tile(u):
-            return placed_tile([P, BANK], F32, f"total{u}", holds_at + total_at[u] * step)
-
-        weave(nc.scalar.copy, 0, 0, P)
-        weave(nc.vector.tensor_copy, 0, P, QUARTER)
+        weave_tile(nc.scalar.copy, 0)
+        weave_tile(nc.vector.tensor_copy, 1)
         clear(1, 2 * BANK, 3 * BANK)
         first_tier(0)
         clear(1, 3 * BANK, T)
-        pages[2] = placed_tile([P, T], F32, "page2", 0)
+        pages[2] = placed_tile(head, [P, T], F32, "page2", page_at[2])
         clear(2, 0, T)
         read_back(0)
         read_back(1)
-        weave(nc.scalar.copy, 1, 0, QUARTER)
+        weave_tile(nc.scalar.copy, 2)
+        weave_tile(nc.scalar.copy, 3)
         first_tier(1)
-        pages[3] = placed_tile([P, T], F32, "page3", PAGE_BYTES + WOVEN_BYTES)
+        pages[3] = placed_tile(head, [P, T], F32, "page3", page_at[3])
         nc.gpsimd.memset(pages[3][:].bitcast(I32), 0)
         read_back(2)
         read_back(3)
         open_sum(0)
         open_sum(1)
-        weave(nc.scalar.copy, 2, 0, QUARTER)
-        for h in range(2):
-            r_woven[h * QUARTER] = own_tile(quarter_shape, BF16, f"r_woven{2 * h}")
-            for b in range(2):
-                subtract(2 * h + b, r_woven[h * QUARTER][:, b * P : (b + 1) * P, :])
-        weave(nc.scalar.copy, 3, 0, QUARTER)
-        second_tier(0, QUARTER, own_tile([P, QUARTER], U32, "r_codes0"))
+        weave(nc.scalar.copy, q_woven[2][:], third[:])
+        subtract(0)
+        subtract(1)
+        weave(nc.scalar.copy, q_woven[3][:], fourth[:])
+        second_tier(0)
+        second_tier(1)
         close_sum(0)
         close_sum(1)
         open_sum(2)
@@ -350,15 +334,16 @@ def tile_list_embg_tgq4_res_kernel(tc, dy, w_words, w_scales, res, wgo, offs, ou
         open_difference(4)
         open_difference(5)
         first_tier(2)
-        second_tier(QUARTER, QUARTER, own_tile([P, QUARTER], U32, "r_codes2"))
         first_tier(3)
+        pieces = [slice(0, QUARTER), slice(QUARTER, BANK)]
         total = total_tile(0)
-        add_residual(0, total)
+        for cols in pieces:
+            nc.vector.tensor_tensor(out=total[:, cols], in0=dx[0][:, cols], in1=residual[0][:, cols], op=ALU.add)
         scaled[0] = keep.tile([P, BANK], F32, name="scaled0")
-        for cols in halves:
+        for cols in pieces:
             nc.vector.tensor_tensor(out=scaled[0][:, cols], in0=total[:, cols], in1=weights[0][:, 0:QUARTER], op=ALU.mult)
         place(0)
-        finish(1, empty_bank(1), total_tile(1))
+        finish(1, empty_bank(1))
 
         read_back(4)
         read_back(5)
@@ -367,34 +352,34 @@ def tile_list_embg_tgq4_res_kernel(tc, dy, w_words, w_scales, res, wgo, offs, ou
         close_difference(4)
         close_difference(5)
         close_sum(2)
-        sums = {2: empty_bank(2)}
-        turn_back(4, 2, placed_tile(quarter_shape, BF16, "r_woven4", holds_at + 21 * step))
+        sums2 = empty_bank(2)
+        turn_back(2)
         read_back(6)
         read_back(7)
         close_sum(3)
-        sums[3] = empty_bank(3)
+        sums3 = empty_bank(3)
         place(1)
 
         negate(6)
         open_difference(6)
         negate(7)
         open_difference(7)
-        finish(2, sums[2], total_tile(2))
-        second_tier(4 * P, QUARTER, placed_tile([P, QUARTER], U32, "r_codes4", turned_at[5]))
+        finish(2, sums2)
+        second_tier(2)
         place(2)
         close_difference(6)
         close_difference(7)
-        turn_back(6, 2, placed_tile(quarter_shape, BF16, "r_woven6", holds_at + 27 * step))
-        finish(3, sums[3], total_tile(3))
+        turn_back(3)
+        finish(3, sums3)
         open_sum(4)
         close_sum(4)
-        sums = empty_bank(4)
-        second_tier(6 * P, QUARTER, placed_tile([P, QUARTER], U32, "r_codes6", turned_at[7]))
+        sums4 = empty_bank(4)
+        second_tier(3)
         place(3)
-        finish(4, sums, total_tile(4))
+        finish(4, sums4)
         place(4)
         for u in range(5, len(UNITS)):
             open_sum(u)
             close_sum(u)
-            finish(u, empty_bank(u), total_tile(u))
+            finish(u, empty_bank(u))
             place(u)

@@ -28,13 +28,11 @@ PAD_WORDS = MX_ALIGN // 4
 PAGE_BYTES = 4 * T
 WOVEN_BYTES = 2 * PACK * QUARTER
 
-UNITS = [
-    unit
-    for half in (0, BANK)
-    for unit in (
-        [((0, j0), (1, j0)) for j0 in (half, half + QUARTER)] + [((i, half), (i, half + QUARTER)) for i in (2, 3)]
-    )
-]
+UNITS = (
+    [((i, j0), (i + 1, j0)) for j0 in (0, QUARTER) for i in (0, 2)]
+    + [((0, j0), (1, j0)) for j0 in (BANK, BANK + QUARTER)]
+    + [((i, BANK), (i, BANK + QUARTER)) for i in (2, 3)]
+)
 BACK_BANKS = (0, 1, 2, 3, 2, 3, 2, 3)
 DIFFERENCE_BANKS = {4: 0, 5: 1, 6: 0, 7: 1}
 PAIRS_BANKS = {2: 4, 3: 5}
@@ -75,27 +73,24 @@ def tile_list_embg_tgq4_res_kernel(tc, dy, w_words, w_scales, res, wgo, offs, ou
         w_codes = own_tile([P, 2 * N], U8, "w_codes")
         w_scale = own_tile([P, N], U8, "w_scale")
         weights = [keep.tile([P, BANK], F32, name=f"weights{c}") for c in range(2)]
-        residual = {}
+        residual = [keep.tile([P, BANK], F32, name=f"residual{u}") for u in range(len(UNITS))]
         dy_rows = dy.rearrange("(p t) j -> p t j", t=PACK)
-        raw = {}
+        raw_quarter = [
+            keep.tile([P, PACK, QUARTER], F32, name=f"raw{h}", tag=f"raw{h}", align_bytes=MX_ALIGN)
+            for h in range(J // QUARTER)
+        ]
+        raw = [raw_quarter[b // 2][:, :, b % 2 * P : (b % 2 + 1) * P] for b in range(J // P)]
 
-        def load_dy(first, count):
-            rows = keep.tile([P, PACK, count * P], F32, name=f"raw{first}", tag=f"raw{first}", align_bytes=MX_ALIGN)
-            nc.sync.dma_start(out=rows[:], in_=dy_rows[:, :, first * P : (first + count) * P])
-            for b in range(count):
-                raw[first + b] = rows[:, :, b * P : (b + 1) * P]
-            return rows
+        def load_dy(h):
+            nc.sync.dma_start(out=raw_quarter[h][:], in_=dy_rows[:, :, h * QUARTER : (h + 1) * QUARTER])
 
-        def load_residual(u, units=1):
+        def load_residual(u):
             i, j0 = UNITS[u][0]
-            row_tiles, width = (units, BANK) if one_row_tile(u) else (2, QUARTER)
-            rows = keep.tile([P, units * BANK], F32, name=f"residual{u}")
+            row_tiles = 1 if one_row_tile(u) else 2
             nc.sync.dma_start(
-                out=rows[:].rearrange("p (i j) -> p i j", i=row_tiles),
-                in_=res[i * P : (i + row_tiles) * P, j0 : j0 + width].rearrange("(i p) j -> p i j", p=P),
+                out=residual[u][:].rearrange("p (i j) -> p i j", i=row_tiles),
+                in_=res[i * P : (i + row_tiles) * P, j0 : j0 + BANK // row_tiles].rearrange("(i p) j -> p i j", p=P),
             )
-            for n in range(units):
-                residual[u + n] = rows[:, n * BANK : (n + 1) * BANK]
 
         def load_weights(c):
             nc.sync.dma_start(out=weights[c][:], in_=wgo[:, c * BANK : (c + 1) * BANK])
@@ -109,25 +104,23 @@ def tile_list_embg_tgq4_res_kernel(tc, dy, w_words, w_scales, res, wgo, offs, ou
         nc.vector.memset(w_scale[:].bitcast(I32), 0)
         nc.vector.memset(eye_words[:, QUARTER : QUARTER + PAD_WORDS].bitcast(I32), 0)
 
-        load_dy(0, 2)
-        load_dy(2, 1)
-        load_dy(3, 1)
-        third = load_dy(4, 2)
+        load_dy(0)
+        load_dy(1)
         nc.sync.dma_start(out=w_codes[:].bitcast(I32), in_=w_words[0].bitcast(I32))
         for q in range(QUADRANTS):
             nc.sync.dma_start(
                 out=w_scale[32 * q : 32 * q + 4, :].bitcast(I32), in_=w_scales[0, 4 * q : 4 * q + 4, :].bitcast(I32)
             )
-        fourth = load_dy(6, 2)
+        load_dy(2)
+        load_dy(3)
         load_residual(0)
         load_weights(0)
         nc.sync.dma_start(offsets[:], offs)
-        for u in range(1, 4):
+        for u in range(1, len(UNITS) // 2):
             load_residual(u)
         load_weights(1)
-        load_residual(4)
-        load_residual(5)
-        load_residual(6, units=2)
+        for u in range(len(UNITS) // 2, len(UNITS)):
+            load_residual(u)
 
         ones = eye_woven[:, 2 : 2 + 2 * (K + 1)].rearrange("p (a c) -> p a c", a=2)[:, :, 0:K:PACK]
         nc.vector.tensor_scalar(
@@ -167,9 +160,6 @@ def tile_list_embg_tgq4_res_kernel(tc, dy, w_words, w_scales, res, wgo, offs, ou
                 out=woven.rearrange("p (g i) t -> p g t i", i=PACK),
                 in_=rows.rearrange("p t (g i) -> p g t i", i=PACK),
             )
-
-        def weave_tile(copy, b):
-            weave(copy, q_woven[b // 2][:, b % 2 * P : (b % 2 + 1) * P, :], raw[b])
 
         def quantize(operand, woven, h, fmt, codes, name):
             scale = own_tile([P, QUARTER], U8, name)
@@ -245,7 +235,7 @@ def tile_list_embg_tgq4_res_kernel(tc, dy, w_words, w_scales, res, wgo, offs, ou
             total = total_tile(u)
             scaled[u] = keep.tile([P, BANK], F32, name=f"scaled{u}")
             c, j0 = divmod(UNITS[u][0][1], BANK)
-            nc.gpsimd.tensor_tensor(out=total[:], in0=sums[:], in1=residual[u], op=ALU.add)
+            nc.gpsimd.tensor_tensor(out=total[:], in0=sums[:], in1=residual[u][:], op=ALU.add)
             if one_row_tile(u):
                 nc.gpsimd.tensor_tensor(out=scaled[u][:], in0=total[:], in1=weights[c][:], op=ALU.mult)
             else:
@@ -303,8 +293,8 @@ def tile_list_embg_tgq4_res_kernel(tc, dy, w_words, w_scales, res, wgo, offs, ou
                 out=woven_words.rearrange("p (j v) -> p j v", v=2), in_=pairs[:].rearrange("p (v j) -> p j v", v=2)
             )
 
-        weave_tile(nc.scalar.copy, 0)
-        weave_tile(nc.vector.tensor_copy, 1)
+        weave(nc.scalar.copy, q_woven[0][:, 0:P, :], raw[0])
+        weave(nc.vector.tensor_copy, q_woven[0][:, P:QUARTER, :], raw[1])
         clear(1, 2 * BANK, 3 * BANK)
         first_tier(0)
         clear(1, 3 * BANK, T)
@@ -312,8 +302,7 @@ def tile_list_embg_tgq4_res_kernel(tc, dy, w_words, w_scales, res, wgo, offs, ou
         clear(2, 0, T)
         read_back(0)
         read_back(1)
-        weave_tile(nc.scalar.copy, 2)
-        weave_tile(nc.scalar.copy, 3)
+        weave(nc.scalar.copy, q_woven[1][:], raw_quarter[1][:])
         first_tier(1)
         pages[3] = placed_tile(head, [P, T], F32, "page3", page_at[3])
         nc.gpsimd.memset(pages[3][:].bitcast(I32), 0)
@@ -321,12 +310,11 @@ def tile_list_embg_tgq4_res_kernel(tc, dy, w_words, w_scales, res, wgo, offs, ou
         read_back(3)
         open_sum(0)
         open_sum(1)
-        weave(nc.scalar.copy, q_woven[2][:], third[:])
+        weave(nc.scalar.copy, q_woven[2][:], raw_quarter[2][:])
         subtract(0)
         subtract(1)
-        weave(nc.scalar.copy, q_woven[3][:], fourth[:])
+        weave(nc.scalar.copy, q_woven[3][:], raw_quarter[3][:])
         second_tier(0)
-        second_tier(1)
         close_sum(0)
         close_sum(1)
         open_sum(2)
@@ -334,6 +322,7 @@ def tile_list_embg_tgq4_res_kernel(tc, dy, w_words, w_scales, res, wgo, offs, ou
         open_difference(4)
         open_difference(5)
         first_tier(2)
+        second_tier(1)
         first_tier(3)
         pieces = [slice(0, QUARTER), slice(QUARTER, BANK)]
         total = total_tile(0)

@@ -28,15 +28,21 @@ PAD_WORDS = MX_ALIGN // 4
 PAGE_BYTES = 4 * T
 WOVEN_BYTES = 2 * PACK * QUARTER
 
-UNITS = (
-    [((i, j0), (i + 1, j0)) for j0 in (0, QUARTER) for i in (0, 2)]
-    + [((0, j0), (1, j0)) for j0 in (BANK, BANK + QUARTER)]
-    + [((i, BANK), (i, BANK + QUARTER)) for i in (2, 3)]
-)
+BATCHES = {
+    "ab0": ((0, 0), (1, 0)),
+    "cd0": ((2, 0), (3, 0)),
+    "ab1": ((0, 1), (1, 1)),
+    "cd1": ((2, 1), (3, 1)),
+    "ab2": ((0, 2), (1, 2)),
+    "c2": ((2, 2),),
+    "ab3": ((0, 3), (1, 3)),
+    "c3": ((2, 3),),
+    "d23": ((3, 2), (3, 3)),
+}
+DX_BANKS = {"ab0": 4, "cd0": 5, "ab1": 6, "cd1": 7, "ab2": 1, "c2": 5, "ab3": 2, "c3": 3, "d23": 1}
 BACK_BANKS = (0, 1, 2, 3, 2, 3, 2, 3)
 DIFFERENCE_BANKS = {4: 0, 5: 1, 6: 0, 7: 1}
 PAIRS_BANKS = {2: 4, 3: 5}
-DX_BANKS = (4, 5, 6, 7, 5, 0, 1, 5)
 
 
 def tile_list_embg_tgq4_res_kernel(tc, dy, w_words, w_scales, res, wgo, offs, out):
@@ -45,11 +51,10 @@ def tile_list_embg_tgq4_res_kernel(tc, dy, w_words, w_scales, res, wgo, offs, ou
         keep = ctx.enter_context(tc.tile_pool(name="keep", bufs=1))
         early = ctx.enter_context(tc.tile_pool(name="early", bufs=1))
         head = ctx.enter_context(tc.tile_pool(name="head", bufs=1))
-        late = ctx.enter_context(tc.tile_pool(name="late", bufs=1))
         psum = ctx.enter_context(tc.psum_pool(name="psum", bufs=1))
 
-        def own_tile(shape, dtype, name):
-            return keep.tile(shape, dtype, name=name, align_bytes=MX_ALIGN)
+        def own_tile(shape, dtype, name, tag=None):
+            return keep.tile(shape, dtype, name=name, tag=tag or name, align_bytes=MX_ALIGN)
 
         def placed_tile(pool, shape, dtype, name, offset):
             return pool.tile(shape, dtype, name=name, offset=offset, align_bytes=MX_ALIGN)
@@ -57,39 +62,30 @@ def tile_list_embg_tgq4_res_kernel(tc, dy, w_words, w_scales, res, wgo, offs, ou
         def bank(b, name):
             return psum.tile([P, BANK], F32, name=name, tag=f"bank{b}")
 
-        def one_row_tile(u):
-            return UNITS[u][0][0] == UNITS[u][1][0]
-
         diagonal_at = PAGE_BYTES - 2 * P
         q_woven_at = (PAGE_BYTES - WOVEN_BYTES // 2, PAGE_BYTES + WOVEN_BYTES, PAGE_BYTES)
         eye_woven_at = q_woven_at[0] + WOVEN_BYTES - MX_ALIGN
         page_at = {2: 0, 3: q_woven_at[1]}
-        step = WOVEN_BYTES // 8
-        total_at = [step * 7 * max(u - 1, 0) for u in range(4)] + [step * 20] * 4
-        turned_at = {2 * h + 1: total_at[h] + step for h in (2, 3)}
-        r_woven_at = {h: total_at[h + 1] + 7 * step for h in (2, 3)}
 
         offsets = keep.tile([P, J // GROUP], U16, name="offsets")
         w_codes = own_tile([P, 2 * N], U8, "w_codes")
         w_scale = own_tile([P, N], U8, "w_scale")
         weights = [keep.tile([P, BANK], F32, name=f"weights{c}") for c in range(2)]
-        residual = [keep.tile([P, BANK], F32, name=f"residual{u}") for u in range(len(UNITS))]
         dy_rows = dy.rearrange("(p t) j -> p t j", t=PACK)
-        raw_quarter = [
-            keep.tile([P, PACK, QUARTER], F32, name=f"raw{h}", tag=f"raw{h}", align_bytes=MX_ALIGN)
-            for h in range(J // QUARTER)
-        ]
+        raw_quarter = [own_tile([P, PACK, QUARTER], F32, f"raw{h}") for h in range(J // QUARTER)]
         raw = [raw_quarter[b // 2][:, :, b % 2 * P : (b % 2 + 1) * P] for b in range(J // P)]
+        residual = {}
 
         def load_dy(h):
             nc.sync.dma_start(out=raw_quarter[h][:], in_=dy_rows[:, :, h * QUARTER : (h + 1) * QUARTER])
 
-        def load_residual(u):
-            i, j0 = UNITS[u][0]
-            row_tiles = 1 if one_row_tile(u) else 2
+        def load_residual(first, second):
+            (i, h), (i2, h2) = first, second
+            tile = keep.tile([P, BANK], F32, name=f"residual{i}{h}")
+            residual[first], residual[second] = (tile, 0), (tile, QUARTER)
             nc.sync.dma_start(
-                out=residual[u][:].rearrange("p (i j) -> p i j", i=row_tiles),
-                in_=res[i * P : (i + row_tiles) * P, j0 : j0 + BANK // row_tiles].rearrange("(i p) j -> p i j", p=P),
+                out=tile[:].rearrange("p (i j) -> p i j", i=i2 - i + 1),
+                in_=res[i * P : (i2 + 1) * P, h * QUARTER : (h2 + 1) * QUARTER].rearrange("(i p) j -> p i j", p=P),
             )
 
         def load_weights(c):
@@ -113,14 +109,16 @@ def tile_list_embg_tgq4_res_kernel(tc, dy, w_words, w_scales, res, wgo, offs, ou
             )
         load_dy(2)
         load_dy(3)
-        load_residual(0)
+        load_residual(*BATCHES["ab0"])
         load_weights(0)
         nc.sync.dma_start(offsets[:], offs)
-        for u in range(1, len(UNITS) // 2):
-            load_residual(u)
+        for name in ("cd0", "ab1", "cd1"):
+            load_residual(*BATCHES[name])
         load_weights(1)
-        for u in range(len(UNITS) // 2, len(UNITS)):
-            load_residual(u)
+        load_residual(*BATCHES["ab2"])
+        load_residual(BATCHES["c2"][0], BATCHES["c3"][0])
+        load_residual(*BATCHES["ab3"])
+        load_residual(*BATCHES["d23"])
 
         ones = eye_woven[:, 2 : 2 + 2 * (K + 1)].rearrange("p (a c) -> p a c", a=2)[:, :, 0:K:PACK]
         nc.vector.tensor_scalar(
@@ -153,6 +151,8 @@ def tile_list_embg_tgq4_res_kernel(tc, dy, w_words, w_scales, res, wgo, offs, ou
         difference = {}
         turned = {}
         dx = {}
+        sums = {}
+        total = {}
         scaled = {}
 
         def weave(copy, woven, rows):
@@ -170,12 +170,8 @@ def tile_list_embg_tgq4_res_kernel(tc, dy, w_words, w_scales, res, wgo, offs, ou
         def first_tier(h):
             quantize(q_operand, q_woven[h], h, E5M2, own_tile([P, QUARTER], U32, f"q_codes{h}"), f"q_scale{h}")
 
-        def second_tier(h):
-            if h in r_woven_at:
-                codes = placed_tile(late, [P, QUARTER], U32, f"r_codes{h}", turned_at[2 * h + 1])
-            else:
-                codes = own_tile([P, QUARTER], U32, f"r_codes{h}")
-            quantize(r_operand, r_woven[h], h, E4M3, codes, f"r_scale{h}")
+        def second_tier(h, tag=None):
+            quantize(r_operand, r_woven[h], h, E4M3, own_tile([P, QUARTER], U32, f"r_codes{h}", tag), f"r_scale{h}")
 
         def read_back(b):
             back[b] = bank(BACK_BANKS[b], f"back{b}")
@@ -201,11 +197,11 @@ def tile_list_embg_tgq4_res_kernel(tc, dy, w_words, w_scales, res, wgo, offs, ou
                     op=ALU.subtract,
                 )
 
-        def product(u, n, operand, fmt, start, stop):
-            i, j0 = UNITS[u][n]
-            codes, scale = operand[j0]
+        def product(name, n, operand, fmt, start, stop):
+            i, h = BATCHES[name][n]
+            codes, scale = operand[h * QUARTER]
             nc.tensor.matmul_mx(
-                out=dx[u][:, n * QUARTER : (n + 1) * QUARTER],
+                out=columns(dx, [(i, h)]),
                 lhsT=w_codes[:, 2 * P * i : 2 * P * (i + 1)].bitcast(E2M1),
                 lhsT_scale=w_scale[:, P * i : P * (i + 1)],
                 rhs=codes.bitcast(fmt),
@@ -214,48 +210,63 @@ def tile_list_embg_tgq4_res_kernel(tc, dy, w_words, w_scales, res, wgo, offs, ou
                 stop=stop,
             )
 
-        def open_sum(u):
-            dx[u] = bank(DX_BANKS[u], f"dx{u}")
-            for n in range(2):
-                product(u, n, q_operand, E5M2, n == 0, False)
+        def columns(table, pieces):
+            tile, at = table[pieces[0]]
+            return tile[:, at : at + len(pieces) * QUARTER]
 
-        def close_sum(u):
-            for n in range(2):
-                product(u, n, r_operand, E4M3, False, n == 1)
+        def assign(table, pieces, tile):
+            for n, piece in enumerate(pieces):
+                table[piece] = (tile, n * QUARTER)
 
-        def total_tile(u):
-            return placed_tile(late, [P, BANK], F32, f"total{u}", total_at[u])
+        def fresh(table, pieces, name, tag=None):
+            i, h = pieces[0]
+            assign(table, pieces, own_tile([P, len(pieces) * QUARTER], F32, f"{name}{i}{h}", tag))
 
-        def empty_bank(u):
-            sums = keep.tile([P, BANK], F32, name=f"sums{u}")
-            nc.scalar.copy(out=sums[:], in_=dx[u][:])
-            return sums
+        def open_sum(name):
+            assign(dx, BATCHES[name], bank(DX_BANKS[name], f"dx_{name}"))
+            for n in range(len(BATCHES[name])):
+                product(name, n, q_operand, E5M2, n == 0, False)
 
-        def finish(u, sums):
-            total = total_tile(u)
-            scaled[u] = keep.tile([P, BANK], F32, name=f"scaled{u}")
-            c, j0 = divmod(UNITS[u][0][1], BANK)
-            nc.gpsimd.tensor_tensor(out=total[:], in0=sums[:], in1=residual[u][:], op=ALU.add)
-            if one_row_tile(u):
-                nc.gpsimd.tensor_tensor(out=scaled[u][:], in0=total[:], in1=weights[c][:], op=ALU.mult)
-            else:
-                nc.gpsimd.tensor_tensor(
-                    out=scaled[u][:].rearrange("p (i j) -> p i j", i=2),
-                    in0=total[:].rearrange("p (i j) -> p i j", i=2),
-                    in1=weights[c][:, j0 : j0 + QUARTER].unsqueeze(1).to_broadcast([P, 2, QUARTER]),
-                    op=ALU.mult,
-                )
+        def close_sum(name):
+            for n in range(len(BATCHES[name])):
+                product(name, n, r_operand, E4M3, False, n == len(BATCHES[name]) - 1)
 
-        def place(u):
-            width = BANK if one_row_tile(u) else QUARTER
-            for n in range(BANK // width):
-                i, j0 = UNITS[u][n]
-                nc.vector.tensor_copy(
-                    out=pages[i][:].indirect(offsets[:, j0 // GROUP : (j0 + width) // GROUP]),
-                    in_=scaled[u][:, n * width : (n + 1) * width],
-                )
-                if j0 + width == J:
-                    nc.sync.dma_start(out=out[i * P : (i + 1) * P, :], in_=pages[i][:])
+        def empty(pieces, tag=None):
+            fresh(sums, pieces, "sums", tag)
+            nc.scalar.copy(out=columns(sums, pieces), in_=columns(dx, pieces))
+
+        def add(pieces, tag):
+            fresh(total, pieces, "total", tag)
+            nc.gpsimd.tensor_tensor(
+                out=columns(total, pieces), in0=columns(sums, pieces), in1=columns(residual, pieces), op=ALU.add
+            )
+
+        def weight_columns(h, count=1):
+            c, j0 = divmod(h * QUARTER, BANK)
+            return weights[c][:, j0 : j0 + count * QUARTER]
+
+        def multiply(pieces):
+            if pieces[0] not in scaled:
+                fresh(scaled, pieces, "scaled")
+            shape = [P, len(pieces), QUARTER]
+            nc.gpsimd.tensor_tensor(
+                out=columns(scaled, pieces).rearrange("p (i j) -> p i j", i=len(pieces)),
+                in0=columns(total, pieces).rearrange("p (i j) -> p i j", i=len(pieces)),
+                in1=weight_columns(pieces[0][1]).unsqueeze(1).to_broadcast(shape),
+                op=ALU.mult,
+            )
+
+        def window(i, h, count=1):
+            return pages[i][:].indirect(offsets[:, h * QUARTER // GROUP : (h + count) * QUARTER // GROUP])
+
+        def store(i):
+            nc.sync.dma_start(out=out[i * P : (i + 1) * P, :], in_=pages[i][:])
+
+        def place(pieces):
+            for i, h in pieces:
+                nc.vector.tensor_copy(out=window(i, h), in_=columns(scaled, [(i, h)]))
+                if (h + 1) * QUARTER == J:
+                    store(i)
 
         def add_transposed(b, t, rows, start, stop):
             nc.tensor.matmul(
@@ -274,10 +285,7 @@ def tile_list_embg_tgq4_res_kernel(tc, dy, w_words, w_scales, res, wgo, offs, ou
         def close_difference(b):
             for t in range(PACK):
                 add_transposed(b, t, minus[b][:, t * P : (t + 1) * P], False, t == PACK - 1)
-            if b in turned_at:
-                turned[b] = placed_tile(late, [P, 2, P, 2], BF16, f"turned{b}", turned_at[b])
-            else:
-                turned[b] = keep.tile([P, 2, P, 2], BF16, name=f"turned{b}")
+            turned[b] = own_tile([P, 2, P, 2], BF16, f"turned{b}")
             nc.scalar.copy(out=turned[b][:], in_=difference[b][:].rearrange("j (v e p) -> j v p e", v=2, e=2))
 
         def turn_back(h):
@@ -287,7 +295,7 @@ def tile_list_embg_tgq4_res_kernel(tc, dy, w_words, w_scales, res, wgo, offs, ou
                 for v in range(2):
                     at = v * QUARTER + b * P
                     nc.tensor.transpose(pairs[:, at : at + P], words[:, v * P : (v + 1) * P], eye[:])
-            r_woven[h] = placed_tile(late, quarter_shape, BF16, f"r_woven{h}", r_woven_at[h])
+            r_woven[h] = own_tile(quarter_shape, BF16, f"r_woven{h}")
             woven_words = r_woven[h][:].rearrange("p j t -> p (j t)").bitcast(F32)
             nc.scalar.copy(
                 out=woven_words.rearrange("p (j v) -> p j v", v=2), in_=pairs[:].rearrange("p (v j) -> p j v", v=2)
@@ -308,67 +316,90 @@ def tile_list_embg_tgq4_res_kernel(tc, dy, w_words, w_scales, res, wgo, offs, ou
         nc.gpsimd.memset(pages[3][:].bitcast(I32), 0)
         read_back(2)
         read_back(3)
-        open_sum(0)
-        open_sum(1)
+        open_sum("ab0")
+        open_sum("cd0")
         weave(nc.scalar.copy, q_woven[2][:], raw_quarter[2][:])
         subtract(0)
         subtract(1)
         weave(nc.scalar.copy, q_woven[3][:], raw_quarter[3][:])
         second_tier(0)
-        close_sum(0)
-        close_sum(1)
-        open_sum(2)
-        open_sum(3)
+        close_sum("ab0")
+        close_sum("cd0")
+        open_sum("ab1")
+        open_sum("cd1")
         open_difference(4)
         open_difference(5)
         first_tier(2)
         second_tier(1)
         first_tier(3)
-        pieces = [slice(0, QUARTER), slice(QUARTER, BANK)]
-        total = total_tile(0)
-        for cols in pieces:
-            nc.vector.tensor_tensor(out=total[:, cols], in0=dx[0][:, cols], in1=residual[0][:, cols], op=ALU.add)
-        scaled[0] = keep.tile([P, BANK], F32, name="scaled0")
-        for cols in pieces:
-            nc.vector.tensor_tensor(out=scaled[0][:, cols], in0=total[:, cols], in1=weights[0][:, 0:QUARTER], op=ALU.mult)
-        place(0)
-        finish(1, empty_bank(1))
+        ab0, cd0, ab1, cd1, ab2, c2, ab3, c3, d23 = BATCHES.values()
+        fresh(total, ab0, "total", "totals")
+        for piece in ab0:
+            nc.vector.tensor_tensor(
+                out=columns(total, [piece]), in0=columns(dx, [piece]), in1=columns(residual, [piece]), op=ALU.add
+            )
+        fresh(scaled, ab0, "scaled")
+        for piece in ab0:
+            nc.vector.tensor_tensor(
+                out=columns(scaled, [piece]), in0=columns(total, [piece]), in1=weight_columns(0), op=ALU.mult
+            )
+        place(ab0)
+        empty(cd0)
+        add(cd0, "totals")
+        multiply(cd0)
+        place(cd0)
 
         read_back(4)
         read_back(5)
+        close_sum("ab1")
+        close_sum("cd1")
         negate(4)
         negate(5)
+        empty(ab1[:1])
+        add(ab1[:1], "totals")
+        multiply(ab1[:1])
+        place(ab1[:1])
         close_difference(4)
         close_difference(5)
-        close_sum(2)
-        sums2 = empty_bank(2)
+        empty(cd1)
+        add(cd1, "totals")
         turn_back(2)
+        empty(ab1[1:], "turned5")
+        add(ab1[1:], "total_b1")
+        multiply(ab1[1:])
+        second_tier(2, "total_b1")
+        place(ab1[1:])
+        fresh(scaled, cd1, "scaled", "r_woven2")
+        for piece in cd1:
+            multiply([piece])
+            place([piece])
+
         read_back(6)
         read_back(7)
-        close_sum(3)
-        sums3 = empty_bank(3)
-        place(1)
-
         negate(6)
         open_difference(6)
         negate(7)
         open_difference(7)
-        finish(2, sums2)
-        second_tier(2)
-        place(2)
         close_difference(6)
         close_difference(7)
         turn_back(3)
-        finish(3, sums3)
-        open_sum(4)
-        close_sum(4)
-        sums4 = empty_bank(4)
-        second_tier(3)
-        place(3)
-        finish(4, sums4)
-        place(4)
-        for u in range(5, len(UNITS)):
-            open_sum(u)
-            close_sum(u)
-            finish(u, empty_bank(u))
-            place(u)
+        open_sum("ab2")
+        close_sum("ab2")
+        empty(ab2, "turned7")
+        add(ab2, "totals")
+        multiply(ab2)
+        second_tier(3, "totals")
+        place(ab2)
+        for name in ("c2", "ab3", "c3"):
+            open_sum(name)
+            close_sum(name)
+            empty(BATCHES[name])
+            add(BATCHES[name], "r_woven3")
+            multiply(BATCHES[name])
+            place(BATCHES[name])
+        open_sum("d23")
+        close_sum("d23")
+        empty(d23)
+        add(d23, "r_woven3")
+        nc.vector.tensor_tensor(out=window(3, 2, 2), in0=columns(total, d23), in1=weight_columns(2, 2), op=ALU.mult)
+        store(3)

@@ -23,6 +23,8 @@ GROUP = 16
 QUADRANTS = 4
 BANK = 512
 QUARTER = 256
+SPAN = 64
+SCALAR_SHARE = 160
 MX_ALIGN = 64
 PAD_WORDS = MX_ALIGN // 4
 PAGE_BYTES = 4 * T
@@ -30,19 +32,20 @@ WOVEN_BYTES = 2 * PACK * QUARTER
 
 BATCHES = {
     "ab0": ((0, 0), (1, 0)),
-    "cd0": ((2, 0), (3, 0)),
+    "c0": ((2, 0),),
     "ab1": ((0, 1), (1, 1)),
-    "cd1": ((2, 1), (3, 1)),
+    "c1": ((2, 1),),
     "ab2": ((0, 2), (1, 2)),
     "c2": ((2, 2),),
-    "ab3": ((0, 3), (1, 3)),
-    "c3": ((2, 3),),
+    "a3": ((0, 3),),
+    "bc3": ((1, 3), (2, 3)),
+    "d01": ((3, 0), (3, 1)),
     "d23": ((3, 2), (3, 3)),
 }
-DX_BANKS = {"ab0": 4, "cd0": 5, "ab1": 6, "cd1": 7, "ab2": 1, "c2": 5, "ab3": 2, "c3": 3, "d23": 1}
-BACK_BANKS = (0, 1, 2, 3, 2, 3, 2, 3)
-DIFFERENCE_BANKS = {4: 0, 5: 1, 6: 0, 7: 1}
-PAIRS_BANKS = {2: 4, 3: 5}
+DX_BANKS = {"ab0": 0, "c0": 1, "ab1": 6, "c1": 7, "ab2": 4, "c2": 1, "a3": 3, "bc3": 2, "d01": 4, "d23": 5}
+BACK_BANKS = (0, 1, 2, 3, 4, 5, 2, 3)
+DIFFERENCE_BANKS = {4: 2, 5: 3, 6: 4, 7: 5}
+PAIRS_BANKS = {4: 0, 5: 1, 6: 0, 7: 1}
 
 
 def tile_list_embg_tgq4_res_kernel(tc, dy, w_words, w_scales, res, wgo, offs, out):
@@ -62,41 +65,46 @@ def tile_list_embg_tgq4_res_kernel(tc, dy, w_words, w_scales, res, wgo, offs, ou
         def bank(b, name):
             return psum.tile([P, BANK], F32, name=name, tag=f"bank{b}")
 
-        diagonal_at = PAGE_BYTES - 2 * P
-        q_woven_at = (PAGE_BYTES - WOVEN_BYTES // 2, PAGE_BYTES + WOVEN_BYTES, PAGE_BYTES)
-        eye_woven_at = q_woven_at[0] + WOVEN_BYTES - MX_ALIGN
-        page_at = {2: 0, 3: q_woven_at[1]}
+        diagonal_at = PAGE_BYTES - 2 * SPAN
+        eye_woven_at = WOVEN_BYTES - MX_ALIGN
+        eye_at = WOVEN_BYTES
+        q_woven_at = (0, eye_woven_at + 2 * K - MX_ALIGN, 0)
 
         offsets = keep.tile([P, J // GROUP], U16, name="offsets")
         w_codes = own_tile([P, 2 * N], U8, "w_codes")
         w_scale = own_tile([P, N], U8, "w_scale")
-        weights = [keep.tile([P, BANK], F32, name=f"weights{c}") for c in range(2)]
+        weights = keep.tile([P, J], F32, name="weights")
         dy_rows = dy.rearrange("(p t) j -> p t j", t=PACK)
         raw_quarter = [own_tile([P, PACK, QUARTER], F32, f"raw{h}") for h in range(J // QUARTER)]
         raw = [raw_quarter[b // 2][:, :, b % 2 * P : (b % 2 + 1) * P] for b in range(J // P)]
-        residual = {}
+        early_rows = keep.tile([P, 3 * J], F32, name="early_rows")
+        last_rows = keep.tile([P, J], F32, name="last_rows")
+        residual = {
+            (i, h): (early_rows, (3 * h + i) * QUARTER) if i < 3 else (last_rows, h * QUARTER)
+            for i in range(4)
+            for h in range(4)
+        }
 
         def load_dy(h):
             nc.sync.dma_start(out=raw_quarter[h][:], in_=dy_rows[:, :, h * QUARTER : (h + 1) * QUARTER])
 
-        def load_residual(first, second):
-            (i, h), (i2, h2) = first, second
-            tile = keep.tile([P, BANK], F32, name=f"residual{i}{h}")
-            residual[first], residual[second] = (tile, 0), (tile, QUARTER)
+        def load_residual(first, last, h):
+            tile, at = residual[first, h]
             nc.sync.dma_start(
-                out=tile[:].rearrange("p (i j) -> p i j", i=i2 - i + 1),
-                in_=res[i * P : (i2 + 1) * P, h * QUARTER : (h2 + 1) * QUARTER].rearrange("(i p) j -> p i j", p=P),
+                out=tile[:, at : at + (last - first) * QUARTER].rearrange("p (i j) -> p i j", j=QUARTER),
+                in_=res[first * P : last * P, h * QUARTER : (h + 1) * QUARTER].rearrange("(i p) j -> p i j", p=P),
             )
 
         def load_weights(c):
-            nc.sync.dma_start(out=weights[c][:], in_=wgo[:, c * BANK : (c + 1) * BANK])
+            nc.sync.dma_start(out=weights[:, c * BANK : (c + 1) * BANK], in_=wgo[:, c * BANK : (c + 1) * BANK])
 
-        diagonal = placed_tile(early, [P, P], I32, "diagonal", diagonal_at)
-        nc.gpsimd.iota(diagonal[:], pattern=[[1, P]], base=0, channel_multiplier=-1)
-        eye_woven = placed_tile(head, [P, 2 * K + MX_ALIGN // 2], BF16, "eye_woven", eye_woven_at)
+        diagonal = placed_tile(early, [P, SPAN], I32, "diagonal", diagonal_at)
+        nc.gpsimd.iota(diagonal[:], pattern=[[1, SPAN]], base=0, channel_multiplier=-1)
+        eye_woven = [own_tile([P, K], BF16, "eye_woven0"), placed_tile(head, [P, K], BF16, "eye_woven1", eye_woven_at)]
         eye_words = own_tile([P, 2 * QUARTER + PAD_WORDS], U32, "eye_words")
         eye_scale = own_tile([P, QUARTER], U8, "eye_scale")
-        nc.vector.memset(eye_woven[:, 0 : 2 * K].bitcast(I32), 0)
+        for part in eye_woven:
+            nc.vector.memset(part[:].bitcast(I32), 0)
         nc.vector.memset(w_scale[:].bitcast(I32), 0)
         nc.vector.memset(eye_words[:, QUARTER : QUARTER + PAD_WORDS].bitcast(I32), 0)
 
@@ -109,24 +117,30 @@ def tile_list_embg_tgq4_res_kernel(tc, dy, w_words, w_scales, res, wgo, offs, ou
             )
         load_dy(2)
         load_dy(3)
-        load_residual(*BATCHES["ab0"])
+        load_residual(0, 2, 0)
         load_weights(0)
         nc.sync.dma_start(offsets[:], offs)
-        for name in ("cd0", "ab1", "cd1"):
-            load_residual(*BATCHES[name])
+        load_residual(2, 3, 0)
+        load_residual(0, 3, 1)
         load_weights(1)
-        load_residual(*BATCHES["ab2"])
-        load_residual(BATCHES["c2"][0], BATCHES["c3"][0])
-        load_residual(*BATCHES["ab3"])
-        load_residual(*BATCHES["d23"])
+        load_residual(0, 3, 2)
+        load_residual(0, 3, 3)
+        for c in range(2):
+            cols = slice(c * BANK, (c + 1) * BANK)
+            nc.sync.dma_start(out=last_rows[:, cols], in_=res[3 * P : 4 * P, cols])
 
-        ones = eye_woven[:, 2 : 2 + 2 * (K + 1)].rearrange("p (a c) -> p a c", a=2)[:, :, 0:K:PACK]
-        nc.vector.tensor_scalar(
-            out=ones, in0=diagonal[:].unsqueeze(1).to_broadcast([P, 2, P]), scalar1=0.0, scalar2=None, op0=ALU.is_equal
-        )
-        eye = keep.tile([P, P], F32, name="eye")
-        nc.vector.tensor_scalar(out=eye[:], in0=diagonal[:], scalar1=0.0, scalar2=None, op0=ALU.is_equal)
-        nc.vector.quantize_mx(out=eye_words[:, 0:QUARTER].bitcast(E4M3), scales=eye_scale[:], in_=eye_woven[:, 0 : 2 * K])
+        for a in range(2):
+            for c0 in range(0, P, SPAN):
+                nc.vector.tensor_scalar(
+                    out=eye_woven[a][:, PACK * c0 + 2 + a : PACK * (c0 + SPAN) : PACK],
+                    in0=diagonal[:],
+                    scalar1=float(-c0),
+                    scalar2=None,
+                    op0=ALU.is_equal,
+                )
+        for a in range(2):
+            cols = slice(a * P, (a + 1) * P)
+            nc.vector.quantize_mx(out=eye_words[:, cols].bitcast(E4M3), scales=eye_scale[:, cols], in_=eye_woven[a][:])
         pages = {i: placed_tile(early, [P, T], F32, f"page{i}", i * PAGE_BYTES) for i in range(2)}
 
         def clear(i, first, last):
@@ -161,14 +175,19 @@ def tile_list_embg_tgq4_res_kernel(tc, dy, w_words, w_scales, res, wgo, offs, ou
                 in_=rows.rearrange("p t (g i) -> p g t i", i=PACK),
             )
 
-        def quantize(operand, woven, h, fmt, codes, name):
+        def quantize(operand, woven, h, fmt, codes, name, calls=1):
             scale = own_tile([P, QUARTER], U8, name)
-            nc.vector.quantize_mx(out=codes[:].bitcast(fmt), scales=scale[:], in_=woven[:].rearrange("p j t -> p (j t)"))
+            width = QUARTER // calls
+            for j in range(0, QUARTER, width):
+                cols = slice(j, j + width)
+                nc.vector.quantize_mx(
+                    out=codes[:, cols].bitcast(fmt), scales=scale[:, cols], in_=woven[:, cols, :].rearrange("p j t -> p (j t)")
+                )
             for j in (0, P):
                 operand[h * QUARTER + j] = (codes[:, j:QUARTER], scale[:, j:QUARTER])
 
-        def first_tier(h):
-            quantize(q_operand, q_woven[h], h, E5M2, own_tile([P, QUARTER], U32, f"q_codes{h}"), f"q_scale{h}")
+        def first_tier(h, calls=1):
+            quantize(q_operand, q_woven[h], h, E5M2, own_tile([P, QUARTER], U32, f"q_codes{h}"), f"q_scale{h}", calls)
 
         def second_tier(h, tag=None):
             quantize(r_operand, r_woven[h], h, E4M3, own_tile([P, QUARTER], U32, f"r_codes{h}", tag), f"r_scale{h}")
@@ -242,12 +261,10 @@ def tile_list_embg_tgq4_res_kernel(tc, dy, w_words, w_scales, res, wgo, offs, ou
             )
 
         def weight_columns(h, count=1):
-            c, j0 = divmod(h * QUARTER, BANK)
-            return weights[c][:, j0 : j0 + count * QUARTER]
+            return weights[:, h * QUARTER : (h + count) * QUARTER]
 
-        def multiply(pieces):
-            if pieces[0] not in scaled:
-                fresh(scaled, pieces, "scaled")
+        def multiply(pieces, tag=None):
+            fresh(scaled, pieces, "scaled", tag)
             shape = [P, len(pieces), QUARTER]
             nc.gpsimd.tensor_tensor(
                 out=columns(scaled, pieces).rearrange("p (i j) -> p i j", i=len(pieces)),
@@ -288,51 +305,53 @@ def tile_list_embg_tgq4_res_kernel(tc, dy, w_words, w_scales, res, wgo, offs, ou
             turned[b] = own_tile([P, 2, P, 2], BF16, f"turned{b}")
             nc.scalar.copy(out=turned[b][:], in_=difference[b][:].rearrange("j (v e p) -> j v p e", v=2, e=2))
 
-        def turn_back(h):
-            pairs = bank(PAIRS_BANKS[h], f"pairs{h}")
-            for b in range(2):
-                words = turned[2 * h + b][:].rearrange("j v p e -> j (v p e)").bitcast(F32)
-                for v in range(2):
-                    at = v * QUARTER + b * P
-                    nc.tensor.transpose(pairs[:, at : at + P], words[:, v * P : (v + 1) * P], eye[:])
-            r_woven[h] = own_tile(quarter_shape, BF16, f"r_woven{h}")
-            woven_words = r_woven[h][:].rearrange("p j t -> p (j t)").bitcast(F32)
+        def turn_back(b):
+            pairs = bank(PAIRS_BANKS[b], f"pairs{b}")
+            words = turned[b][:].rearrange("j v p e -> j (v p e)").bitcast(F32)
+            for v in range(2):
+                nc.tensor.transpose(pairs[:, v * P : (v + 1) * P], words[:, v * P : (v + 1) * P], eye[:])
+            if b % 2 == 0:
+                r_woven[b // 2] = own_tile(quarter_shape, BF16, f"r_woven{b // 2}")
+            woven = r_woven[b // 2][:, b % 2 * P : (b % 2 + 1) * P, :]
             nc.scalar.copy(
-                out=woven_words.rearrange("p (j v) -> p j v", v=2), in_=pairs[:].rearrange("p (v j) -> p j v", v=2)
+                out=woven.rearrange("p j t -> p (j t)").bitcast(F32).rearrange("p (j v) -> p j v", v=2),
+                in_=pairs[:, 0 : 2 * P].rearrange("p (v j) -> p j v", v=2),
             )
 
-        weave(nc.scalar.copy, q_woven[0][:, 0:P, :], raw[0])
-        weave(nc.vector.tensor_copy, q_woven[0][:, P:QUARTER, :], raw[1])
+        for b in range(2):
+            weave(nc.vector.tensor_copy, q_woven[0][:, b * P : (b + 1) * P, :], raw[b])
+        first_tier(0, calls=2)
         clear(1, 2 * BANK, 3 * BANK)
-        first_tier(0)
-        clear(1, 3 * BANK, T)
-        pages[2] = placed_tile(head, [P, T], F32, "page2", page_at[2])
-        clear(2, 0, T)
         read_back(0)
         read_back(1)
-        weave(nc.scalar.copy, q_woven[1][:], raw_quarter[1][:])
+        weave(nc.scalar.copy, q_woven[1][:, 0:SCALAR_SHARE, :], raw_quarter[1][:, :, 0:SCALAR_SHARE])
+        eye = placed_tile(head, [P, P], F32, "eye", eye_at)
+        nc.scalar.copy(out=eye[:], in_=eye_woven[0][:, 2:K:PACK])
+        weave(nc.vector.tensor_copy, q_woven[1][:, SCALAR_SHARE:QUARTER, :], raw_quarter[1][:, :, SCALAR_SHARE:QUARTER])
+        clear(1, 3 * BANK, T)
         first_tier(1)
-        pages[3] = placed_tile(head, [P, T], F32, "page3", page_at[3])
-        nc.gpsimd.memset(pages[3][:].bitcast(I32), 0)
+        pages[2] = placed_tile(head, [P, T], F32, "page2", q_woven_at[1])
+        nc.gpsimd.memset(pages[2][:].bitcast(I32), 0)
+        pages[3] = pages[0]
         read_back(2)
         read_back(3)
-        open_sum("ab0")
-        open_sum("cd0")
         weave(nc.scalar.copy, q_woven[2][:], raw_quarter[2][:])
         subtract(0)
+        open_sum("ab0")
+        open_sum("c0")
         subtract(1)
         weave(nc.scalar.copy, q_woven[3][:], raw_quarter[3][:])
         second_tier(0)
         close_sum("ab0")
-        close_sum("cd0")
+        close_sum("c0")
         open_sum("ab1")
-        open_sum("cd1")
+        open_sum("c1")
         open_difference(4)
         open_difference(5)
         first_tier(2)
         second_tier(1)
         first_tier(3)
-        ab0, cd0, ab1, cd1, ab2, c2, ab3, c3, d23 = BATCHES.values()
+        ab0, c0, ab1, c1, ab2, c2, a3, bc3, d01, d23 = BATCHES.values()
         fresh(total, ab0, "total", "totals")
         for piece in ab0:
             nc.vector.tensor_tensor(
@@ -344,35 +363,30 @@ def tile_list_embg_tgq4_res_kernel(tc, dy, w_words, w_scales, res, wgo, offs, ou
                 out=columns(scaled, [piece]), in0=columns(total, [piece]), in1=weight_columns(0), op=ALU.mult
             )
         place(ab0)
-        empty(cd0)
-        add(cd0, "totals")
-        multiply(cd0)
-        place(cd0)
+        empty(c0)
+        add(c0, "totals")
+        multiply(c0)
+        place(c0)
 
         read_back(4)
         read_back(5)
         close_sum("ab1")
-        close_sum("cd1")
+        close_sum("c1")
         negate(4)
         negate(5)
-        empty(ab1[:1])
-        add(ab1[:1], "totals")
-        multiply(ab1[:1])
-        place(ab1[:1])
+        empty(ab1)
+        add(ab1, "totals")
         close_difference(4)
         close_difference(5)
-        empty(cd1)
-        add(cd1, "totals")
-        turn_back(2)
-        empty(ab1[1:], "turned5")
-        add(ab1[1:], "total_b1")
-        multiply(ab1[1:])
-        second_tier(2, "total_b1")
-        place(ab1[1:])
-        fresh(scaled, cd1, "scaled", "r_woven2")
-        for piece in cd1:
-            multiply([piece])
-            place([piece])
+        empty(c1)
+        turn_back(4)
+        turn_back(5)
+        multiply(ab1, "turned5")
+        second_tier(2, "totals")
+        place(ab1)
+        add(c1, "r_woven2")
+        multiply(c1)
+        place(c1)
 
         read_back(6)
         read_back(7)
@@ -382,24 +396,38 @@ def tile_list_embg_tgq4_res_kernel(tc, dy, w_words, w_scales, res, wgo, offs, ou
         open_difference(7)
         close_difference(6)
         close_difference(7)
-        turn_back(3)
         open_sum("ab2")
         close_sum("ab2")
-        empty(ab2, "turned7")
-        add(ab2, "totals")
-        multiply(ab2)
-        second_tier(3, "totals")
+        turn_back(6)
+        empty(ab2)
+        turn_back(7)
+        add(ab2, "r_woven2")
+        multiply(ab2, "turned7")
+        second_tier(3, "r_woven2")
         place(ab2)
-        for name in ("c2", "ab3", "c3"):
+        for name in ("c2", "a3"):
             open_sum(name)
             close_sum(name)
             empty(BATCHES[name])
-            add(BATCHES[name], "r_woven3")
-            multiply(BATCHES[name])
-            place(BATCHES[name])
-        open_sum("d23")
-        close_sum("d23")
-        empty(d23)
-        add(d23, "r_woven3")
-        nc.vector.tensor_tensor(out=window(3, 2, 2), in0=columns(total, d23), in1=weight_columns(2, 2), op=ALU.mult)
+        add(c2, "r_woven3")
+        add(a3, "total_a3")
+        multiply(a3)
+        place(a3)
+        multiply(c2, "total_a3")
+        place(c2)
+        open_sum("bc3")
+        close_sum("bc3")
+        empty(bc3)
+        add(bc3, "r_woven3")
+        for piece in bc3:
+            multiply([piece])
+            place([piece])
+        last = d01 + d23
+        fresh(sums, last, "sums")
+        for name in ("d01", "d23"):
+            open_sum(name)
+            close_sum(name)
+            nc.scalar.copy(out=columns(sums, BATCHES[name]), in_=columns(dx, BATCHES[name]))
+        add(last, "r_woven3")
+        nc.vector.tensor_tensor(out=window(3, 0, 4), in0=columns(total, last), in1=weights[:], op=ALU.mult)
         store(3)

@@ -24,7 +24,7 @@ QUADRANTS = 4
 BANK = 512
 QUARTER = 256
 SPAN = 64
-SCALAR_SHARE = 160
+SCALAR_SHARE = 128
 MX_ALIGN = 64
 PAD_WORDS = MX_ALIGN // 4
 PAGE_BYTES = 4 * T
@@ -42,7 +42,7 @@ BATCHES = {
     "d01": ((3, 0), (3, 1)),
     "d23": ((3, 2), (3, 3)),
 }
-DX_BANKS = {"ab0": 0, "c0": 1, "ab1": 6, "c1": 7, "ab2": 4, "c2": 1, "a3": 3, "bc3": 2, "d01": 4, "d23": 5}
+DX_BANKS = {"ab0": 0, "c0": 1, "ab1": 6, "c1": 5, "ab2": 6, "c2": 1, "a3": 3, "bc3": 2, "d01": 1, "d23": 5}
 BACK_BANKS = (0, 1, 2, 3, 4, 5, 2, 3)
 DIFFERENCE_BANKS = {4: 2, 5: 3, 6: 4, 7: 5}
 PAIRS_BANKS = {4: 0, 5: 1, 6: 0, 7: 1}
@@ -79,11 +79,14 @@ def tile_list_embg_tgq4_res_kernel(tc, dy, w_words, w_scales, res, wgo, offs, ou
         raw = [raw_quarter[b // 2][:, :, b % 2 * P : (b % 2 + 1) * P] for b in range(J // P)]
         early_rows = keep.tile([P, 3 * J], F32, name="early_rows")
         last_rows = keep.tile([P, J], F32, name="last_rows")
+        first_rows = own_tile([P, 3 * QUARTER], F32, "first_rows")
         residual = {
             (i, h): (early_rows, (3 * h + i) * QUARTER) if i < 3 else (last_rows, h * QUARTER)
             for i in range(4)
             for h in range(4)
         }
+        for i in range(3):
+            residual[i, 0] = (first_rows, i * QUARTER)
 
         def load_dy(h):
             nc.sync.dma_start(out=raw_quarter[h][:], in_=dy_rows[:, :, h * QUARTER : (h + 1) * QUARTER])
@@ -95,8 +98,8 @@ def tile_list_embg_tgq4_res_kernel(tc, dy, w_words, w_scales, res, wgo, offs, ou
                 in_=res[first * P : last * P, h * QUARTER : (h + 1) * QUARTER].rearrange("(i p) j -> p i j", p=P),
             )
 
-        def load_weights(c):
-            nc.sync.dma_start(out=weights[:, c * BANK : (c + 1) * BANK], in_=wgo[:, c * BANK : (c + 1) * BANK])
+        def load_weights(first, last):
+            nc.sync.dma_start(out=weights[:, first:last], in_=wgo[:, first:last])
 
         diagonal = placed_tile(early, [P, SPAN], I32, "diagonal", diagonal_at)
         nc.gpsimd.iota(diagonal[:], pattern=[[1, SPAN]], base=0, channel_multiplier=-1)
@@ -110,19 +113,18 @@ def tile_list_embg_tgq4_res_kernel(tc, dy, w_words, w_scales, res, wgo, offs, ou
 
         load_dy(0)
         load_dy(1)
+        load_dy(2)
         nc.sync.dma_start(out=w_codes[:].bitcast(I32), in_=w_words[0].bitcast(I32))
         for q in range(QUADRANTS):
             nc.sync.dma_start(
                 out=w_scale[32 * q : 32 * q + 4, :].bitcast(I32), in_=w_scales[0, 4 * q : 4 * q + 4, :].bitcast(I32)
             )
-        load_dy(2)
         load_dy(3)
-        load_residual(0, 2, 0)
-        load_weights(0)
+        load_residual(0, 3, 0)
+        load_weights(0, QUARTER)
         nc.sync.dma_start(offsets[:], offs)
-        load_residual(2, 3, 0)
         load_residual(0, 3, 1)
-        load_weights(1)
+        load_weights(QUARTER, J)
         load_residual(0, 3, 2)
         load_residual(0, 3, 3)
         for c in range(2):
@@ -186,8 +188,9 @@ def tile_list_embg_tgq4_res_kernel(tc, dy, w_words, w_scales, res, wgo, offs, ou
             for j in (0, P):
                 operand[h * QUARTER + j] = (codes[:, j:QUARTER], scale[:, j:QUARTER])
 
-        def first_tier(h, calls=1):
-            quantize(q_operand, q_woven[h], h, E5M2, own_tile([P, QUARTER], U32, f"q_codes{h}"), f"q_scale{h}", calls)
+        def first_tier(h, calls=1, tag=None):
+            codes = own_tile([P, QUARTER], U32, f"q_codes{h}", tag)
+            quantize(q_operand, q_woven[h], h, E5M2, codes, f"q_scale{h}", calls)
 
         def second_tier(h, tag=None):
             quantize(r_operand, r_woven[h], h, E4M3, own_tile([P, QUARTER], U32, f"r_codes{h}", tag), f"r_scale{h}")
@@ -296,7 +299,7 @@ def tile_list_embg_tgq4_res_kernel(tc, dy, w_words, w_scales, res, wgo, offs, ou
                 add_transposed(b, t, raw[b][:, t, :], t == 0, False)
 
         def negate(b):
-            minus[b] = keep.tile([P, BANK], F32, name=f"minus{b}")
+            minus[b] = own_tile([P, BANK], F32, f"minus{b}")
             nc.scalar.activation(out=minus[b][:], in_=back[b][:], func=COPY, scale=-1.0)
 
         def close_difference(b):
@@ -321,14 +324,13 @@ def tile_list_embg_tgq4_res_kernel(tc, dy, w_words, w_scales, res, wgo, offs, ou
         for b in range(2):
             weave(nc.vector.tensor_copy, q_woven[0][:, b * P : (b + 1) * P, :], raw[b])
         first_tier(0, calls=2)
-        clear(1, 2 * BANK, 3 * BANK)
         read_back(0)
         read_back(1)
         weave(nc.scalar.copy, q_woven[1][:, 0:SCALAR_SHARE, :], raw_quarter[1][:, :, 0:SCALAR_SHARE])
         eye = placed_tile(head, [P, P], F32, "eye", eye_at)
         nc.scalar.copy(out=eye[:], in_=eye_woven[0][:, 2:K:PACK])
         weave(nc.vector.tensor_copy, q_woven[1][:, SCALAR_SHARE:QUARTER, :], raw_quarter[1][:, :, SCALAR_SHARE:QUARTER])
-        clear(1, 3 * BANK, T)
+        clear(1, 2 * BANK, 3 * BANK)
         first_tier(1)
         pages[2] = placed_tile(head, [P, T], F32, "page2", q_woven_at[1])
         nc.gpsimd.memset(pages[2][:].bitcast(I32), 0)
@@ -345,47 +347,47 @@ def tile_list_embg_tgq4_res_kernel(tc, dy, w_words, w_scales, res, wgo, offs, ou
         close_sum("ab0")
         close_sum("c0")
         open_sum("ab1")
-        open_sum("c1")
         open_difference(4)
         open_difference(5)
         first_tier(2)
         second_tier(1)
-        first_tier(3)
+        clear(1, 3 * BANK, T)
         ab0, c0, ab1, c1, ab2, c2, a3, bc3, d01, d23 = BATCHES.values()
-        fresh(total, ab0, "total", "totals")
-        for piece in ab0:
+        fresh(total, ab0, "total")
+        fresh(total, c0, "total", "totals")
+        for piece in ab0 + c0:
             nc.vector.tensor_tensor(
                 out=columns(total, [piece]), in0=columns(dx, [piece]), in1=columns(residual, [piece]), op=ALU.add
             )
+        first_tier(3, tag="first_rows")
         fresh(scaled, ab0, "scaled")
         for piece in ab0:
             nc.vector.tensor_tensor(
                 out=columns(scaled, [piece]), in0=columns(total, [piece]), in1=weight_columns(0), op=ALU.mult
             )
         place(ab0)
-        empty(c0)
-        add(c0, "totals")
-        multiply(c0)
+        multiply(c0, "total00")
         place(c0)
 
         read_back(4)
         read_back(5)
         close_sum("ab1")
-        close_sum("c1")
         negate(4)
         negate(5)
         empty(ab1)
         add(ab1, "totals")
         close_difference(4)
         close_difference(5)
-        empty(c1)
+        open_sum("c1")
+        close_sum("c1")
         turn_back(4)
+        empty(c1)
+        add(c1, "sums01")
         turn_back(5)
         multiply(ab1, "turned5")
         second_tier(2, "totals")
         place(ab1)
-        add(c1, "r_woven2")
-        multiply(c1)
+        multiply(c1, "r_woven2")
         place(c1)
 
         read_back(6)
@@ -394,16 +396,16 @@ def tile_list_embg_tgq4_res_kernel(tc, dy, w_words, w_scales, res, wgo, offs, ou
         open_difference(6)
         negate(7)
         open_difference(7)
-        close_difference(6)
-        close_difference(7)
         open_sum("ab2")
+        close_difference(6)
         close_sum("ab2")
+        empty(ab2, "minus6")
+        close_difference(7)
         turn_back(6)
-        empty(ab2)
         turn_back(7)
-        add(ab2, "r_woven2")
+        add(ab2, "sums01")
         multiply(ab2, "turned7")
-        second_tier(3, "r_woven2")
+        second_tier(3, "sums01")
         place(ab2)
         for name in ("c2", "a3"):
             open_sum(name)

@@ -149,7 +149,7 @@ def tile_list_embg_tgq4_res_kernel(tc, dy, w_words, w_scales, res, wgo, offs, ou
             nc.vector.memset(pages[i][:, first:last].bitcast(I32), 0)
 
         clear(0, 0, T)
-        clear(1, 0, 2 * BANK)
+        clear(1, 0, BANK)
         moved_at = QUARTER + PAD_WORDS
         eye_halves = eye_words[:].bitcast(U16)
         nc.scalar.copy(out=eye_halves[:, 2 * moved_at : 2 * moved_at + K], in_=eye_halves[:, 1 : K + 1])
@@ -321,8 +321,9 @@ def tile_list_embg_tgq4_res_kernel(tc, dy, w_words, w_scales, res, wgo, offs, ou
                 in_=pairs[:, 0 : 2 * P].rearrange("p (v j) -> p j v", v=2),
             )
 
-        for b in range(2):
-            weave(nc.vector.tensor_copy, q_woven[0][:, b * P : (b + 1) * P, :], raw[b])
+        weave(nc.vector.tensor_copy, q_woven[0][:, 0:P, :], raw[0])
+        weave(nc.scalar.copy, q_woven[0][:, P:QUARTER, :], raw[1])
+        clear(1, BANK, 2 * BANK)
         first_tier(0, calls=2)
         read_back(0)
         read_back(1)

@@ -267,7 +267,8 @@ def tile_list_embg_tgq4_res_kernel(tc, dy, w_words, w_scales, res, wgo, offs, ou
             return weights[:, h * QUARTER : (h + count) * QUARTER]
 
         def multiply(pieces, tag=None):
-            fresh(scaled, pieces, "scaled", tag)
+            if pieces[0] not in scaled:
+                fresh(scaled, pieces, "scaled", tag)
             shape = [P, len(pieces), QUARTER]
             nc.gpsimd.tensor_tensor(
                 out=columns(scaled, pieces).rearrange("p (i j) -> p i j", i=len(pieces)),
@@ -354,21 +355,21 @@ def tile_list_embg_tgq4_res_kernel(tc, dy, w_words, w_scales, res, wgo, offs, ou
         second_tier(1)
         clear(1, 3 * BANK, T)
         ab0, c0, ab1, c1, ab2, c2, a3, bc3, d01, d23 = BATCHES.values()
-        fresh(total, ab0, "total")
-        fresh(total, c0, "total", "totals")
+        a0, bc0 = ab0[:1], ab0[1:] + c0
+        fresh(total, a0, "total")
+        fresh(total, bc0, "total", "totals")
         for piece in ab0 + c0:
             nc.vector.tensor_tensor(
                 out=columns(total, [piece]), in0=columns(dx, [piece]), in1=columns(residual, [piece]), op=ALU.add
             )
         first_tier(3, tag="first_rows")
-        fresh(scaled, ab0, "scaled")
-        for piece in ab0:
-            nc.vector.tensor_tensor(
-                out=columns(scaled, [piece]), in0=columns(total, [piece]), in1=weight_columns(0), op=ALU.mult
-            )
-        place(ab0)
-        multiply(c0, "total00")
-        place(c0)
+        fresh(scaled, a0, "scaled")
+        nc.vector.tensor_tensor(out=columns(scaled, a0), in0=columns(total, a0), in1=weight_columns(0), op=ALU.mult)
+        place(a0)
+        fresh(scaled, bc0, "scaled", "raw0")
+        for piece in bc0:
+            multiply([piece])
+            place([piece])
 
         read_back(4)
         read_back(5)
@@ -383,12 +384,12 @@ def tile_list_embg_tgq4_res_kernel(tc, dy, w_words, w_scales, res, wgo, offs, ou
         close_sum("c1")
         turn_back(4)
         empty(c1)
-        add(c1, "sums01")
         turn_back(5)
         multiply(ab1, "turned5")
         second_tier(2, "totals")
         place(ab1)
-        multiply(c1, "r_woven2")
+        add(c1, "r_woven2")
+        multiply(c1)
         place(c1)
 
         read_back(6)
@@ -404,9 +405,9 @@ def tile_list_embg_tgq4_res_kernel(tc, dy, w_words, w_scales, res, wgo, offs, ou
         close_difference(7)
         turn_back(6)
         turn_back(7)
-        add(ab2, "sums01")
+        add(ab2, "r_woven2")
         multiply(ab2, "turned7")
-        second_tier(3, "sums01")
+        second_tier(3, "r_woven2")
         place(ab2)
         for name in ("c2", "a3"):
             open_sum(name)

@@ -24,15 +24,14 @@ QUADRANTS = 4
 BANK = 512
 QUARTER = 256
 SPAN = 64
-SCALAR_SHARE = 128
 MX_ALIGN = 64
 PAD_WORDS = MX_ALIGN // 4
 PAGE_BYTES = 4 * T
 WOVEN_BYTES = 2 * PACK * QUARTER
 
 BATCHES = {
-    "ab0": ((0, 0), (1, 0)),
-    "c0": ((2, 0),),
+    "a0": ((0, 0),),
+    "bc0": ((1, 0), (2, 0)),
     "ab1": ((0, 1), (1, 1)),
     "c1": ((2, 1),),
     "ab2": ((0, 2), (1, 2)),
@@ -42,7 +41,7 @@ BATCHES = {
     "d01": ((3, 0), (3, 1)),
     "d23": ((3, 2), (3, 3)),
 }
-DX_BANKS = {"ab0": 0, "c0": 1, "ab1": 6, "c1": 5, "ab2": 6, "c2": 1, "a3": 3, "bc3": 2, "d01": 1, "d23": 5}
+DX_BANKS = {"a0": 0, "bc0": 1, "ab1": 6, "c1": 5, "ab2": 6, "c2": 1, "a3": 3, "bc3": 2, "d01": 1, "d23": 5}
 BACK_BANKS = (0, 1, 2, 3, 4, 5, 2, 3)
 DIFFERENCE_BANKS = {4: 2, 5: 3, 6: 4, 7: 5}
 PAIRS_BANKS = {4: 0, 5: 1, 6: 0, 7: 1}
@@ -77,25 +76,23 @@ def tile_list_embg_tgq4_res_kernel(tc, dy, w_words, w_scales, res, wgo, offs, ou
         dy_rows = dy.rearrange("(p t) j -> p t j", t=PACK)
         raw_quarter = [own_tile([P, PACK, QUARTER], F32, f"raw{h}") for h in range(J // QUARTER)]
         raw = [raw_quarter[b // 2][:, :, b % 2 * P : (b % 2 + 1) * P] for b in range(J // P)]
-        early_rows = keep.tile([P, 3 * J], F32, name="early_rows")
-        last_rows = keep.tile([P, J], F32, name="last_rows")
         first_rows = own_tile([P, 3 * QUARTER], F32, "first_rows")
-        residual = {
-            (i, h): (early_rows, (3 * h + i) * QUARTER) if i < 3 else (last_rows, h * QUARTER)
-            for i in range(4)
-            for h in range(4)
-        }
+        later_rows = keep.tile([P, 9 * QUARTER], F32, name="later_rows")
+        last_rows = keep.tile([P, J], F32, name="last_rows")
+        residual = {(3, h): (last_rows, h * QUARTER) for h in range(4)}
         for i in range(3):
             residual[i, 0] = (first_rows, i * QUARTER)
+            for h in range(1, 4):
+                residual[i, h] = (later_rows, (3 * (h - 1) + i) * QUARTER)
 
         def load_dy(h):
             nc.sync.dma_start(out=raw_quarter[h][:], in_=dy_rows[:, :, h * QUARTER : (h + 1) * QUARTER])
 
-        def load_residual(first, last, h):
-            tile, at = residual[first, h]
+        def load_residual(h):
+            tile, at = residual[0, h]
             nc.sync.dma_start(
-                out=tile[:, at : at + (last - first) * QUARTER].rearrange("p (i j) -> p i j", j=QUARTER),
-                in_=res[first * P : last * P, h * QUARTER : (h + 1) * QUARTER].rearrange("(i p) j -> p i j", p=P),
+                out=tile[:, at : at + 3 * QUARTER].rearrange("p (i j) -> p i j", j=QUARTER),
+                in_=res[0 : 3 * P, h * QUARTER : (h + 1) * QUARTER].rearrange("(i p) j -> p i j", p=P),
             )
 
         def load_weights(first, last):
@@ -120,23 +117,23 @@ def tile_list_embg_tgq4_res_kernel(tc, dy, w_words, w_scales, res, wgo, offs, ou
                 out=w_scale[32 * q : 32 * q + 4, :].bitcast(I32), in_=w_scales[0, 4 * q : 4 * q + 4, :].bitcast(I32)
             )
         load_dy(3)
-        load_residual(0, 3, 0)
+        load_residual(0)
         load_weights(0, QUARTER)
         nc.sync.dma_start(offsets[:], offs)
-        load_residual(0, 3, 1)
+        load_residual(1)
         load_weights(QUARTER, J)
-        load_residual(0, 3, 2)
-        load_residual(0, 3, 3)
-        for c in range(2):
-            cols = slice(c * BANK, (c + 1) * BANK)
+        load_residual(2)
+        load_residual(3)
+        for half in range(2):
+            cols = slice(half * BANK, (half + 1) * BANK)
             nc.sync.dma_start(out=last_rows[:, cols], in_=res[3 * P : 4 * P, cols])
 
         for a in range(2):
-            for c0 in range(0, P, SPAN):
+            for first in range(0, P, SPAN):
                 nc.vector.tensor_scalar(
-                    out=eye_woven[a][:, PACK * c0 + 2 + a : PACK * (c0 + SPAN) : PACK],
+                    out=eye_woven[a][:, PACK * first + 2 + a : PACK * (first + SPAN) : PACK],
                     in0=diagonal[:],
-                    scalar1=float(-c0),
+                    scalar1=float(-first),
                     scalar2=None,
                     op0=ALU.is_equal,
                 )
@@ -149,7 +146,7 @@ def tile_list_embg_tgq4_res_kernel(tc, dy, w_words, w_scales, res, wgo, offs, ou
             nc.vector.memset(pages[i][:, first:last].bitcast(I32), 0)
 
         clear(0, 0, T)
-        clear(1, 0, BANK)
+        clear(1, 0, 2 * BANK)
         moved_at = QUARTER + PAD_WORDS
         eye_halves = eye_words[:].bitcast(U16)
         nc.scalar.copy(out=eye_halves[:, 2 * moved_at : 2 * moved_at + K], in_=eye_halves[:, 1 : K + 1])
@@ -157,7 +154,7 @@ def tile_list_embg_tgq4_res_kernel(tc, dy, w_words, w_scales, res, wgo, offs, ou
 
         quarter_shape = [P, QUARTER, PACK]
         q_woven = [placed_tile(head, quarter_shape, BF16, f"q_woven{h}", q_woven_at[h]) for h in range(3)]
-        q_woven.append(keep.tile(quarter_shape, BF16, name="q_woven3", tag="raw0", align_bytes=MX_ALIGN))
+        q_woven.append(own_tile(quarter_shape, BF16, "q_woven3", "raw0"))
 
         q_operand = {}
         r_operand = {}
@@ -257,7 +254,7 @@ def tile_list_embg_tgq4_res_kernel(tc, dy, w_words, w_scales, res, wgo, offs, ou
             fresh(sums, pieces, "sums", tag)
             nc.scalar.copy(out=columns(sums, pieces), in_=columns(dx, pieces))
 
-        def add(pieces, tag):
+        def add(pieces, tag=None):
             fresh(total, pieces, "total", tag)
             nc.gpsimd.tensor_tensor(
                 out=columns(total, pieces), in0=columns(sums, pieces), in1=columns(residual, pieces), op=ALU.add
@@ -324,43 +321,42 @@ def tile_list_embg_tgq4_res_kernel(tc, dy, w_words, w_scales, res, wgo, offs, ou
 
         weave(nc.vector.tensor_copy, q_woven[0][:, 0:P, :], raw[0])
         weave(nc.scalar.copy, q_woven[0][:, P:QUARTER, :], raw[1])
-        clear(1, BANK, 2 * BANK)
+        clear(1, 2 * BANK, 3 * BANK)
         first_tier(0, calls=2)
         read_back(0)
         read_back(1)
-        weave(nc.scalar.copy, q_woven[1][:, 0:SCALAR_SHARE, :], raw_quarter[1][:, :, 0:SCALAR_SHARE])
+        weave(nc.scalar.copy, q_woven[1][:, 0:P, :], raw[2])
         eye = placed_tile(head, [P, P], F32, "eye", eye_at)
         nc.scalar.copy(out=eye[:], in_=eye_woven[0][:, 2:K:PACK])
-        weave(nc.vector.tensor_copy, q_woven[1][:, SCALAR_SHARE:QUARTER, :], raw_quarter[1][:, :, SCALAR_SHARE:QUARTER])
-        clear(1, 2 * BANK, 3 * BANK)
+        weave(nc.vector.tensor_copy, q_woven[1][:, P:QUARTER, :], raw[3])
+        clear(1, 3 * BANK, T)
         first_tier(1)
         pages[2] = placed_tile(head, [P, T], F32, "page2", q_woven_at[1])
-        nc.gpsimd.memset(pages[2][:].bitcast(I32), 0)
+        nc.gpsimd.memset(pages[2][:, 0 : T - QUARTER].bitcast(I32), 0)
         pages[3] = pages[0]
         read_back(2)
         read_back(3)
         weave(nc.scalar.copy, q_woven[2][:], raw_quarter[2][:])
         subtract(0)
-        open_sum("ab0")
-        open_sum("c0")
+        open_sum("a0")
+        open_sum("bc0")
         subtract(1)
         weave(nc.scalar.copy, q_woven[3][:], raw_quarter[3][:])
         second_tier(0)
-        close_sum("ab0")
-        close_sum("c0")
+        close_sum("a0")
+        close_sum("bc0")
         open_sum("ab1")
         open_difference(4)
         open_difference(5)
         first_tier(2)
         second_tier(1)
-        clear(1, 3 * BANK, T)
-        ab0, c0, ab1, c1, ab2, c2, a3, bc3, d01, d23 = BATCHES.values()
-        a0, bc0 = ab0[:1], ab0[1:] + c0
+        clear(2, T - QUARTER, T)
+        a0, bc0, ab1, c1, ab2, c2, a3, bc3, d01, d23 = BATCHES.values()
         fresh(total, a0, "total")
         fresh(total, bc0, "total", "totals")
-        for piece in ab0 + c0:
+        for pieces in (a0, bc0):
             nc.vector.tensor_tensor(
-                out=columns(total, [piece]), in0=columns(dx, [piece]), in1=columns(residual, [piece]), op=ALU.add
+                out=columns(total, pieces), in0=columns(dx, pieces), in1=columns(residual, pieces), op=ALU.add
             )
         first_tier(3, tag="first_rows")
         fresh(scaled, a0, "scaled")
@@ -409,15 +405,16 @@ def tile_list_embg_tgq4_res_kernel(tc, dy, w_words, w_scales, res, wgo, offs, ou
         multiply(ab2, "turned7")
         second_tier(3, "r_woven2")
         place(ab2)
+
         for name in ("c2", "a3"):
             open_sum(name)
             close_sum(name)
             empty(BATCHES[name])
         add(c2, "r_woven3")
-        add(a3, "total_a3")
+        add(a3)
         multiply(a3)
         place(a3)
-        multiply(c2, "total_a3")
+        multiply(c2, "total03")
         place(c2)
         open_sum("bc3")
         close_sum("bc3")
@@ -426,6 +423,7 @@ def tile_list_embg_tgq4_res_kernel(tc, dy, w_words, w_scales, res, wgo, offs, ou
         for piece in bc3:
             multiply([piece])
             place([piece])
+
         last = d01 + d23
         fresh(sums, last, "sums")
         for name in ("d01", "d23"):

from contextlib import ExitStack

import concourse.mybir as mybir

K, N, T, J = 512, 512, 2048, 1024
FLOPS = 3 * 2 * K * N * J

F32 = mybir.dt.float32
BF16 = mybir.dt.bfloat16
I32 = mybir.dt.int32
U32 = mybir.dt.uint32
U16 = mybir.dt.uint16
U8 = mybir.dt.uint8
E4M3 = mybir.dt.float8_e4m3fn_x4
E5M2 = mybir.dt.float8_e5m2_x4
E2M1 = mybir.dt.float4_e2m1fn_x4
ALU = mybir.AluOpType
COPY = mybir.ActivationFunctionType.Copy

P = 128
PACK = 4
GROUP = 16
QUADRANTS = 4
BANK = 512
QUARTER = 256
SPAN = 64
MX_ALIGN = 64
PAD_WORDS = MX_ALIGN // 4
PAGE_BYTES = 4 * T
WOVEN_BYTES = 2 * PACK * QUARTER

BATCHES = {
    "a0": ((0, 0),),
    "bc0": ((1, 0), (2, 0)),
    "ab1": ((0, 1), (1, 1)),
    "c1": ((2, 1),),
    "ab2": ((0, 2), (1, 2)),
    "c2": ((2, 2),),
    "a3": ((0, 3),),
    "bc3": ((1, 3), (2, 3)),
    "d01": ((3, 0), (3, 1)),
    "d23": ((3, 2), (3, 3)),
}
DX_BANKS = {"a0": 0, "bc0": 1, "ab1": 6, "c1": 5, "ab2": 6, "c2": 1, "a3": 3, "bc3": 2, "d01": 1, "d23": 5}
BACK_BANKS = (0, 1, 2, 3, 4, 5, 2, 3)
DIFFERENCE_BANKS = {4: 2, 5: 3, 6: 4, 7: 5}
PAIRS_BANKS = {4: 0, 5: 1, 6: 0, 7: 1}


def tile_list_embg_tgq4_res_kernel(tc, dy, w_words, w_scales, res, wgo, offs, out):
    nc = tc.nc
    with ExitStack() as ctx:
        keep = ctx.enter_context(tc.tile_pool(name="keep", bufs=1))
        early = ctx.enter_context(tc.tile_pool(name="early", bufs=1))
        head = ctx.enter_context(tc.tile_pool(name="head", bufs=1))
        psum = ctx.enter_context(tc.psum_pool(name="psum", bufs=1))

        def own_tile(shape, dtype, name, tag=None):
            return keep.tile(shape, dtype, name=name, tag=tag or name, align_bytes=MX_ALIGN)

        def placed_tile(pool, shape, dtype, name, offset):
            return pool.tile(shape, dtype, name=name, offset=offset, align_bytes=MX_ALIGN)

        def bank(b, name):
            return psum.tile([P, BANK], F32, name=name, tag=f"bank{b}")

        diagonal_at = PAGE_BYTES - 2 * SPAN
        eye_woven_at = WOVEN_BYTES - MX_ALIGN
        eye_at = WOVEN_BYTES
        q_woven_at = (0, eye_woven_at + 2 * K - MX_ALIGN, 0)

        offsets = keep.tile([P, J // GROUP], U16, name="offsets")
        w_codes = own_tile([P, 2 * N], U8, "w_codes")
        w_scale = own_tile([P, N], U8, "w_scale")
        weights = keep.tile([P, J], F32, name="weights")
        dy_rows = dy.rearrange("(p t) j -> p t j", t=PACK)
        raw_quarter = [own_tile([P, PACK, QUARTER], F32, f"raw{h}") for h in range(J // QUARTER)]
        raw = [raw_quarter[b // 2][:, :, b % 2 * P : (b % 2 + 1) * P] for b in range(J // P)]
        first_rows = own_tile([P, 3 * QUARTER], F32, "first_rows")
        later_rows = keep.tile([P, 9 * QUARTER], F32, name="later_rows")
        last_rows = keep.tile([P, J], F32, name="last_rows")
        residual = {(3, h): (last_rows, h * QUARTER) for h in range(4)}
        for i in range(3):
            residual[i, 0] = (first_rows, i * QUARTER)
            for h in range(1, 4):
                residual[i, h] = (later_rows, (3 * (h - 1) + i) * QUARTER)

        def load_dy(h):
            nc.sync.dma_start(out=raw_quarter[h][:], in_=dy_rows[:, :, h * QUARTER : (h + 1) * QUARTER])

        def load_residual(h):
            tile, at = residual[0, h]
            nc.sync.dma_start(
                out=tile[:, at : at + 3 * QUARTER].rearrange("p (i j) -> p i j", j=QUARTER),
                in_=res[0 : 3 * P, h * QUARTER : (h + 1) * QUARTER].rearrange("(i p) j -> p i j", p=P),
            )

        def load_weights(first, last):
            nc.sync.dma_start(out=weights[:, first:last], in_=wgo[:, first:last])

        diagonal = placed_tile(early, [P, SPAN], I32, "diagonal", diagonal_at)
        nc.gpsimd.iota(diagonal[:], pattern=[[1, SPAN]], base=0, channel_multiplier=-1)
        eye_woven = [own_tile([P, K], BF16, "eye_woven0"), placed_tile(head, [P, K], BF16, "eye_woven1", eye_woven_at)]
        eye_words = own_tile([P, 2 * QUARTER + PAD_WORDS], U32, "eye_words")
        eye_scale = own_tile([P, QUARTER], U8, "eye_scale")
        for part in eye_woven:
            nc.vector.memset(part[:].bitcast(I32), 0)
        nc.vector.memset(w_scale[:].bitcast(I32), 0)
        nc.vector.memset(eye_words[:, QUARTER : QUARTER + PAD_WORDS].bitcast(I32), 0)

        load_dy(0)
        load_dy(1)
        load_dy(2)
        nc.sync.dma_start(out=w_codes[:].bitcast(I32), in_=w_words[0].bitcast(I32))
        for q in range(QUADRANTS):
            nc.sync.dma_start(
                out=w_scale[32 * q : 32 * q + 4, :].bitcast(I32), in_=w_scales[0, 4 * q : 4 * q + 4, :].bitcast(I32)
            )
        load_dy(3)
        load_residual(0)
        load_weights(0, QUARTER)
        nc.sync.dma_start(offsets[:], offs)
        load_residual(1)
        load_weights(QUARTER, J)
        load_residual(2)
        load_residual(3)
        for half in range(2):
            cols = slice(half * BANK, (half + 1) * BANK)
            nc.sync.dma_start(out=last_rows[:, cols], in_=res[3 * P : 4 * P, cols])

        for a in range(2):
            for first in range(0, P, SPAN):
                nc.vector.tensor_scalar(
                    out=eye_woven[a][:, PACK * first + 2 + a : PACK * (first + SPAN) : PACK],
                    in0=diagonal[:],
                    scalar1=float(-first),
                    scalar2=None,
                    op0=ALU.is_equal,
                )
        for a in range(2):
            cols = slice(a * P, (a + 1) * P)
            nc.vector.quantize_mx(out=eye_words[:, cols].bitcast(E4M3), scales=eye_scale[:, cols], in_=eye_woven[a][:])
        pages = {i: placed_tile(early, [P, T], F32, f"page{i}", i * PAGE_BYTES) for i in range(2)}

        def clear(i, first, last):
            nc.vector.memset(pages[i][:, first:last].bitcast(I32), 0)

        clear(0, 0, T)
        clear(1, 0, 2 * BANK)
        moved_at = QUARTER + PAD_WORDS
        eye_halves = eye_words[:].bitcast(U16)
        nc.scalar.copy(out=eye_halves[:, 2 * moved_at : 2 * moved_at + K], in_=eye_halves[:, 1 : K + 1])
        eye_part = [eye_words[:, at : at + P] for at in (moved_at, moved_at + P, 0, P)]

        quarter_shape = [P, QUARTER, PACK]
        q_woven = [placed_tile(head, quarter_shape, BF16, f"q_woven{h}", q_woven_at[h]) for h in range(3)]
        q_woven.append(own_tile(quarter_shape, BF16, "q_woven3", "raw0"))

        q_operand = {}
        r_operand = {}
        r_woven = {}
        back = {}
        minus = {}
        difference = {}
        turned = {}
        dx = {}
        sums = {}
        total = {}
        scaled = {}

        def weave(copy, woven, rows):
            copy(
                out=woven.rearrange("p (g i) t -> p g t i", i=PACK),
                in_=rows.rearrange("p t (g i) -> p g t i", i=PACK),
            )

        def quantize(operand, woven, h, fmt, codes, name, calls=1):
            scale = own_tile([P, QUARTER], U8, name)
            width = QUARTER // calls
            for j in range(0, QUARTER, width):
                cols = slice(j, j + width)
                nc.vector.quantize_mx(
                    out=codes[:, cols].bitcast(fmt), scales=scale[:, cols], in_=woven[:, cols, :].rearrange("p j t -> p (j t)")
                )
            for j in (0, P):
                operand[h * QUARTER + j] = (codes[:, j:QUARTER], scale[:, j:QUARTER])

        def first_tier(h, calls=1, tag=None):
            codes = own_tile([P, QUARTER], U32, f"q_codes{h}", tag)
            quantize(q_operand, q_woven[h], h, E5M2, codes, f"q_scale{h}", calls)

        def second_tier(h, tag=None):
            quantize(r_operand, r_woven[h], h, E4M3, own_tile([P, QUARTER], U32, f"r_codes{h}", tag), f"r_scale{h}")

        def read_back(b):
            back[b] = bank(BACK_BANKS[b], f"back{b}")
            codes, scale = q_operand[b * P]
            for t in range(PACK):
                nc.tensor.matmul_mx(
                    out=back[b][:, t * P : (t + 1) * P],
                    lhsT=eye_part[t].bitcast(E4M3),
                    lhsT_scale=eye_scale[:, 0:P],
                    rhs=codes[:, 0:P].bitcast(E5M2),
                    rhs_scale=scale[:, 0:P],
                    start=True,
                    stop=True,
                )

        def subtract(h):
            r_woven[h] = own_tile(quarter_shape, BF16, f"r_woven{h}")
            for b in (2 * h, 2 * h + 1):
                nc.vector.tensor_tensor(
                    out=r_woven[h][:, b % 2 * P : (b % 2 + 1) * P, :].rearrange("p (g i) t -> p g t i", i=2),
                    in0=raw[b].rearrange("p t (g i) -> p g t i", i=2),
                    in1=back[b][:].rearrange("p (t g i) -> p g t i", t=PACK, i=2),
                    op=ALU.subtract,
                )

        def product(name, n, operand, fmt, start, stop):
            i, h = BATCHES[name][n]
            codes, scale = operand[h * QUARTER]
            nc.tensor.matmul_mx(
                out=columns(dx, [(i, h)]),
                lhsT=w_codes[:, 2 * P * i : 2 * P * (i + 1)].bitcast(E2M1),
                lhsT_scale=w_scale[:, P * i : P * (i + 1)],
                rhs=codes.bitcast(fmt),
                rhs_scale=scale,
                start=start,
                stop=stop,
            )

        def columns(table, pieces):
            tile, at = table[pieces[0]]
            return tile[:, at : at + len(pieces) * QUARTER]

        def assign(table, pieces, tile):
            for n, piece in enumerate(pieces):
                table[piece] = (tile, n * QUARTER)

        def fresh(table, pieces, name, tag=None):
            i, h = pieces[0]
            assign(table, pieces, own_tile([P, len(pieces) * QUARTER], F32, f"{name}{i}{h}", tag))

        def open_sum(name):
            assign(dx, BATCHES[name], bank(DX_BANKS[name], f"dx_{name}"))
            for n in range(len(BATCHES[name])):
                product(name, n, q_operand, E5M2, n == 0, False)

        def close_sum(name):
            for n in range(len(BATCHES[name])):
                product(name, n, r_operand, E4M3, False, n == len(BATCHES[name]) - 1)

        def empty(pieces, tag=None):
            fresh(sums, pieces, "sums", tag)
            nc.scalar.copy(out=columns(sums, pieces), in_=columns(dx, pieces))

        def add(pieces, tag=None):
            fresh(total, pieces, "total", tag)
            nc.gpsimd.tensor_tensor(
                out=columns(total, pieces), in0=columns(sums, pieces), in1=columns(residual, pieces), op=ALU.add
            )

        def weight_columns(h, count=1):
            return weights[:, h * QUARTER : (h + count) * QUARTER]

        def multiply(pieces, tag=None):
            if pieces[0] not in scaled:
                fresh(scaled, pieces, "scaled", tag)
            shape = [P, len(pieces), QUARTER]
            nc.gpsimd.tensor_tensor(
                out=columns(scaled, pieces).rearrange("p (i j) -> p i j", i=len(pieces)),
                in0=columns(total, pieces).rearrange("p (i j) -> p i j", i=len(pieces)),
                in1=weight_columns(pieces[0][1]).unsqueeze(1).to_broadcast(shape),
                op=ALU.mult,
            )

        def window(i, h, count=1):
            return pages[i][:].indirect(offsets[:, h * QUARTER // GROUP : (h + count) * QUARTER // GROUP])

        def store(i):
            nc.sync.dma_start(out=out[i * P : (i + 1) * P, :], in_=pages[i][:])

        def place(pieces):
            for i, h in pieces:
                nc.vector.tensor_copy(out=window(i, h), in_=columns(scaled, [(i, h)]))
                if (h + 1) * QUARTER == J:
                    store(i)

        def add_transposed(b, t, rows, start, stop):
            nc.tensor.matmul(
                out=difference[b][:, t * P : (t + 1) * P], lhsT=rows, rhs=eye[:], start=start, stop=stop, is_transpose=True
            )

        def open_difference(b):
            difference[b] = bank(DIFFERENCE_BANKS[b], f"difference{b}")
            for t in range(PACK):
                add_transposed(b, t, raw[b][:, t, :], t == 0, False)

        def negate(b):
            minus[b] = own_tile([P, BANK], F32, f"minus{b}")
            nc.scalar.activation(out=minus[b][:], in_=back[b][:], func=COPY, scale=-1.0)

        def close_difference(b):
            for t in range(PACK):
                add_transposed(b, t, minus[b][:, t * P : (t + 1) * P], False, t == PACK - 1)
            turned[b] = own_tile([P, 2, P, 2], BF16, f"turned{b}")
            nc.scalar.copy(out=turned[b][:], in_=difference[b][:].rearrange("j (v e p) -> j v p e", v=2, e=2))

        def turn_back(b):
            pairs = bank(PAIRS_BANKS[b], f"pairs{b}")
            words = turned[b][:].rearrange("j v p e -> j (v p e)").bitcast(F32)
            for v in range(2):
                nc.tensor.transpose(pairs[:, v * P : (v + 1) * P], words[:, v * P : (v + 1) * P], eye[:])
            if b % 2 == 0:
                r_woven[b // 2] = own_tile(quarter_shape, BF16, f"r_woven{b // 2}")
            woven = r_woven[b // 2][:, b % 2 * P : (b % 2 + 1) * P, :]
            nc.scalar.copy(
                out=woven.rearrange("p j t -> p (j t)").bitcast(F32).rearrange("p (j v) -> p j v", v=2),
                in_=pairs[:, 0 : 2 * P].rearrange("p (v j) -> p j v", v=2),
            )

        weave(nc.vector.tensor_copy, q_woven[0][:, 0:P, :], raw[0])
        weave(nc.scalar.copy, q_woven[0][:, P:QUARTER, :], raw[1])
        clear(1, 2 * BANK, 3 * BANK)
        first_tier(0, calls=2)
        read_back(0)
        read_back(1)
        weave(nc.scalar.copy, q_woven[1][:, 0:P, :], raw[2])
        eye = placed_tile(head, [P, P], F32, "eye", eye_at)
        nc.scalar.copy(out=eye[:], in_=eye_woven[0][:, 2:K:PACK])
        weave(nc.vector.tensor_copy, q_woven[1][:, P:QUARTER, :], raw[3])
        clear(1, 3 * BANK, T)
        first_tier(1)
        pages[2] = placed_tile(head, [P, T], F32, "page2", q_woven_at[1])
        nc.gpsimd.memset(pages[2][:, 0 : T - QUARTER].bitcast(I32), 0)
        pages[3] = pages[0]
        read_back(2)
        read_back(3)
        weave(nc.scalar.copy, q_woven[2][:], raw_quarter[2][:])
        subtract(0)
        open_sum("a0")
        open_sum("bc0")
        subtract(1)
        weave(nc.scalar.copy, q_woven[3][:], raw_quarter[3][:])
        second_tier(0)
        close_sum("a0")
        close_sum("bc0")
        open_sum("ab1")
        open_difference(4)
        open_difference(5)
        first_tier(2)
        second_tier(1)
        clear(2, T - QUARTER, T)
        a0, bc0, ab1, c1, ab2, c2, a3, bc3, d01, d23 = BATCHES.values()
        fresh(total, a0, "total")
        fresh(total, bc0, "total", "totals")
        for pieces in (a0, bc0):
            nc.vector.tensor_tensor(
                out=columns(total, pieces), in0=columns(dx, pieces), in1=columns(residual, pieces), op=ALU.add
            )
        first_tier(3, tag="first_rows")
        fresh(scaled, a0, "scaled")
        nc.vector.tensor_tensor(out=columns(scaled, a0), in0=columns(total, a0), in1=weight_columns(0), op=ALU.mult)
        place(a0)
        fresh(scaled, bc0, "scaled", "raw0")
        for piece in bc0:
            multiply([piece])
            place([piece])

        read_back(4)
        read_back(5)
        close_sum("ab1")
        negate(4)
        negate(5)
        empty(ab1)
        add(ab1, "totals")
        close_difference(4)
        close_difference(5)
        open_sum("c1")
        close_sum("c1")
        turn_back(4)
        empty(c1)
        turn_back(5)
        multiply(ab1, "turned5")
        second_tier(2, "totals")
        place(ab1)
        add(c1, "r_woven2")
        multiply(c1)
        place(c1)

        read_back(6)
        read_back(7)
        negate(6)
        open_difference(6)
        negate(7)
        open_difference(7)
        open_sum("ab2")
        close_difference(6)
        close_sum("ab2")
        empty(ab2, "minus6")
        close_difference(7)
        turn_back(6)
        turn_back(7)
        add(ab2, "r_woven2")
        multiply(ab2, "turned7")
        second_tier(3, "r_woven2")
        place(ab2)

        for name in ("c2", "a3"):
            open_sum(name)
            close_sum(name)
            empty(BATCHES[name])
        add(c2, "r_woven3")
        add(a3)
        multiply(a3)
        place(a3)
        multiply(c2, "total03")
        place(c2)
        open_sum("bc3")
        close_sum("bc3")
        empty(bc3)
        add(bc3, "r_woven3")
        for piece in bc3:
            multiply([piece])
            place([piece])

        last = d01 + d23
        fresh(sums, last, "sums")
        for name in ("d01", "d23"):
            open_sum(name)
            close_sum(name)
            nc.scalar.copy(out=columns(sums, BATCHES[name]), in_=columns(dx, BATCHES[name]))
        add(last, "r_woven3")
        nc.vector.tensor_tensor(out=window(3, 0, 4), in0=columns(total, last), in1=weights[:], op=ALU.mult)
        store(3)
